import numpy as np
import ml_dtypes


def mxq(x, axis, fmt="e4m3"):
    dtype, down = {"e4m3": (ml_dtypes.float8_e4m3fn, 7), "e5m2": (ml_dtypes.float8_e5m2, 14)}[fmt]
    v = np.moveaxis(np.asarray(x, np.float32).astype(ml_dtypes.bfloat16).astype(np.float64), axis, -1)
    blocks = v.reshape(v.shape[:-1] + (-1, 32))
    amax = np.abs(blocks).max(-1, keepdims=True)
    byte = np.maximum(np.where(amax > 0, np.frexp(amax)[1] - 1 + 127, 0) - down, 1)
    scale = np.exp2(byte - 127.0)
    codes = (blocks / scale).astype(np.float32).astype(dtype).astype(np.float64)
    return np.moveaxis((codes * scale).reshape(v.shape), -1, axis)


WIDE = False


def mx_kscale(k):
    if not WIDE:
        return np.ones(k)
    levels = np.array([10, -10, 5, -5, 0])
    if k % 512:
        return np.exp2(np.random.permutation(np.resize(levels, k // 32))).repeat(32)
    a = np.empty((k // 512, 16))
    for p in range(k // 512):
        a[p, :8] = np.random.permutation(np.resize(levels, 8))
        for g in range(8):
            far = levels[np.abs(levels - a[p, g]) >= 10]
            a[p, g + 8] = far[np.random.randint(len(far))]
    return np.exp2(a.ravel()).repeat(32)


def f64(x):
    return np.asarray(x).astype(np.float64)


def striped(idx):
    return np.tile(idx.reshape(-1, 16).T, (8, 1)).astype(np.uint16)


def unstriped(offs):
    return offs[:16].T.reshape(-1).astype(np.int64)


E2M1 = np.array([0.0, 0.5, 1.0, 1.5, 2.0, 3.0, 4.0, 6.0, -0.0, -0.5, -1.0, -1.5, -2.0, -3.0, -4.0, -6.0])


def pack_weight(w, fmt):
    k, n = w.shape
    w = f64(np.asarray(w, np.float32).astype(ml_dtypes.bfloat16)).reshape(k // 32, 32, n)
    amax = np.abs(w).max(1)
    if fmt == "e4m3":
        byte = np.frexp(amax)[1] - 1 + 127 - 7
    else:
        mant, ex = np.frexp(amax / 6.0)
        byte = np.where(mant > 0.5, ex, ex - 1) + 127
    byte = np.clip(np.where(amax > 0, byte, 1), 1, 254)
    scaled = (w * np.exp2(127.0 - byte)[:, None, :]).reshape(k, n).astype(np.float32)
    by_word = np.ascontiguousarray(scaled.reshape(k // 512, 128, 4, n).transpose(0, 1, 3, 2))
    if fmt == "e4m3":
        words = by_word.astype(ml_dtypes.float8_e4m3fn).view(np.uint8)
    else:
        c = by_word.astype(ml_dtypes.float4_e2m1fn).view(np.uint8) & 0xF
        words = (c[..., 0::2] | (c[..., 1::2] << 4)).reshape(k // 512, 128, 2 * n)
    return np.ascontiguousarray(words), np.ascontiguousarray(byte.astype(np.uint8).reshape(k // 512, 16, n))


def unpack_weight(words, scales, fmt):
    g, _, n = scales.shape
    words = np.ascontiguousarray(words).reshape(g, 128, n, -1)
    if fmt == "e4m3":
        vals = words.view(ml_dtypes.float8_e4m3fn).astype(np.float64)
    else:
        nib = np.empty((g, 128, n, 4), np.uint8)
        nib[..., 0::2] = words & 0xF
        nib[..., 1::2] = words >> 4
        vals = E2M1[nib]
    vals = vals * np.repeat(np.exp2(scales.astype(np.float64) - 127.0), 8, axis=1)[..., None]
    return vals.transpose(0, 1, 3, 2).reshape(g * 512, n)


def planes(y):
    n, m = y.shape
    v = y.astype(np.float32).astype(ml_dtypes.bfloat16).astype(np.float64).reshape(n // 32, 32, m)
    top = np.abs(v).max(1)
    byte = np.clip(np.where(top > 0, np.frexp(top)[1] - 1 + 127 - 7, 1), 1, 254)
    codes = (v * np.exp2(127.0 - byte)[:, None, :]).reshape(n, m).astype(np.float32).astype(ml_dtypes.float8_e4m3fn).view(np.uint8)
    words = codes.reshape(n // 512, 128, 4, m).transpose(0, 1, 3, 2)
    return np.ascontiguousarray(words), np.ascontiguousarray(byte.astype(np.uint8).reshape(n // 512, 16, m))


def sigmoid(v):
    return 1.0 / (1.0 + np.exp(-np.maximum(v, -700.0)))


K, T, E1, C1, E2, C2, H = 1024, 768, 3, 256, 6, 128, 512
N = 512


def by_expert(wq, xq, E, C):
    return np.concatenate([wq[e].T @ xq[:, e * C:(e + 1) * C] for e in range(E)], axis=1)


def setup_inputs():
    n = np.random.standard_normal
    s = mx_kscale(K)
    u = mx_kscale(H)
    slots1, slots2 = np.random.permutation(T), np.random.permutation(T)
    x = pack_weight(n((K, T)) * s[:, None], "e4m3")
    wa = [pack_weight(m, "e2m1") for m in n((E1, K, H)) / np.sqrt(K) / s[None, :, None]]
    wb = [pack_weight(m, "e2m1") for m in n((E2, K, H)) / np.sqrt(K) / s[None, :, None] * u]
    w2 = pack_weight(n((H, N)) / np.sqrt(H) / u[:, None], "e2m1")
    return {
        "x_words": x[0],
        "x_scales": x[1],
        "wa_words": np.stack([m[0] for m in wa]),
        "wa_scales": np.stack([m[1] for m in wa]),
        "wb_words": np.stack([m[0] for m in wb]),
        "wb_scales": np.stack([m[1] for m in wb]),
        "w2_words": w2[0],
        "w2_scales": w2[1],
        "offs": striped(slots1),
        "offs2": striped(slots2),
    }


def reference(x_words, x_scales, wa_words, wa_scales, wb_words, wb_scales, w2_words, w2_scales, offs, offs2):
    wa = np.stack([unpack_weight(wa_words[e], wa_scales[e], "e2m1") for e in range(E1)])
    wb = np.stack([unpack_weight(wb_words[e], wb_scales[e], "e2m1") for e in range(E2)])
    w2 = unpack_weight(w2_words, w2_scales, "e2m1")
    idx, idx2 = unstriped(offs), unstriped(offs2)
    x = unpack_weight(x_words, x_scales, "e4m3")
    a, c = np.zeros((H, T)), np.zeros((H, T))
    a[:, idx] = by_expert(wa, x[:, idx], E1, C1)
    c[:, idx2] = by_expert(wb, x[:, idx2], E2, C2)
    out_0 = w2.T @ mxq(sigmoid(a) * c, 0, "e4m3")
    return (out_0,) + planes(out_0)

@@ -1,0 +1,250 @@
+from contextlib import ExitStack
+
+import concourse.mybir as mybir
+from concourse.masks import make_identity
+
+F32 = mybir.dt.float32
+BF16 = mybir.dt.bfloat16
+I32 = mybir.dt.int32
+U32 = mybir.dt.uint32
+U16 = mybir.dt.uint16
+U8 = mybir.dt.uint8
+FP8X4 = mybir.dt.float8_e4m3fn_x4
+FP4X4 = mybir.dt.float4_e2m1fn_x4
+SIGMOID = mybir.ActivationFunctionType.Sigmoid
+MULT = mybir.AluOpType.mult
+
+P = 128
+K, T, H, N = 1024, 768, 512, 512
+E1, C1, E2, C2 = 3, 256, 6, 128
+PASSES = 2
+WIDE = 1024
+CHUNK = 256
+FLOPS = 2 * K * H * T * 2 + 2 * H * N * T
+
+
+def tile_moe_pool_sigmoid_kernel(
+    tc, x_words, x_scales, wa_words, wa_scales, wb_words, wb_scales, w2_words, w2_scales, offs, offs2, out_0, out_1, out_2
+):
+    nc = tc.nc
+    with ExitStack() as ctx:
+        keep = ctx.enter_context(tc.tile_pool(name="keep", bufs=1))
+        ring = ctx.enter_context(tc.tile_pool(name="ring", bufs=3))
+        psum_mm = ctx.enter_context(tc.psum_pool(name="psum_mm", bufs=3))
+        psum_tr = ctx.enter_context(tc.psum_pool(name="psum_tr", bufs=2))
+        psum_y = ctx.enter_context(tc.psum_pool(name="psum_y", bufs=3))
+
+        def held(shape, dtype, name):
+            return keep.tile(shape, dtype, name=name, align_bytes=64)
+
+        list_a = keep.tile([P, T // 16], U16, name="list_a")
+        list_b = keep.tile([P, T // 16], U16, name="list_b")
+        xs = held([P, WIDE], U8, "xs")
+        xw = [held([P, WIDE], I32, "xw%d" % s) for s in range(PASSES)]
+        was = held([P, E1 * PASSES, H], U8, "was")
+        wbs = held([P, E2 * PASSES, H], U8, "wbs")
+        w2s = held([P, N], U8, "w2s")
+        gs = [held([P, T], U8, "gs%d" % l) for l in range(2)]
+        gs1 = [held([P, T], U8, "gs1%d" % l) for l in range(2)]
+        ident = held([P, P], F32, "ident")
+        warm = held([P, 2], F32, "warm")
+
+        nc.gpsimd.memset(xs[:].bitcast(I32), 0)
+        for s in range(PASSES):
+            nc.vector.memset(xw[s][:, T:WIDE], 0)
+        nc.vector.memset(was[:].bitcast(I32), 0)
+        for l in range(2):
+            nc.vector.memset(gs1[l][:].bitcast(I32), 0)
+        nc.vector.memset(wbs[:].bitcast(I32), 0)
+        nc.vector.memset(w2s[:].bitcast(I32), 0)
+        nc.gpsimd.memset(warm[:, 1:2], 0.0)
+        nc.scalar.activation(warm[:, 0:1], warm[:, 1:2], SIGMOID)
+        make_identity(nc, ident[:])
+
+        def load_x(s):
+            nc.sync.dma_start(xw[s][:, 0:T], x_words[s].rearrange("p t d -> p (t d)").bitcast(I32))
+
+        nc.sync.dma_start(list_a[:], offs)
+        for q in range(4):
+            nc.sync.dma_start(
+                xs[32 * q : 32 * q + 8, 0:T].bitcast(I32), x_scales[:, 4 * q : 4 * q + 4, :].bitcast(I32)
+            )
+        load_x(0)
+        load_x(1)
+        nc.sync.dma_start(list_b[:], offs2)
+
+        def load_scales(plane, scales):
+            for q in range(4):
+                nc.sync.dma_start(
+                    plane[32 * q : 32 * q + 4].bitcast(I32),
+                    scales[:, :, 4 * q : 4 * q + 4, :].rearrange("e s r i -> r (e s) i").bitcast(I32),
+                )
+
+        def load_words(words, name):
+            experts = words.shape[0]
+            tile = held([P, experts * PASSES, 2 * H], U8, name)
+            nc.sync.dma_start(tile[:].bitcast(I32), words.rearrange("e s p n -> p (e s) n").bitcast(I32))
+            return tile
+
+        load_scales(was, wa_scales)
+        wa = [load_words(wa_words[e : e + 1], "wa%d" % e) for e in range(E1)]
+        load_scales(wbs, wb_scales)
+        wb = [load_words(wb_words[2 * g : 2 * g + 2], "wb%d" % g) for g in range(E2 // 2)]
+        w2 = held([P, 2 * N], U8, "w2")
+        nc.sync.dma_start(w2[:].bitcast(I32), w2_words[0].bitcast(I32))
+        for q in range(4):
+            nc.sync.dma_start(w2s[32 * q : 32 * q + 4].bitcast(I32), w2_scales[0, 4 * q : 4 * q + 4, :].bitcast(I32))
+
+        lists = [list_a, list_b]
+        gw = [[held([P, T], U32, "gw%d%d" % (l, s)) for s in range(PASSES)] for l in range(2)]
+
+        def gather_words(l, s):
+            nc.vector.tensor_copy(gw[l][s][:], xw[s][:].bitcast(U32).indirect(lists[l][:]))
+
+        def gather_scales(l, queue):
+            nc.vector.tensor_copy(gs[l][:], xs[:].indirect(lists[l][:]))
+            for q in range(4):
+                queue.dma_start(gs1[l][32 * q : 32 * q + 4].bitcast(I32), gs[l][32 * q + 4 : 32 * q + 8].bitcast(I32))
+
+        gather_scales(0, nc.scalar)
+        gather_words(0, 0)
+        gather_words(0, 1)
+        gather_scales(1, nc.sync)
+        gather_words(1, 0)
+        gather_words(1, 1)
+        planes = [gs, gs1]
+
+        w2d = held([P, 2 * N], U8, "w2d")
+        w2sd = held([P, N], U8, "w2sd")
+        nc.vector.tensor_copy(
+            w2d[:].bitcast(U16).rearrange("p (j m) -> p j m", j=4), w2[:].bitcast(U16).rearrange("p (m j) -> p j m", j=4)
+        )
+        nc.vector.tensor_copy(w2sd[:].rearrange("p (j m) -> p m j", j=4), w2s[:].rearrange("p (m j) -> p m j", j=4))
+
+        def expert_tile(l, slot0, words, scales, dest, gate):
+            acc = psum_mm.tile([P, H], F32, name="acc")
+            for s in range(PASSES):
+                nc.tensor.matmul_mx(
+                    out=acc[:],
+                    lhsT=gw[l][s][:, slot0 : slot0 + P].bitcast(FP8X4),
+                    lhsT_scale=planes[s][l][:, slot0 : slot0 + P],
+                    rhs=words[s].bitcast(FP4X4),
+                    rhs_scale=scales[s],
+                    start=(s == 0),
+                    stop=(s == PASSES - 1),
+                )
+            dealt = ring.tile([P, 4, P], F32, name="dealt")
+            by_j = acc[:].rearrange("p (m j) -> p j m", j=4)
+            if gate:
+                nc.scalar.activation(dealt[:], by_j, SIGMOID)
+            else:
+                nc.scalar.copy(dealt[:], by_j)
+            turned = psum_tr.tile([P, 4, P], F32, name="turned")
+            for j in range(4):
+                nc.tensor.transpose(turned[:, j, :], dealt[:, j, :], ident[:])
+            nc.scalar.copy(dest, turned[:])
+
+        src_a = [held([P, 4, C1], F32, "src_a%d" % e) for e in range(E1)]
+        for e in range(E1):
+            for u in range(C1 // P):
+                expert_tile(
+                    0, e * C1 + u * P, [wa[e][:, s, :] for s in range(PASSES)],
+                    [was[:, e * PASSES + s, :] for s in range(PASSES)], src_a[e][:, :, u * P : (u + 1) * P], True,
+                )
+        src_c = held([P, 4, T], F32, "src_c")
+        for f in range(E2):
+            expert_tile(
+                1, f * C2, [wb[f // 2][:, (f % 2) * PASSES + s, :] for s in range(PASSES)],
+                [wbs[:, f * PASSES + s, :] for s in range(PASSES)], src_c[:, :, f * C2 : (f + 1) * C2], False,
+            )
+
+        gate = [held([P, T], F32, "gate%d" % j) for j in range(4)]
+        for e in range(E1):
+            for j in range(4):
+                cols = slice(e * C1 // 16, (e + 1) * C1 // 16)
+                nc.vector.tensor_copy(gate[j][:].indirect(list_a[:, cols]), src_a[e][:, j, :])
+
+        edges = [0, 128, 384, 640, 768]
+        chunks = [slice(edges[c], edges[c + 1]) for c in range(4)]
+        width = [edges[c + 1] - edges[c] for c in range(4)]
+        hq = [held([P, width[c], 4], BF16, "hq%d" % c) for c in range(4)]
+        value = [held([P, WIDE], F32, "value%d" % j) for j in range(4)]
+        for j in range(4):
+            nc.vector.tensor_copy(value[j][:].indirect(list_b[:]), src_c[:, j, :])
+            if j < 3:
+                hb = held([P, T], BF16, "hb%d" % j)
+                nc.vector.tensor_tensor(hb[:], gate[j][:], value[j][:, 0:T], MULT)
+                for c, cols in enumerate(chunks):
+                    if j < 2:
+                        nc.scalar.copy(hq[c][:, :, j], hb[:, cols])
+                    else:
+                        nc.scalar.copy(hq[c][:, :, 2:4], hb[:, cols].unsqueeze(2).to_broadcast([P, width[c], 2]))
+
+        y_codes = held([P, T], U32, "y_codes")
+        y_scales = held([P, T], U8, "y_scales")
+        rows = out_0.rearrange("(p j) t -> p j t", j=4)
+        h_codes = [held([P, width[c]], U32, "h_codes%d" % c) for c in range(4)]
+        h_scales = [held([P, width[c]], U8, "h_scales%d" % c) for c in range(4)]
+        y = [held([P, 4, width[c]], F32, "y%d" % c) for c in range(4)]
+        yq = [held([P, width[c], 4], BF16, "yq%d" % c) for c in range(4)]
+
+        def last_product(c):
+            nc.vector.tensor_tensor(hq[c][:, :, 3], gate[3][:, chunks[c]], value[3][:, chunks[c]], MULT)
+
+        def last_product_by_scalar(c):
+            hb = held([P, width[c]], BF16, "hb3")
+            nc.vector.tensor_tensor(hb[:], gate[3][:, chunks[c]], value[3][:, chunks[c]], MULT)
+            nc.scalar.copy(hq[c][:, :, 3], hb[:])
+
+        def second_layer(c):
+            nc.vector.quantize_mx(
+                out=h_codes[c][:].bitcast(FP8X4), scales=h_scales[c][:], in_=hq[c][:].rearrange("p t j -> p (t j)")
+            )
+            for u in range(width[c] // P):
+                half = slice(u * P, (u + 1) * P)
+                acc = psum_y.tile([P, 4, P], F32, name="acc_y")
+                for j in range(4):
+                    nc.tensor.matmul_mx(
+                        out=acc[:, j, :],
+                        lhsT=w2d[:, 2 * P * j : 2 * P * (j + 1)].bitcast(FP4X4),
+                        lhsT_scale=w2sd[:, P * j : P * (j + 1)],
+                        rhs=h_codes[c][:, half].bitcast(FP8X4),
+                        rhs_scale=h_scales[c][:, half],
+                        start=True,
+                        stop=True,
+                    )
+                nc.scalar.copy(y[c][:, :, half], acc[:])
+            nc.sync.dma_start(rows[:, :, chunks[c]], y[c][:])
+
+        def regroup(c):
+            nc.vector.tensor_copy(
+                yq[c][:].rearrange("p (c i) j -> p c j i", i=4), y[c][:].rearrange("p j (c i) -> p c j i", i=4)
+            )
+
+        def result_planes(c):
+            cols = chunks[c]
+            nc.vector.quantize_mx(
+                out=y_codes[:, cols].bitcast(FP8X4), scales=y_scales[:, cols], in_=yq[c][:].rearrange("p t j -> p (t j)")
+            )
+            nc.sync.dma_start(
+                out_1[0, :, cols, :].rearrange("p t d -> p (t d)").bitcast(I32), y_codes[:, cols].bitcast(I32)
+            )
+
+        last_product(0)
+        last_product_by_scalar(1)
+        second_layer(0)
+        last_product(2)
+        second_layer(1)
+        last_product(3)
+        second_layer(2)
+        second_layer(3)
+        regroup(0)
+        regroup(1)
+        result_planes(0)
+        result_planes(1)
+        regroup(2)
+        regroup(3)
+        result_planes(2)
+        result_planes(3)
+        for q in range(4):
+            nc.scalar.dma_start(out_2[0, 4 * q : 4 * q + 4, :].bitcast(I32), y_scales[32 * q : 32 * q + 4].bitcast(I32))

@@ -55,10 +55,10 @@ def tile_moe_pool_sigmoid_kernel(
         nc.vector.memset(was[:].bitcast(I32), 0)
         for l in range(2):
             nc.vector.memset(gs1[l][:].bitcast(I32), 0)
-        nc.vector.memset(wbs[:].bitcast(I32), 0)
         nc.vector.memset(w2s[:].bitcast(I32), 0)
         nc.gpsimd.memset(warm[:, 1:2], 0.0)
         nc.scalar.activation(warm[:, 0:1], warm[:, 1:2], SIGMOID)
+        nc.gpsimd.memset(wbs[:].bitcast(I32), 0)
         make_identity(nc, ident[:])
 
         def load_x(s):
@@ -116,10 +116,10 @@ def tile_moe_pool_sigmoid_kernel(
 
         w2d = held([P, 2 * N], U8, "w2d")
         w2sd = held([P, N], U8, "w2sd")
-        nc.vector.tensor_copy(
-            w2d[:].bitcast(U16).rearrange("p (j m) -> p j m", j=4), w2[:].bitcast(U16).rearrange("p (m j) -> p j m", j=4)
+        nc.gpsimd.tensor_copy(
+            w2d[:].rearrange("p (j m b) -> p j m b", j=4, b=2), w2[:].rearrange("p (m j b) -> p j m b", j=4, b=2)
         )
-        nc.vector.tensor_copy(w2sd[:].rearrange("p (j m) -> p m j", j=4), w2s[:].rearrange("p (m j) -> p m j", j=4))
+        nc.gpsimd.tensor_copy(w2sd[:].rearrange("p (j m) -> p j m", j=4), w2s[:].rearrange("p (m j) -> p j m", j=4))
 
         def expert_tile(l, slot0, words, scales, dest, gate):
             acc = psum_mm.tile([P, H], F32, name="acc")
@@ -144,12 +144,13 @@ def tile_moe_pool_sigmoid_kernel(
                 nc.tensor.transpose(turned[:, j, :], dealt[:, j, :], ident[:])
             nc.scalar.copy(dest, turned[:])
 
-        src_a = [held([P, 4, C1], F32, "src_a%d" % e) for e in range(E1)]
+        pieces = [slice(0, C1), slice(C1, T)]
+        src_a = [held([P, 4, piece.stop - piece.start], F32, "src_a%d" % i) for i, piece in enumerate(pieces)]
         for e in range(E1):
             for u in range(C1 // P):
                 expert_tile(
                     0, e * C1 + u * P, [wa[e][:, s, :] for s in range(PASSES)],
-                    [was[:, e * PASSES + s, :] for s in range(PASSES)], src_a[e][:, :, u * P : (u + 1) * P], True,
+                    [was[:, e * PASSES + s, :] for s in range(PASSES)], src_a[min(e, 1)][:, :, max(e - 1, 0) * C1 + u * P : max(e - 1, 0) * C1 + (u + 1) * P], True,
                 )
         src_c = held([P, 4, T], F32, "src_c")
         for f in range(E2):
@@ -159,92 +160,108 @@ def tile_moe_pool_sigmoid_kernel(
             )
 
         gate = [held([P, T], F32, "gate%d" % j) for j in range(4)]
-        for e in range(E1):
+        for i, piece in enumerate(pieces):
             for j in range(4):
-                cols = slice(e * C1 // 16, (e + 1) * C1 // 16)
-                nc.vector.tensor_copy(gate[j][:].indirect(list_a[:, cols]), src_a[e][:, j, :])
+                cols = slice(piece.start // 16, piece.stop // 16)
+                nc.vector.tensor_copy(gate[j][:].indirect(list_a[:, cols]), src_a[i][:, j, :])
 
-        edges = [0, 128, 384, 640, 768]
-        chunks = [slice(edges[c], edges[c + 1]) for c in range(4)]
-        width = [edges[c + 1] - edges[c] for c in range(4)]
-        hq = [held([P, width[c], 4], BF16, "hq%d" % c) for c in range(4)]
-        value = [held([P, WIDE], F32, "value%d" % j) for j in range(4)]
+        hq = held([P, T, 4], BF16, "hq")
+        value = [held([P, WIDE], F32, name) for name in ("value0", "value1", "value2", "value3")]
+        hb = held([P, 3, T], BF16, "hb")
         for j in range(4):
             nc.vector.tensor_copy(value[j][:].indirect(list_b[:]), src_c[:, j, :])
-            if j < 3:
-                hb = held([P, T], BF16, "hb%d" % j)
-                nc.vector.tensor_tensor(hb[:], gate[j][:], value[j][:, 0:T], MULT)
-                for c, cols in enumerate(chunks):
-                    if j < 2:
-                        nc.scalar.copy(hq[c][:, :, j], hb[:, cols])
-                    else:
-                        nc.scalar.copy(hq[c][:, :, 2:4], hb[:, cols].unsqueeze(2).to_broadcast([P, width[c], 2]))
+            if j < 2:
+                nc.gpsimd.tensor_tensor(hb[:, (j + 2) % 3, :], gate[j][:], value[j][:, 0:T], MULT)
+            if j == 0:
+                nc.scalar.copy(hq[:, :, 0], hb[:, 2, :])
+            if j == 2:
+                for cols in (slice(0, T // 2), slice(T // 2, T)):
+                    nc.gpsimd.tensor_tensor(hb[:, 1, cols], gate[j][:, cols], value[j][:, cols], MULT)
+                    nc.scalar.copy(hq[:, cols, 1:4], hb[:, :, cols].rearrange("p j t -> p t j"))
 
         y_codes = held([P, T], U32, "y_codes")
         y_scales = held([P, T], U8, "y_scales")
+        h_codes = held([P, T], U32, "h_codes")
+        h_scales = held([P, T], U8, "h_scales")
         rows = out_0.rearrange("(p j) t -> p j t", j=4)
-        h_codes = [held([P, width[c]], U32, "h_codes%d" % c) for c in range(4)]
-        h_scales = [held([P, width[c]], U8, "h_scales%d" % c) for c in range(4)]
-        y = [held([P, 4, width[c]], F32, "y%d" % c) for c in range(4)]
-        yq = [held([P, width[c], 4], BF16, "yq%d" % c) for c in range(4)]
+        y = held([P, 4, T], F32, "y")
+        yq = held([P, T, 4], BF16, "yq")
+        banks = {}
 
-        def last_product(c):
-            nc.vector.tensor_tensor(hq[c][:, :, 3], gate[3][:, chunks[c]], value[3][:, chunks[c]], MULT)
+        def span(b0, b1):
+            return slice(b0 * P, b1 * P)
 
-        def last_product_by_scalar(c):
-            hb = held([P, width[c]], BF16, "hb3")
-            nc.vector.tensor_tensor(hb[:], gate[3][:, chunks[c]], value[3][:, chunks[c]], MULT)
-            nc.scalar.copy(hq[c][:, :, 3], hb[:])
+        def last_product(cols):
+            nc.vector.tensor_tensor(hq[:, cols, 3], gate[3][:, cols], value[3][:, cols], MULT)
 
-        def second_layer(c):
+        def last_product_by_scalar(cols):
+            nc.vector.tensor_tensor(hb[:, 0, cols], gate[3][:, cols], value[3][:, cols], MULT)
+            nc.scalar.copy(hq[:, cols, 3], hb[:, 0, cols])
+
+        def second_layer(b0, b1):
+            cols = span(b0, b1)
             nc.vector.quantize_mx(
-                out=h_codes[c][:].bitcast(FP8X4), scales=h_scales[c][:], in_=hq[c][:].rearrange("p t j -> p (t j)")
+                out=h_codes[:, cols].bitcast(FP8X4), scales=h_scales[:, cols], in_=hq[:, cols, :].rearrange("p t j -> p (t j)")
             )
-            for u in range(width[c] // P):
-                half = slice(u * P, (u + 1) * P)
-                acc = psum_y.tile([P, 4, P], F32, name="acc_y")
+            for b in range(b0, b1):
+                pool, name = (psum_y, "acc_y") if b % 2 == 0 else (psum_mm, "acc")
+                banks[b] = pool.tile([P, 4, P], F32, name=name)
                 for j in range(4):
                     nc.tensor.matmul_mx(
-                        out=acc[:, j, :],
+                        out=banks[b][:, j, :],
                         lhsT=w2d[:, 2 * P * j : 2 * P * (j + 1)].bitcast(FP4X4),
                         lhsT_scale=w2sd[:, P * j : P * (j + 1)],
-                        rhs=h_codes[c][:, half].bitcast(FP8X4),
-                        rhs_scale=h_scales[c][:, half],
+                        rhs=h_codes[:, span(b, b + 1)].bitcast(FP8X4),
+                        rhs_scale=h_scales[:, span(b, b + 1)],
                         start=True,
                         stop=True,
                     )
-                nc.scalar.copy(y[c][:, :, half], acc[:])
-            nc.sync.dma_start(rows[:, :, chunks[c]], y[c][:])
 
-        def regroup(c):
-            nc.vector.tensor_copy(
-                yq[c][:].rearrange("p (c i) j -> p c j i", i=4), y[c][:].rearrange("p j (c i) -> p c j i", i=4)
-            )
+        def sums_out(b):
+            nc.scalar.copy(y[:, :, span(b, b + 1)], banks[b][:])
 
-        def result_planes(c):
-            cols = chunks[c]
+        def store_sums(b0, b1):
+            nc.sync.dma_start(rows[:, :, span(b0, b1)], y[:, :, span(b0, b1)])
+
+        def round_sums(b, copy):
+            copy(yq[:, span(b, b + 1), :], banks[b][:].rearrange("p j t -> p t j"))
+
+        def result_planes(b0, b1):
+            cols = span(b0, b1)
             nc.vector.quantize_mx(
-                out=y_codes[:, cols].bitcast(FP8X4), scales=y_scales[:, cols], in_=yq[c][:].rearrange("p t j -> p (t j)")
+                out=y_codes[:, cols].bitcast(FP8X4), scales=y_scales[:, cols], in_=yq[:, cols, :].rearrange("p t j -> p (t j)")
             )
             nc.sync.dma_start(
                 out_1[0, :, cols, :].rearrange("p t d -> p (t d)").bitcast(I32), y_codes[:, cols].bitcast(I32)
             )
 
-        last_product(0)
-        last_product_by_scalar(1)
-        second_layer(0)
-        last_product(2)
-        second_layer(1)
-        last_product(3)
-        second_layer(2)
-        second_layer(3)
-        regroup(0)
-        regroup(1)
-        result_planes(0)
-        result_planes(1)
-        regroup(2)
-        regroup(3)
-        result_planes(2)
-        result_planes(3)
+        last_product(span(0, 1))
+        last_product_by_scalar(span(1, 3))
+        second_layer(0, 1)
+        last_product_by_scalar(span(3, 4))
+        last_product(span(4, 6))
+        second_layer(1, 3)
+        second_layer(4, 6)
+        second_layer(3, 4)
+        sums_out(0)
+        store_sums(0, 1)
+        round_sums(0, nc.scalar.copy)
+        round_sums(1, nc.vector.tensor_copy)
+        sums_out(2)
+        result_planes(0, 1)
+        sums_out(1)
+        store_sums(1, 3)
+        round_sums(2, nc.vector.tensor_copy)
+        round_sums(4, nc.vector.tensor_copy)
+        result_planes(1, 3)
+        sums_out(5)
+        sums_out(4)
+        store_sums(4, 6)
+        round_sums(5, nc.vector.tensor_copy)
+        sums_out(3)
+        store_sums(3, 4)
+        round_sums(3, nc.scalar.copy)
+        result_planes(4, 6)
+        result_planes(3, 4)
         for q in range(4):
             nc.scalar.dma_start(out_2[0, 4 * q : 4 * q + 4, :].bitcast(I32), y_scales[32 * q : 32 * q + 4].bitcast(I32))

@@ -115,11 +115,9 @@ def tile_moe_pool_sigmoid_kernel(
         planes = [gs, gs1]
 
         w2d = held([P, 2 * N], U8, "w2d")
-        w2sd = held([P, N], U8, "w2sd")
         nc.gpsimd.tensor_copy(
             w2d[:].rearrange("p (j m b) -> p j m b", j=4, b=2), w2[:].rearrange("p (m j b) -> p j m b", j=4, b=2)
         )
-        nc.gpsimd.tensor_copy(w2sd[:].rearrange("p (j m) -> p j m", j=4), w2s[:].rearrange("p (m j) -> p j m", j=4))
 
         def expert_tile(l, slot0, words, scales, dest, gate):
             acc = psum_mm.tile([P, H], F32, name="acc")
@@ -159,37 +157,57 @@ def tile_moe_pool_sigmoid_kernel(
                 [wbs[:, f * PASSES + s, :] for s in range(PASSES)], src_c[:, :, f * C2 : (f + 1) * C2], False,
             )
 
-        gate = [held([P, T], F32, "gate%d" % j) for j in range(4)]
-        for i, piece in enumerate(pieces):
-            for j in range(4):
-                cols = slice(piece.start // 16, piece.stop // 16)
-                nc.vector.tensor_copy(gate[j][:].indirect(list_a[:, cols]), src_a[i][:, j, :])
+        gate = [held([P, T], F32, "gate%d" % j) for j in range(3)]
+
+        def scatter_gate(i, j):
+            cols = slice(pieces[i].start // 16, pieces[i].stop // 16)
+            nc.vector.tensor_copy(gate[j][:].indirect(list_a[:, cols]), src_a[i][:, j, :])
+
+        for i in range(2):
+            for j in range(3):
+                scatter_gate(i, j)
 
         hq = held([P, T, 4], BF16, "hq")
-        value = [held([P, WIDE], F32, name) for name in ("value0", "value1", "value2", "value3")]
         hb = held([P, 3, T], BF16, "hb")
-        for j in range(4):
+        value = []
+
+        def scatter_value(j, name):
+            value.append(held([P, WIDE], F32, name))
             nc.vector.tensor_copy(value[j][:].indirect(list_b[:]), src_c[:, j, :])
-            if j < 2:
-                nc.gpsimd.tensor_tensor(hb[:, (j + 2) % 3, :], gate[j][:], value[j][:, 0:T], MULT)
+
+        for j in range(3):
+            scatter_value(j, "value%d" % j)
+            nc.gpsimd.tensor_tensor(hb[:, (j + 2) % 3, :], gate[j][:], value[j][:, 0:T], MULT)
             if j == 0:
                 nc.scalar.copy(hq[:, :, 0], hb[:, 2, :])
-            if j == 2:
-                for cols in (slice(0, T // 2), slice(T // 2, T)):
-                    nc.gpsimd.tensor_tensor(hb[:, 1, cols], gate[j][:, cols], value[j][:, cols], MULT)
-                    nc.scalar.copy(hq[:, cols, 1:4], hb[:, :, cols].rearrange("p j t -> p t j"))
+        nc.scalar.copy(hq[:, :, 1:4], hb[:].rearrange("p j t -> p t j"))
+        gate.append(held([P, T], F32, "gate1"))
+        scatter_gate(0, 3)
+        scatter_value(3, "value1")
+        scatter_gate(1, 3)
+
+        w2sd = held([P, N], U8, "src_c")
+        nc.gpsimd.tensor_copy(w2sd[:].rearrange("p (j m) -> p j m", j=4), w2s[:].rearrange("p (m j) -> p j m", j=4))
+        idle = psum_tr.tile([P, N], F32, name="turned")
+        for s in range(7):
+            nc.tensor.matmul_mx(
+                out=idle[:],
+                lhsT=gw[1][0][:, 0:P].bitcast(FP8X4),
+                lhsT_scale=gs[1][:, 0:P],
+                rhs=w2d[:].bitcast(FP4X4),
+                rhs_scale=w2sd[:],
+                start=True,
+                stop=True,
+            )
 
         y_codes = held([P, T], U32, "y_codes")
         y_scales = held([P, T], U8, "y_scales")
         h_codes = held([P, T], U32, "h_codes")
         h_scales = held([P, T], U8, "h_scales")
         rows = out_0.rearrange("(p j) t -> p j t", j=4)
-        y = held([P, 4, T], F32, "y")
+        chunks = [slice(t0, t0 + CHUNK) for t0 in range(0, T, CHUNK)]
+        y = [held([P, 4, CHUNK], F32, "y%d" % c) for c in range(3)]
         yq = held([P, T, 4], BF16, "yq")
-        banks = {}
-
-        def span(b0, b1):
-            return slice(b0 * P, b1 * P)
 
         def last_product(cols):
             nc.vector.tensor_tensor(hq[:, cols, 3], gate[3][:, cols], value[3][:, cols], MULT)
@@ -198,36 +216,29 @@ def tile_moe_pool_sigmoid_kernel(
             nc.vector.tensor_tensor(hb[:, 0, cols], gate[3][:, cols], value[3][:, cols], MULT)
             nc.scalar.copy(hq[:, cols, 3], hb[:, 0, cols])
 
-        def second_layer(b0, b1):
-            cols = span(b0, b1)
+        def second_layer(c):
+            cols = chunks[c]
             nc.vector.quantize_mx(
                 out=h_codes[:, cols].bitcast(FP8X4), scales=h_scales[:, cols], in_=hq[:, cols, :].rearrange("p t j -> p (t j)")
             )
-            for b in range(b0, b1):
-                pool, name = (psum_y, "acc_y") if b % 2 == 0 else (psum_mm, "acc")
-                banks[b] = pool.tile([P, 4, P], F32, name=name)
-                for j in range(4):
+            for pool, name, j0 in ((psum_y, "acc_y", 0), (psum_mm, "acc", 2)):
+                bank = pool.tile([P, 2, CHUNK], F32, name=name)
+                for j in range(j0, j0 + 2):
                     nc.tensor.matmul_mx(
-                        out=banks[b][:, j, :],
+                        out=bank[:, j - j0, :],
                         lhsT=w2d[:, 2 * P * j : 2 * P * (j + 1)].bitcast(FP4X4),
                         lhsT_scale=w2sd[:, P * j : P * (j + 1)],
-                        rhs=h_codes[:, span(b, b + 1)].bitcast(FP8X4),
-                        rhs_scale=h_scales[:, span(b, b + 1)],
+                        rhs=h_codes[:, cols].bitcast(FP8X4),
+                        rhs_scale=h_scales[:, cols],
                         start=True,
                         stop=True,
                     )
+                nc.scalar.copy(y[c][:, j0 : j0 + 2, :], bank[:])
+                nc.sync.dma_start(rows[:, j0 : j0 + 2, cols], y[c][:, j0 : j0 + 2, :])
 
-        def sums_out(b):
-            nc.scalar.copy(y[:, :, span(b, b + 1)], banks[b][:])
-
-        def store_sums(b0, b1):
-            nc.sync.dma_start(rows[:, :, span(b0, b1)], y[:, :, span(b0, b1)])
-
-        def round_sums(b, copy):
-            copy(yq[:, span(b, b + 1), :], banks[b][:].rearrange("p j t -> p t j"))
-
-        def result_planes(b0, b1):
-            cols = span(b0, b1)
+        def result_planes(c):
+            cols = chunks[c]
+            nc.vector.tensor_copy(yq[:, cols, :], y[c][:].rearrange("p j t -> p t j"))
             nc.vector.quantize_mx(
                 out=y_codes[:, cols].bitcast(FP8X4), scales=y_scales[:, cols], in_=yq[:, cols, :].rearrange("p t j -> p (t j)")
             )
@@ -235,33 +246,15 @@ def tile_moe_pool_sigmoid_kernel(
                 out_1[0, :, cols, :].rearrange("p t d -> p (t d)").bitcast(I32), y_codes[:, cols].bitcast(I32)
             )
 
-        last_product(span(0, 1))
-        last_product_by_scalar(span(1, 3))
-        second_layer(0, 1)
-        last_product_by_scalar(span(3, 4))
-        last_product(span(4, 6))
-        second_layer(1, 3)
-        second_layer(4, 6)
-        second_layer(3, 4)
-        sums_out(0)
-        store_sums(0, 1)
-        round_sums(0, nc.scalar.copy)
-        round_sums(1, nc.vector.tensor_copy)
-        sums_out(2)
-        result_planes(0, 1)
-        sums_out(1)
-        store_sums(1, 3)
-        round_sums(2, nc.vector.tensor_copy)
-        round_sums(4, nc.vector.tensor_copy)
-        result_planes(1, 3)
-        sums_out(5)
-        sums_out(4)
-        store_sums(4, 6)
-        round_sums(5, nc.vector.tensor_copy)
-        sums_out(3)
-        store_sums(3, 4)
-        round_sums(3, nc.scalar.copy)
-        result_planes(4, 6)
-        result_planes(3, 4)
+        last_product_by_scalar(slice(P, CHUNK))
+        last_product(slice(0, P))
+        last_product_by_scalar(chunks[1])
+        second_layer(0)
+        last_product(chunks[2])
+        second_layer(1)
+        second_layer(2)
+        for c in range(3):
+            result_planes(c)
         for q in range(4):
-            nc.scalar.dma_start(out_2[0, 4 * q : 4 * q + 4, :].bitcast(I32), y_scales[32 * q : 32 * q + 4].bitcast(I32))
+            queue = nc.scalar if q % 2 else nc.sync
+            queue.dma_start(out_2[0, 4 * q : 4 * q + 4, :].bitcast(I32), y_scales[32 * q : 32 * q + 4].bitcast(I32))

@@ -50,16 +50,16 @@ def tile_moe_pool_sigmoid_kernel(
         warm = held([P, 2], F32, "warm")
 
         nc.gpsimd.memset(xs[:].bitcast(I32), 0)
-        for s in range(PASSES):
-            nc.vector.memset(xw[s][:, T:WIDE], 0)
-        nc.vector.memset(was[:].bitcast(I32), 0)
-        for l in range(2):
-            nc.vector.memset(gs1[l][:].bitcast(I32), 0)
-        nc.vector.memset(w2s[:].bitcast(I32), 0)
+        nc.gpsimd.memset(xw[0][:, T:WIDE], 0)
+        nc.gpsimd.memset(was[:].bitcast(I32), 0)
         nc.gpsimd.memset(warm[:, 1:2], 0.0)
         nc.scalar.activation(warm[:, 0:1], warm[:, 1:2], SIGMOID)
-        nc.gpsimd.memset(wbs[:].bitcast(I32), 0)
+        nc.gpsimd.memset(xw[1][:, T:WIDE], 0)
+        nc.gpsimd.memset(gs1[0][:].bitcast(I32), 0)
         make_identity(nc, ident[:])
+        nc.gpsimd.memset(wbs[:].bitcast(I32), 0)
+        nc.gpsimd.memset(gs1[1][:].bitcast(I32), 0)
+        nc.gpsimd.memset(w2s[:].bitcast(I32), 0)
 
         def load_x(s):
             nc.sync.dma_start(xw[s][:, 0:T], x_words[s].rearrange("p t d -> p (t d)").bitcast(I32))
@@ -142,13 +142,14 @@ def tile_moe_pool_sigmoid_kernel(
                 nc.tensor.transpose(turned[:, j, :], dealt[:, j, :], ident[:])
             nc.scalar.copy(dest, turned[:])
 
-        pieces = [slice(0, C1), slice(C1, T)]
-        src_a = [held([P, 4, piece.stop - piece.start], F32, "src_a%d" % i) for i, piece in enumerate(pieces)]
+        pieces = [slice(e * C1, (e + 1) * C1) for e in range(E1)]
+        src_a = held([P, 4, T], F32, "src_a")
         for e in range(E1):
             for u in range(C1 // P):
+                slot0 = e * C1 + u * P
                 expert_tile(
-                    0, e * C1 + u * P, [wa[e][:, s, :] for s in range(PASSES)],
-                    [was[:, e * PASSES + s, :] for s in range(PASSES)], src_a[min(e, 1)][:, :, max(e - 1, 0) * C1 + u * P : max(e - 1, 0) * C1 + (u + 1) * P], True,
+                    0, slot0, [wa[e][:, s, :] for s in range(PASSES)],
+                    [was[:, e * PASSES + s, :] for s in range(PASSES)], src_a[:, :, slot0 : slot0 + P], True,
                 )
         src_c = held([P, 4, T], F32, "src_c")
         for f in range(E2):
@@ -157,45 +158,46 @@ def tile_moe_pool_sigmoid_kernel(
                 [wbs[:, f * PASSES + s, :] for s in range(PASSES)], src_c[:, :, f * C2 : (f + 1) * C2], False,
             )
 
-        gate = [held([P, T], F32, "gate%d" % j) for j in range(3)]
-
-        def scatter_gate(i, j):
-            cols = slice(pieces[i].start // 16, pieces[i].stop // 16)
-            nc.vector.tensor_copy(gate[j][:].indirect(list_a[:, cols]), src_a[i][:, j, :])
-
-        for i in range(2):
-            for j in range(3):
-                scatter_gate(i, j)
+        gate = [held([P, T], F32, "gate%d" % j) for j in range(4)]
+        for piece in pieces:
+            for j in range(4):
+                cols = slice(piece.start // 16, piece.stop // 16)
+                nc.vector.tensor_copy(gate[j][:].indirect(list_a[:, cols]), src_a[:, j, piece])
 
         hq = held([P, T, 4], BF16, "hq")
         hb = held([P, 3, T], BF16, "hb")
-        value = []
 
-        def scatter_value(j, name):
-            value.append(held([P, WIDE], F32, name))
+        def half_units(row, half):
+            return row.rearrange("p (u h t) -> p u h t", h=2, t=P // 2)[:, :, half, :]
+
+        value = [held([P, WIDE], F32, "value%d" % j) for j in range(4)]
+        for j in range(4):
             nc.vector.tensor_copy(value[j][:].indirect(list_b[:]), src_c[:, j, :])
+            if j < 2:
+                nc.gpsimd.tensor_tensor(hb[:, j + 1, :], gate[j][:], value[j][:, 0:T], MULT)
+                nc.scalar.copy(hq[:, :, j], hb[:, j + 1, :])
+            if j == 2:
+                for half in range(2):
+                    nc.gpsimd.tensor_tensor(half_units(hb[:, 0, :], half), half_units(gate[j][:], half), half_units(value[j][:, 0:T], half), MULT)
+                    nc.scalar.copy(
+                        hq[:].rearrange("p (u h t) j -> p u h t j", h=2, t=P // 2)[:, :, half, :, 2:4],
+                        hb[:].rearrange("p j (u h t) -> p u h t j", h=2, t=P // 2)[:, :, half, :, 0:2],
+                    )
 
-        for j in range(3):
-            scatter_value(j, "value%d" % j)
-            nc.gpsimd.tensor_tensor(hb[:, (j + 2) % 3, :], gate[j][:], value[j][:, 0:T], MULT)
-            if j == 0:
-                nc.scalar.copy(hq[:, :, 0], hb[:, 2, :])
-        nc.scalar.copy(hq[:, :, 1:4], hb[:].rearrange("p j t -> p t j"))
-        gate.append(held([P, T], F32, "gate1"))
-        scatter_gate(0, 3)
-        scatter_value(3, "value1")
-        scatter_gate(1, 3)
-
-        w2sd = held([P, N], U8, "src_c")
-        nc.gpsimd.tensor_copy(w2sd[:].rearrange("p (j m) -> p j m", j=4), w2s[:].rearrange("p (m j) -> p j m", j=4))
+        by_j = w2s[:].rearrange("p (m j) -> p j m", j=4)
+        w2sd_rest = held([P, 3, P], U8, "w2sd_rest")
+        nc.gpsimd.tensor_copy(w2sd_rest[:], by_j[:, 1:4, :])
+        w2sd_first = held([P, P], U8, "gate2")
+        nc.gpsimd.tensor_copy(w2sd_first[:], by_j[:, 0, :])
+        w2sd = [w2sd_first[:]] + [w2sd_rest[:, j, :] for j in range(3)]
         idle = psum_tr.tile([P, N], F32, name="turned")
-        for s in range(7):
+        for s in range(6):
             nc.tensor.matmul_mx(
                 out=idle[:],
-                lhsT=gw[1][0][:, 0:P].bitcast(FP8X4),
-                lhsT_scale=gs[1][:, 0:P],
-                rhs=w2d[:].bitcast(FP4X4),
-                rhs_scale=w2sd[:],
+                lhsT=w2d[:, 0 : 2 * P].bitcast(FP4X4),
+                lhsT_scale=w2sd[0],
+                rhs=gw[1][0][:, 0:N].bitcast(FP8X4),
+                rhs_scale=gs[1][:, 0:N],
                 start=True,
                 stop=True,
             )
@@ -205,56 +207,85 @@ def tile_moe_pool_sigmoid_kernel(
         h_codes = held([P, T], U32, "h_codes")
         h_scales = held([P, T], U8, "h_scales")
         rows = out_0.rearrange("(p j) t -> p j t", j=4)
-        chunks = [slice(t0, t0 + CHUNK) for t0 in range(0, T, CHUNK)]
-        y = [held([P, 4, CHUNK], F32, "y%d" % c) for c in range(3)]
+        runs = [slice(0, 128), slice(128, 256), slice(256, 512), slice(512, 768)]
+        y = [held([P, 4, run.stop - run.start], F32, "y%d" % r) for r, run in enumerate(runs)]
         yq = held([P, T, 4], BF16, "yq")
 
-        def last_product(cols):
+        def unit(u):
+            return slice(P * u, P * (u + 1))
+
+        def y_of(u):
+            r = [i for i, run in enumerate(runs) if run.start <= P * u < run.stop][0]
+            t0 = P * u - runs[r].start
+            return r, y[r][:, :, t0 : t0 + P]
+
+        def last_product(u):
+            cols = unit(u)
             nc.vector.tensor_tensor(hq[:, cols, 3], gate[3][:, cols], value[3][:, cols], MULT)
 
-        def last_product_by_scalar(cols):
-            nc.vector.tensor_tensor(hb[:, 0, cols], gate[3][:, cols], value[3][:, cols], MULT)
-            nc.scalar.copy(hq[:, cols, 3], hb[:, 0, cols])
+        def last_product_by_scalar(u):
+            cols = unit(u)
+            nc.vector.tensor_tensor(hb[:, 1, cols], gate[3][:, cols], value[3][:, cols], MULT)
+            nc.scalar.copy(hq[:, cols, 3], hb[:, 1, cols])
 
-        def second_layer(c):
-            cols = chunks[c]
+        def second_layer(u):
+            cols = unit(u)
             nc.vector.quantize_mx(
                 out=h_codes[:, cols].bitcast(FP8X4), scales=h_scales[:, cols], in_=hq[:, cols, :].rearrange("p t j -> p (t j)")
             )
-            for pool, name, j0 in ((psum_y, "acc_y", 0), (psum_mm, "acc", 2)):
-                bank = pool.tile([P, 2, CHUNK], F32, name=name)
-                for j in range(j0, j0 + 2):
-                    nc.tensor.matmul_mx(
-                        out=bank[:, j - j0, :],
-                        lhsT=w2d[:, 2 * P * j : 2 * P * (j + 1)].bitcast(FP4X4),
-                        lhsT_scale=w2sd[:, P * j : P * (j + 1)],
-                        rhs=h_codes[:, cols].bitcast(FP8X4),
-                        rhs_scale=h_scales[:, cols],
-                        start=True,
-                        stop=True,
-                    )
-                nc.scalar.copy(y[c][:, j0 : j0 + 2, :], bank[:])
-                nc.sync.dma_start(rows[:, j0 : j0 + 2, cols], y[c][:, j0 : j0 + 2, :])
+            bank = psum_y.tile([P, 4, P], F32, name="acc_y") if u % 2 == 0 else psum_mm.tile([P, 4, P], F32, name="acc")
+            for j in range(4):
+                nc.tensor.matmul_mx(
+                    out=bank[:, j, :],
+                    lhsT=w2d[:, 2 * P * j : 2 * P * (j + 1)].bitcast(FP4X4),
+                    lhsT_scale=w2sd[j],
+                    rhs=h_codes[:, cols].bitcast(FP8X4),
+                    rhs_scale=h_scales[:, cols],
+                    start=True,
+                    stop=True,
+                )
+            r, dest = y_of(u)
+            nc.scalar.copy(dest, bank[:])
+            if P * (u + 1) == runs[r].stop:
+                nc.sync.dma_start(rows[:, :, runs[r]], y[r][:])
 
-        def result_planes(c):
-            cols = chunks[c]
-            nc.vector.tensor_copy(yq[:, cols, :], y[c][:].rearrange("p j t -> p t j"))
+        def round_result(u):
+            nc.vector.tensor_copy(yq[:, unit(u), :], y_of(u)[1].rearrange("p j t -> p t j"))
+
+        def quantise_result(u):
+            cols = slice(P * u, P * (u + 2))
             nc.vector.quantize_mx(
                 out=y_codes[:, cols].bitcast(FP8X4), scales=y_scales[:, cols], in_=yq[:, cols, :].rearrange("p t j -> p (t j)")
             )
+
+        def store_codes(cols):
             nc.sync.dma_start(
                 out_1[0, :, cols, :].rearrange("p t d -> p (t d)").bitcast(I32), y_codes[:, cols].bitcast(I32)
             )
 
-        last_product_by_scalar(slice(P, CHUNK))
-        last_product(slice(0, P))
-        last_product_by_scalar(chunks[1])
+        last_product_by_scalar(1)
+        last_product(0)
+        last_product_by_scalar(2)
         second_layer(0)
-        last_product(chunks[2])
         second_layer(1)
+        last_product(3)
         second_layer(2)
-        for c in range(3):
-            result_planes(c)
+        last_product(4)
+        second_layer(3)
+        last_product(5)
+        second_layer(4)
+        round_result(0)
+        second_layer(5)
+        round_result(1)
+        round_result(2)
+        quantise_result(0)
+        round_result(3)
+        round_result(4)
+        quantise_result(2)
+        store_codes(slice(0, 4 * P))
+        round_result(5)
+        quantise_result(4)
+        store_codes(slice(4 * P, T))
         for q in range(4):
             queue = nc.scalar if q % 2 else nc.sync
             queue.dma_start(out_2[0, 4 * q : 4 * q + 4, :].bitcast(I32), y_scales[32 * q : 32 * q + 4].bitcast(I32))

@@ -142,7 +142,7 @@ def tile_moe_pool_sigmoid_kernel(
                 nc.tensor.transpose(turned[:, j, :], dealt[:, j, :], ident[:])
             nc.scalar.copy(dest, turned[:])
 
-        pieces = [slice(e * C1, (e + 1) * C1) for e in range(E1)]
+        pieces = [slice(0, C1), slice(C1, T)]
         src_a = held([P, 4, T], F32, "src_a")
         for e in range(E1):
             for u in range(C1 // P):
@@ -158,11 +158,12 @@ def tile_moe_pool_sigmoid_kernel(
                 [wbs[:, f * PASSES + s, :] for s in range(PASSES)], src_c[:, :, f * C2 : (f + 1) * C2], False,
             )
 
-        gate = [held([P, T], F32, "gate%d" % j) for j in range(4)]
+        gate = [held([P, T if j < 3 else WIDE], F32, "gate%d" % j) for j in range(4)]
         for piece in pieces:
-            for j in range(4):
+            for j in range(3):
                 cols = slice(piece.start // 16, piece.stop // 16)
                 nc.vector.tensor_copy(gate[j][:].indirect(list_a[:, cols]), src_a[:, j, piece])
+        nc.vector.tensor_copy(gate[3][:].indirect(list_a[:]), src_a[:, 3, :])
 
         hq = held([P, T, 4], BF16, "hq")
         hb = held([P, 3, T], BF16, "hb")
@@ -207,7 +208,7 @@ def tile_moe_pool_sigmoid_kernel(
         h_codes = held([P, T], U32, "h_codes")
         h_scales = held([P, T], U8, "h_scales")
         rows = out_0.rearrange("(p j) t -> p j t", j=4)
-        runs = [slice(0, 128), slice(128, 256), slice(256, 512), slice(512, 768)]
+        runs = [slice(0, 128), slice(128, 256), slice(256, 512), slice(512, 640), slice(640, 768)]
         y = [held([P, 4, run.stop - run.start], F32, "y%d" % r) for r, run in enumerate(runs)]
         yq = held([P, T, 4], BF16, "yq")
 

@@ -98,8 +98,9 @@ def tile_moe_pool_sigmoid_kernel(
         lists = [list_a, list_b]
         gw = [[held([P, T], U32, "gw%d%d" % (l, s)) for s in range(PASSES)] for l in range(2)]
 
-        def gather_words(l, s):
-            nc.vector.tensor_copy(gw[l][s][:], xw[s][:].bitcast(U32).indirect(lists[l][:]))
+        def gather_words(l, s, slots=slice(0, T)):
+            offsets = lists[l][:, slots.start // 16 : slots.stop // 16]
+            nc.vector.tensor_copy(gw[l][s][:, slots], xw[s][:].bitcast(U32).indirect(offsets))
 
         def gather_scales(l, queue):
             nc.vector.tensor_copy(gs[l][:], xs[:].indirect(lists[l][:]))
@@ -107,8 +108,9 @@ def tile_moe_pool_sigmoid_kernel(
                 queue.dma_start(gs1[l][32 * q : 32 * q + 4].bitcast(I32), gs[l][32 * q + 4 : 32 * q + 8].bitcast(I32))
 
         gather_scales(0, nc.scalar)
-        gather_words(0, 0)
-        gather_words(0, 1)
+        for slots in (slice(0, C1), slice(C1, T)):
+            for s in range(PASSES):
+                gather_words(0, s, slots)
         gather_scales(1, nc.sync)
         gather_words(1, 0)
         gather_words(1, 1)
@@ -142,7 +144,7 @@ def tile_moe_pool_sigmoid_kernel(
                 nc.tensor.transpose(turned[:, j, :], dealt[:, j, :], ident[:])
             nc.scalar.copy(dest, turned[:])
 
-        pieces = [slice(0, C1), slice(C1, T)]
+        pieces = [slice(e * C1, (e + 1) * C1) for e in range(E1)]
         src_a = held([P, 4, T], F32, "src_a")
         for e in range(E1):
             for u in range(C1 // P):
@@ -158,12 +160,20 @@ def tile_moe_pool_sigmoid_kernel(
                 [wbs[:, f * PASSES + s, :] for s in range(PASSES)], src_c[:, :, f * C2 : (f + 1) * C2], False,
             )
 
-        gate = [held([P, T if j < 3 else WIDE], F32, "gate%d" % j) for j in range(4)]
+        gate = [held([P, T], F32, "gate%d" % j) for j in range(4)]
         for piece in pieces:
-            for j in range(3):
+            for j in range(4):
                 cols = slice(piece.start // 16, piece.stop // 16)
                 nc.vector.tensor_copy(gate[j][:].indirect(list_a[:, cols]), src_a[:, j, piece])
-        nc.vector.tensor_copy(gate[3][:].indirect(list_a[:]), src_a[:, 3, :])
+
+        there = psum_tr.tile([P, 3, P], F32, name="turned")
+        for u in range(3):
+            nc.tensor.transpose(there[:, u, :], gate[3][:, P * u : P * (u + 1)], ident[:])
+        gate_turned = ring.tile([P, 3, P], F32, name="dealt")
+        nc.scalar.copy(gate_turned[:], there[:])
+        gate_bank = psum_tr.tile([P, 3, P], F32, name="turned")
+        for u in range(3):
+            nc.tensor.transpose(gate_bank[:, u, :], gate_turned[:, u, :], ident[:])
 
         hq = held([P, T, 4], BF16, "hq")
         hb = held([P, 3, T], BF16, "hb")
@@ -208,36 +218,34 @@ def tile_moe_pool_sigmoid_kernel(
         h_codes = held([P, T], U32, "h_codes")
         h_scales = held([P, T], U8, "h_scales")
         rows = out_0.rearrange("(p j) t -> p j t", j=4)
-        runs = [slice(0, 128), slice(128, 256), slice(256, 512), slice(512, 640), slice(640, 768)]
+        runs = [slice(0, 128), slice(128, 256), slice(256, 512), slice(512, 768)]
         y = [held([P, 4, run.stop - run.start], F32, "y%d" % r) for r, run in enumerate(runs)]
         yq = held([P, T, 4], BF16, "yq")
 
         def unit(u):
             return slice(P * u, P * (u + 1))
 
-        def y_of(u):
-            r = [i for i, run in enumerate(runs) if run.start <= P * u < run.stop][0]
-            t0 = P * u - runs[r].start
-            return r, y[r][:, :, t0 : t0 + P]
+        def gate_of(u):
+            return gate_bank[:, u, :] if u < 3 else gate[3][:, unit(u)]
 
-        def last_product(u):
-            cols = unit(u)
-            nc.vector.tensor_tensor(hq[:, cols, 3], gate[3][:, cols], value[3][:, cols], MULT)
+        def last_product(engine, u):
+            engine.tensor_tensor(hq[:, unit(u), 3], value[3][:, unit(u)], gate_of(u), MULT)
 
         def last_product_by_scalar(u):
             cols = unit(u)
-            nc.vector.tensor_tensor(hb[:, 1, cols], gate[3][:, cols], value[3][:, cols], MULT)
+            nc.vector.tensor_tensor(hb[:, 1, cols], value[3][:, cols], gate_of(u), MULT)
             nc.scalar.copy(hq[:, cols, 3], hb[:, 1, cols])
 
-        def second_layer(u):
-            cols = unit(u)
+        def quantise(codes, scales, values, cols):
             nc.vector.quantize_mx(
-                out=h_codes[:, cols].bitcast(FP8X4), scales=h_scales[:, cols], in_=hq[:, cols, :].rearrange("p t j -> p (t j)")
+                out=codes[:, cols].bitcast(FP8X4), scales=scales[:, cols], in_=values[:, cols, :].rearrange("p t j -> p (t j)")
             )
-            bank = psum_y.tile([P, 4, P], F32, name="acc_y") if u % 2 == 0 else psum_mm.tile([P, 4, P], F32, name="acc")
-            for j in range(4):
+
+        def multiply(pool, name, cols, j0, j1, dest):
+            bank = pool.tile([P, j1 - j0, cols.stop - cols.start], F32, name=name)
+            for j in range(j0, j1):
                 nc.tensor.matmul_mx(
-                    out=bank[:, j, :],
+                    out=bank[:, j - j0, :],
                     lhsT=w2d[:, 2 * P * j : 2 * P * (j + 1)].bitcast(FP4X4),
                     lhsT_scale=w2sd[j],
                     rhs=h_codes[:, cols].bitcast(FP8X4),
@@ -245,48 +253,51 @@ def tile_moe_pool_sigmoid_kernel(
                     start=True,
                     stop=True,
                 )
-            r, dest = y_of(u)
             nc.scalar.copy(dest, bank[:])
-            if P * (u + 1) == runs[r].stop:
-                nc.sync.dma_start(rows[:, :, runs[r]], y[r][:])
 
-        def round_result(u):
-            nc.vector.tensor_copy(yq[:, unit(u), :], y_of(u)[1].rearrange("p j t -> p t j"))
+        def second_layer_by_pairs(r):
+            quantise(h_codes, h_scales, hq, runs[r])
+            for pool, name, j0 in ((psum_y, "acc_y", 0), (psum_mm, "acc", 2)):
+                multiply(pool, name, runs[r], j0, j0 + 2, y[r][:, j0 : j0 + 2, :])
+                nc.sync.dma_start(rows[:, j0 : j0 + 2, runs[r]], y[r][:, j0 : j0 + 2, :])
 
-        def quantise_result(u):
-            cols = slice(P * u, P * (u + 2))
-            nc.vector.quantize_mx(
-                out=y_codes[:, cols].bitcast(FP8X4), scales=y_scales[:, cols], in_=yq[:, cols, :].rearrange("p t j -> p (t j)")
-            )
+        def second_layer_by_units(r):
+            quantise(h_codes, h_scales, hq, runs[r])
+            for t0 in range(0, runs[r].stop - runs[r].start, P):
+                cols = slice(runs[r].start + t0, runs[r].start + t0 + P)
+                pool, name = (psum_mm, "acc") if t0 else (psum_y, "acc_y")
+                multiply(pool, name, cols, 0, 4, y[r][:, :, t0 : t0 + P])
+            nc.sync.dma_start(rows[:, :, runs[r]], y[r][:])
+
+        def round_result(r, t0, t1, copy=nc.vector.tensor_copy):
+            cols = slice(runs[r].start + t0, runs[r].start + t1)
+            copy(yq[:, cols, :], y[r][:, :, t0:t1].rearrange("p j t -> p t j"))
 
         def store_codes(cols):
             nc.sync.dma_start(
                 out_1[0, :, cols, :].rearrange("p t d -> p (t d)").bitcast(I32), y_codes[:, cols].bitcast(I32)
             )
 
+        last_product(nc.gpsimd, 3)
+        last_product(nc.vector, 0)
         last_product_by_scalar(1)
-        last_product(0)
-        last_product_by_scalar(2)
-        second_layer(0)
-        second_layer(1)
-        last_product(3)
-        second_layer(2)
-        last_product(4)
-        second_layer(3)
-        last_product(5)
-        second_layer(4)
-        round_result(0)
-        second_layer(5)
-        round_result(1)
-        round_result(2)
-        quantise_result(0)
-        round_result(3)
-        round_result(4)
-        quantise_result(2)
+        second_layer_by_pairs(0)
+        last_product(nc.vector, 2)
+        second_layer_by_units(1)
+        second_layer_by_pairs(2)
+        last_product(nc.vector, 4)
+        last_product(nc.vector, 5)
+        round_result(0, 0, P)
+        second_layer_by_pairs(3)
+        round_result(1, 0, P)
+        quantise(y_codes, y_scales, yq, slice(0, 2 * P))
+        round_result(2, 0, 2 * P)
+        quantise(y_codes, y_scales, yq, runs[2])
         store_codes(slice(0, 4 * P))
-        round_result(5)
-        quantise_result(4)
-        store_codes(slice(4 * P, T))
+        round_result(3, 0, P)
+        round_result(3, P, 2 * P, nc.scalar.copy)
+        quantise(y_codes, y_scales, yq, runs[3])
+        store_codes(runs[3])
         for q in range(4):
             queue = nc.scalar if q % 2 else nc.sync
             queue.dma_start(out_2[0, 4 * q : 4 * q + 4, :].bitcast(I32), y_scales[32 * q : 32 * q + 4].bitcast(I32))

@@ -47,13 +47,10 @@ def tile_moe_pool_sigmoid_kernel(
         gs = [held([P, T], U8, "gs%d" % l) for l in range(2)]
         gs1 = [held([P, T], U8, "gs1%d" % l) for l in range(2)]
         ident = held([P, P], F32, "ident")
-        warm = held([P, 2], F32, "warm")
 
         nc.gpsimd.memset(xs[:].bitcast(I32), 0)
         nc.gpsimd.memset(xw[0][:, T:WIDE], 0)
         nc.gpsimd.memset(was[:].bitcast(I32), 0)
-        nc.gpsimd.memset(warm[:, 1:2], 0.0)
-        nc.scalar.activation(warm[:, 0:1], warm[:, 1:2], SIGMOID)
         nc.gpsimd.memset(xw[1][:, T:WIDE], 0)
         nc.gpsimd.memset(gs1[0][:].bitcast(I32), 0)
         make_identity(nc, ident[:])
@@ -195,23 +192,9 @@ def tile_moe_pool_sigmoid_kernel(
                         hb[:].rearrange("p j (u h t) -> p u h t j", h=2, t=P // 2)[:, :, half, :, 0:2],
                     )
 
-        by_j = w2s[:].rearrange("p (m j) -> p j m", j=4)
-        w2sd_rest = held([P, 3, P], U8, "w2sd_rest")
-        nc.gpsimd.tensor_copy(w2sd_rest[:], by_j[:, 1:4, :])
-        w2sd_first = held([P, P], U8, "gate2")
-        nc.gpsimd.tensor_copy(w2sd_first[:], by_j[:, 0, :])
-        w2sd = [w2sd_first[:]] + [w2sd_rest[:, j, :] for j in range(3)]
-        idle = psum_tr.tile([P, N], F32, name="turned")
-        for s in range(6):
-            nc.tensor.matmul_mx(
-                out=idle[:],
-                lhsT=w2d[:, 0 : 2 * P].bitcast(FP4X4),
-                lhsT_scale=w2sd[0],
-                rhs=gw[1][0][:, 0:N].bitcast(FP8X4),
-                rhs_scale=gs[1][:, 0:N],
-                start=True,
-                stop=True,
-            )
+        w2sd_all = held([P, 4, P], U8, "w2sd_all")
+        nc.gpsimd.tensor_copy(w2sd_all[:], w2s[:].rearrange("p (m j) -> p j m", j=4))
+        w2sd = [w2sd_all[:, j, :] for j in range(4)]
 
         y_codes = held([P, T], U32, "y_codes")
         y_scales = held([P, T], U8, "y_scales")

@@ -42,30 +42,21 @@ def tile_moe_pool_sigmoid_kernel(
         xs = held([P, WIDE], U8, "xs")
         xw = [held([P, WIDE], I32, "xw%d" % s) for s in range(PASSES)]
         was = held([P, E1 * PASSES, H], U8, "was")
-        wbs = held([P, E2 * PASSES, H], U8, "wbs")
-        w2s = held([P, N], U8, "w2s")
-        gs = [held([P, T], U8, "gs%d" % l) for l in range(2)]
-        gs1 = [held([P, T], U8, "gs1%d" % l) for l in range(2)]
+        planes = [[held([P, T], U8, "plane%d%d" % (s, l)) for l in range(2)] for s in range(PASSES)]
         ident = held([P, P], F32, "ident")
 
-        nc.gpsimd.memset(xs[:].bitcast(I32), 0)
+        nc.gpsimd.memset(xs[64:128].bitcast(I32), 0)
+        nc.gpsimd.memset(xs[32:64].bitcast(I32), 0)
+        nc.gpsimd.memset(xs[0:32, T:WIDE].bitcast(I32), 0)
         nc.gpsimd.memset(xw[0][:, T:WIDE], 0)
-        nc.gpsimd.memset(was[:].bitcast(I32), 0)
         nc.gpsimd.memset(xw[1][:, T:WIDE], 0)
-        nc.gpsimd.memset(gs1[0][:].bitcast(I32), 0)
         make_identity(nc, ident[:])
-        nc.gpsimd.memset(wbs[:].bitcast(I32), 0)
-        nc.gpsimd.memset(gs1[1][:].bitcast(I32), 0)
-        nc.gpsimd.memset(w2s[:].bitcast(I32), 0)
 
         def load_x(s):
             nc.sync.dma_start(xw[s][:, 0:T], x_words[s].rearrange("p t d -> p (t d)").bitcast(I32))
 
         nc.sync.dma_start(list_a[:], offs)
-        for q in range(4):
-            nc.sync.dma_start(
-                xs[32 * q : 32 * q + 8, 0:T].bitcast(I32), x_scales[:, 4 * q : 4 * q + 4, :].bitcast(I32)
-            )
+        nc.sync.dma_start(xs[0:32, 0:T].bitcast(I32), x_scales.rearrange("s b t -> (s b) t").bitcast(I32))
         load_x(0)
         load_x(1)
         nc.sync.dma_start(list_b[:], offs2)
@@ -77,20 +68,13 @@ def tile_moe_pool_sigmoid_kernel(
                     scales[:, :, 4 * q : 4 * q + 4, :].rearrange("e s r i -> r (e s) i").bitcast(I32),
                 )
 
-        def load_words(words, name):
-            experts = words.shape[0]
-            tile = held([P, experts * PASSES, 2 * H], U8, name)
-            nc.sync.dma_start(tile[:].bitcast(I32), words.rearrange("e s p n -> p (e s) n").bitcast(I32))
+        def load_words(words, tile):
+            nc.sync.dma_start(tile.bitcast(I32), words.rearrange("e s p n -> p (e s) n").bitcast(I32))
             return tile
 
+        wa0 = held([P, PASSES, 2 * H], U8, "wa0")
+        wa = [load_words(wa_words[0:1], wa0[:])]
         load_scales(was, wa_scales)
-        wa = [load_words(wa_words[e : e + 1], "wa%d" % e) for e in range(E1)]
-        load_scales(wbs, wb_scales)
-        wb = [load_words(wb_words[2 * g : 2 * g + 2], "wb%d" % g) for g in range(E2 // 2)]
-        w2 = held([P, 2 * N], U8, "w2")
-        nc.sync.dma_start(w2[:].bitcast(I32), w2_words[0].bitcast(I32))
-        for q in range(4):
-            nc.sync.dma_start(w2s[32 * q : 32 * q + 4].bitcast(I32), w2_scales[0, 4 * q : 4 * q + 4, :].bitcast(I32))
 
         lists = [list_a, list_b]
         gw = [[held([P, T], U32, "gw%d%d" % (l, s)) for s in range(PASSES)] for l in range(2)]
@@ -99,23 +83,38 @@ def tile_moe_pool_sigmoid_kernel(
             offsets = lists[l][:, slots.start // 16 : slots.stop // 16]
             nc.vector.tensor_copy(gw[l][s][:, slots], xw[s][:].bitcast(U32).indirect(offsets))
 
-        def gather_scales(l, queue):
-            nc.vector.tensor_copy(gs[l][:], xs[:].indirect(lists[l][:]))
-            for q in range(4):
-                queue.dma_start(gs1[l][32 * q : 32 * q + 4].bitcast(I32), gs[l][32 * q + 4 : 32 * q + 8].bitcast(I32))
+        def gather_scales(l, queue, name):
+            gs = held([P, T], U8, name)
+            nc.vector.tensor_copy(gs[:], xs[:].indirect(lists[l][:]))
+            for s in range(PASSES):
+                for q in range(4):
+                    row = 16 * s + 4 * q
+                    queue.dma_start(planes[s][l][32 * q : 32 * q + 4].bitcast(I32), gs[row : row + 4].bitcast(I32))
 
-        gather_scales(0, nc.scalar)
+        gather_scales(0, nc.sync, "late")
+        late = held([P, 24, 2 * H], U8, "late")
+        for e in range(1, E1):
+            wa.append(load_words(wa_words[e : e + 1], late[:, 2 * e - 2 : 2 * e, :]))
+        wbs = late[:, 16:22, :].rearrange("p a (b i) -> p (a b) i", b=2)
+        load_scales(wbs, wb_scales)
+        wb = [load_words(wb_words[2 * g : 2 * g + 2], late[:, 4 + 4 * g : 8 + 4 * g, :]) for g in range(E2 // 2)]
+        w2 = late[:, 22, :]
+        w2s = late[:, 23, 0:N]
+        nc.gpsimd.memset(w2s.bitcast(I32), 0)
+        nc.sync.dma_start(w2.bitcast(I32), w2_words[0].bitcast(I32))
+        for q in range(4):
+            nc.sync.dma_start(w2s[32 * q : 32 * q + 4].bitcast(I32), w2_scales[0, 4 * q : 4 * q + 4, :].bitcast(I32))
+
         for slots in (slice(0, C1), slice(C1, T)):
             for s in range(PASSES):
                 gather_words(0, s, slots)
-        gather_scales(1, nc.sync)
+        gather_scales(1, nc.sync, "gs1")
         gather_words(1, 0)
         gather_words(1, 1)
-        planes = [gs, gs1]
 
         w2d = held([P, 2 * N], U8, "w2d")
         nc.gpsimd.tensor_copy(
-            w2d[:].rearrange("p (j m b) -> p j m b", j=4, b=2), w2[:].rearrange("p (m j b) -> p j m b", j=4, b=2)
+            w2d[:].rearrange("p (j m b) -> p j m b", j=4, b=2), w2.rearrange("p (m j b) -> p j m b", j=4, b=2)
         )
 
         def expert_tile(l, slot0, words, scales, dest, gate):
@@ -193,7 +192,7 @@ def tile_moe_pool_sigmoid_kernel(
                     )
 
         w2sd_all = held([P, 4, P], U8, "w2sd_all")
-        nc.gpsimd.tensor_copy(w2sd_all[:], w2s[:].rearrange("p (m j) -> p j m", j=4))
+        nc.gpsimd.tensor_copy(w2sd_all[:], w2s.rearrange("p (m j) -> p j m", j=4))
         w2sd = [w2sd_all[:, j, :] for j in range(4)]
 
         y_codes = held([P, T], U32, "y_codes")

@@ -56,7 +56,7 @@ def tile_moe_pool_sigmoid_kernel(
             nc.sync.dma_start(xw[s][:, 0:T], x_words[s].rearrange("p t d -> p (t d)").bitcast(I32))
 
         nc.sync.dma_start(list_a[:], offs)
-        nc.sync.dma_start(xs[0:32, 0:T].bitcast(I32), x_scales.rearrange("s b t -> (s b) t").bitcast(I32))
+        nc.scalar.dma_start(xs[0:32, 0:T].bitcast(I32), x_scales.rearrange("s b t -> (s b) t").bitcast(I32))
         load_x(0)
         load_x(1)
         nc.sync.dma_start(list_b[:], offs2)
@@ -117,7 +117,7 @@ def tile_moe_pool_sigmoid_kernel(
             w2d[:].rearrange("p (j m b) -> p j m b", j=4, b=2), w2.rearrange("p (m j b) -> p j m b", j=4, b=2)
         )
 
-        def expert_tile(l, slot0, words, scales, dest, gate):
+        def expert_tile(l, slot0, words, scales, dest, gate, place):
             acc = psum_mm.tile([P, H], F32, name="acc")
             for s in range(PASSES):
                 nc.tensor.matmul_mx(
@@ -137,23 +137,27 @@ def tile_moe_pool_sigmoid_kernel(
                 nc.scalar.copy(dealt[:], by_j)
             turned = psum_tr.tile([P, 4, P], F32, name="turned")
             for j in range(4):
-                nc.tensor.transpose(turned[:, j, :], dealt[:, j, :], ident[:])
-            nc.scalar.copy(dest, turned[:])
+                nc.tensor.transpose(turned[:, place[j], :], dealt[:, j, :], ident[:])
+            for first, part in dest:
+                nc.scalar.copy(part, turned[:, first : first + part.shape[1], :])
 
-        pieces = [slice(e * C1, (e + 1) * C1) for e in range(E1)]
+        pieces = [slice(0, P), slice(P, C1), slice(C1, 2 * C1), slice(2 * C1, T)]
         src_a = held([P, 4, T], F32, "src_a")
         for e in range(E1):
             for u in range(C1 // P):
                 slot0 = e * C1 + u * P
                 expert_tile(
                     0, slot0, [wa[e][:, s, :] for s in range(PASSES)],
-                    [was[:, e * PASSES + s, :] for s in range(PASSES)], src_a[:, :, slot0 : slot0 + P], True,
+                    [was[:, e * PASSES + s, :] for s in range(PASSES)], [(0, src_a[:, :, slot0 : slot0 + P])], True, [0, 1, 2, 3],
                 )
-        src_c = held([P, 4, T], F32, "src_c")
+        src_c = held([P, 3, T], F32, "src_c")
+        src_third = held([P, 1, T], F32, "src_third")
+        sources = [src_c[:, 0, :], src_c[:, 1, :], src_third[:, 0, :], src_c[:, 2, :]]
         for f in range(E2):
             expert_tile(
                 1, f * C2, [wb[f // 2][:, (f % 2) * PASSES + s, :] for s in range(PASSES)],
-                [wbs[:, f * PASSES + s, :] for s in range(PASSES)], src_c[:, :, f * C2 : (f + 1) * C2], False,
+                [wbs[:, f * PASSES + s, :] for s in range(PASSES)],
+                [(0, src_c[:, :, f * C2 : (f + 1) * C2]), (3, src_third[:, :, f * C2 : (f + 1) * C2])], False, [0, 1, 3, 2],
             )
 
         gate = [held([P, T], F32, "gate%d" % j) for j in range(4)]
@@ -163,33 +167,40 @@ def tile_moe_pool_sigmoid_kernel(
                 nc.vector.tensor_copy(gate[j][:].indirect(list_a[:, cols]), src_a[:, j, piece])
 
         there = psum_tr.tile([P, 3, P], F32, name="turned")
+        banked = [0, 2, 3]
         for u in range(3):
-            nc.tensor.transpose(there[:, u, :], gate[3][:, P * u : P * (u + 1)], ident[:])
-        gate_turned = ring.tile([P, 3, P], F32, name="dealt")
-        nc.scalar.copy(gate_turned[:], there[:])
-        gate_bank = psum_tr.tile([P, 3, P], F32, name="turned")
-        for u in range(3):
-            nc.tensor.transpose(gate_bank[:, u, :], gate_turned[:, u, :], ident[:])
+            nc.tensor.transpose(there[:, u, :], gate[3][:, P * banked[u] : P * (banked[u] + 1)], ident[:])
 
         hq = held([P, T, 4], BF16, "hq")
-        hb = held([P, 3, T], BF16, "hb")
+        hb = held([P, 2, T], BF16, "hb")
 
         def half_units(row, half):
             return row.rearrange("p (u h t) -> p u h t", h=2, t=P // 2)[:, :, half, :]
 
         value = [held([P, WIDE], F32, "value%d" % j) for j in range(4)]
         for j in range(4):
-            nc.vector.tensor_copy(value[j][:].indirect(list_b[:]), src_c[:, j, :])
+            nc.vector.tensor_copy(value[j][:].indirect(list_b[:]), sources[j])
             if j < 2:
-                nc.gpsimd.tensor_tensor(hb[:, j + 1, :], gate[j][:], value[j][:, 0:T], MULT)
-                nc.scalar.copy(hq[:, :, j], hb[:, j + 1, :])
+                nc.gpsimd.tensor_tensor(hq[:, :, j], gate[j][:], value[j][:, 0:T], MULT)
             if j == 2:
                 for half in range(2):
                     nc.gpsimd.tensor_tensor(half_units(hb[:, 0, :], half), half_units(gate[j][:], half), half_units(value[j][:, 0:T], half), MULT)
                     nc.scalar.copy(
                         hq[:].rearrange("p (u h t) j -> p u h t j", h=2, t=P // 2)[:, :, half, :, 2:4],
-                        hb[:].rearrange("p j (u h t) -> p u h t j", h=2, t=P // 2)[:, :, half, :, 0:2],
+                        half_units(hb[:, 0, :], half).unsqueeze(3).to_broadcast([P, T // P, P // 2, 2]),
                     )
+
+        gate_turned = held([P, 3, P], F32, "src_third")
+        nc.scalar.copy(gate_turned[:], there[:])
+        gate_bank = psum_tr.tile([P, 3, P], F32, name="turned")
+        for u in range(3):
+            nc.tensor.transpose(gate_bank[:, u, :], gate_turned[:, u, :], ident[:])
+        warm = psum_tr.tile([P, H], F32, name="turned")
+        for repeat in range(7):
+            nc.tensor.matmul_mx(
+                out=warm[:], lhsT=gw[0][0][:, 0:P].bitcast(FP8X4), lhsT_scale=planes[0][0][:, 0:P],
+                rhs=wa[0][:, 0, :].bitcast(FP4X4), rhs_scale=was[:, 0, :], start=True, stop=True,
+            )
 
         w2sd_all = held([P, 4, P], U8, "w2sd_all")
         nc.gpsimd.tensor_copy(w2sd_all[:], w2s.rearrange("p (m j) -> p j m", j=4))
@@ -208,14 +219,14 @@ def tile_moe_pool_sigmoid_kernel(
             return slice(P * u, P * (u + 1))
 
         def gate_of(u):
-            return gate_bank[:, u, :] if u < 3 else gate[3][:, unit(u)]
+            return gate_bank[:, banked.index(u), :] if u in banked else gate[3][:, unit(u)]
 
         def last_product(engine, u):
             engine.tensor_tensor(hq[:, unit(u), 3], value[3][:, unit(u)], gate_of(u), MULT)
 
-        def last_product_by_scalar(u):
-            cols = unit(u)
-            nc.vector.tensor_tensor(hb[:, 1, cols], value[3][:, cols], gate_of(u), MULT)
+        def last_product_by_scalar(cols):
+            gates = gate_bank[:, 1:3, :].rearrange("p u t -> p (u t)")
+            nc.vector.tensor_tensor(hb[:, 1, cols], value[3][:, cols], gates, MULT)
             nc.scalar.copy(hq[:, cols, 3], hb[:, 1, cols])
 
         def quantise(codes, scales, values, cols):
@@ -237,11 +248,11 @@ def tile_moe_pool_sigmoid_kernel(
                 )
             nc.scalar.copy(dest, bank[:])
 
-        def second_layer_by_pairs(r):
+        def second_layer_by_pairs(r, cut=2):
             quantise(h_codes, h_scales, hq, runs[r])
-            for pool, name, j0 in ((psum_y, "acc_y", 0), (psum_mm, "acc", 2)):
-                multiply(pool, name, runs[r], j0, j0 + 2, y[r][:, j0 : j0 + 2, :])
-                nc.sync.dma_start(rows[:, j0 : j0 + 2, runs[r]], y[r][:, j0 : j0 + 2, :])
+            for pool, name, j0, j1 in ((psum_y, "acc_y", 0, cut), (psum_mm, "acc", cut, 4)):
+                multiply(pool, name, runs[r], j0, j1, y[r][:, j0:j1, :])
+                nc.sync.dma_start(rows[:, j0:j1, runs[r]], y[r][:, j0:j1, :])
 
         def second_layer_by_units(r):
             quantise(h_codes, h_scales, hq, runs[r])
@@ -260,14 +271,13 @@ def tile_moe_pool_sigmoid_kernel(
                 out_1[0, :, cols, :].rearrange("p t d -> p (t d)").bitcast(I32), y_codes[:, cols].bitcast(I32)
             )
 
-        last_product(nc.gpsimd, 3)
+        last_product(nc.gpsimd, 1)
         last_product(nc.vector, 0)
-        last_product_by_scalar(1)
-        second_layer_by_pairs(0)
-        last_product(nc.vector, 2)
+        last_product_by_scalar(runs[2])
+        second_layer_by_pairs(0, 1)
         second_layer_by_units(1)
-        second_layer_by_pairs(2)
         last_product(nc.vector, 4)
+        second_layer_by_pairs(2)
         last_product(nc.vector, 5)
         round_result(0, 0, P)
         second_layer_by_pairs(3)

@@ -166,9 +166,9 @@ def tile_moe_pool_sigmoid_kernel(
                 cols = slice(piece.start // 16, piece.stop // 16)
                 nc.vector.tensor_copy(gate[j][:].indirect(list_a[:, cols]), src_a[:, j, piece])
 
-        there = psum_tr.tile([P, 3, P], F32, name="turned")
-        banked = [0, 2, 3]
-        for u in range(3):
+        there = psum_tr.tile([P, 4, P], F32, name="turned")
+        banked = [0, 2, 3, 4]
+        for u in range(4):
             nc.tensor.transpose(there[:, u, :], gate[3][:, P * banked[u] : P * (banked[u] + 1)], ident[:])
 
         hq = held([P, T, 4], BF16, "hq")
@@ -190,10 +190,10 @@ def tile_moe_pool_sigmoid_kernel(
                         half_units(hb[:, 0, :], half).unsqueeze(3).to_broadcast([P, T // P, P // 2, 2]),
                     )
 
-        gate_turned = held([P, 3, P], F32, "src_third")
+        gate_turned = held([P, 4, P], F32, "src_third")
         nc.scalar.copy(gate_turned[:], there[:])
-        gate_bank = psum_tr.tile([P, 3, P], F32, name="turned")
-        for u in range(3):
+        gate_bank = psum_tr.tile([P, 4, P], F32, name="turned")
+        for u in range(4):
             nc.tensor.transpose(gate_bank[:, u, :], gate_turned[:, u, :], ident[:])
         warm = psum_tr.tile([P, H], F32, name="turned")
         for repeat in range(7):
@@ -211,7 +211,7 @@ def tile_moe_pool_sigmoid_kernel(
         h_codes = held([P, T], U32, "h_codes")
         h_scales = held([P, T], U8, "h_scales")
         rows = out_0.rearrange("(p j) t -> p j t", j=4)
-        runs = [slice(0, 128), slice(128, 256), slice(256, 512), slice(512, 768)]
+        runs = [slice(0, 128), slice(128, 256), slice(256, 768)]
         y = [held([P, 4, run.stop - run.start], F32, "y%d" % r) for r, run in enumerate(runs)]
         yq = held([P, T, 4], BF16, "yq")
 
@@ -224,10 +224,9 @@ def tile_moe_pool_sigmoid_kernel(
         def last_product(engine, u):
             engine.tensor_tensor(hq[:, unit(u), 3], value[3][:, unit(u)], gate_of(u), MULT)
 
-        def last_product_by_scalar(cols):
-            gates = gate_bank[:, 1:3, :].rearrange("p u t -> p (u t)")
-            nc.vector.tensor_tensor(hb[:, 1, cols], value[3][:, cols], gates, MULT)
-            nc.scalar.copy(hq[:, cols, 3], hb[:, 1, cols])
+        def last_product_by_scalar(u):
+            nc.vector.tensor_tensor(hb[:, 1, unit(u)], value[3][:, unit(u)], gate_of(u), MULT)
+            nc.scalar.copy(hq[:, unit(u), 3], hb[:, 1, unit(u)])
 
         def quantise(codes, scales, values, cols):
             nc.vector.quantize_mx(
@@ -264,32 +263,55 @@ def tile_moe_pool_sigmoid_kernel(
 
         def round_result(r, t0, t1, copy=nc.vector.tensor_copy):
             cols = slice(runs[r].start + t0, runs[r].start + t1)
-            copy(yq[:, cols, :], y[r][:, :, t0:t1].rearrange("p j t -> p t j"))
+            copy(
+                yq[:, cols, :].rearrange("p (c i) j -> p c j i", i=4),
+                y[r][:, :, t0:t1].rearrange("p j (c i) -> p c j i", i=4),
+            )
 
         def store_codes(cols):
             nc.sync.dma_start(
                 out_1[0, :, cols, :].rearrange("p t d -> p (t d)").bitcast(I32), y_codes[:, cols].bitcast(I32)
             )
 
+        def long_run_slice(j, copy):
+            pool, name = (psum_mm, "acc") if j in (1, 2) else (psum_y, "acc_y")
+            bank = pool.tile([P, 4 * P], F32, name=name)
+            nc.tensor.matmul_mx(
+                out=bank[:],
+                lhsT=w2d[:, 2 * P * j : 2 * P * (j + 1)].bitcast(FP4X4),
+                lhsT_scale=w2sd[j],
+                rhs=h_codes[:, runs[2]].bitcast(FP8X4),
+                rhs_scale=h_scales[:, runs[2]],
+                start=True,
+                stop=True,
+            )
+            copy(y[2][:, j, :], bank[:])
+            nc.sync.dma_start(rows[:, j, runs[2]], y[2][:, j, :])
+
         last_product(nc.gpsimd, 1)
+        last_product(nc.gpsimd, 5)
+        last_product_by_scalar(2)
         last_product(nc.vector, 0)
-        last_product_by_scalar(runs[2])
+        last_product_by_scalar(3)
         second_layer_by_pairs(0, 1)
         second_layer_by_units(1)
         last_product(nc.vector, 4)
-        second_layer_by_pairs(2)
-        last_product(nc.vector, 5)
+        quantise(h_codes, h_scales, hq, slice(2 * P, 4 * P))
+        quantise(h_codes, h_scales, hq, slice(4 * P, 6 * P))
         round_result(0, 0, P)
-        second_layer_by_pairs(3)
         round_result(1, 0, P)
+        long_run_slice(0, nc.scalar.copy)
         quantise(y_codes, y_scales, yq, slice(0, 2 * P))
+        long_run_slice(1, nc.vector.tensor_copy)
+        long_run_slice(2, nc.scalar.copy)
+        long_run_slice(3, nc.scalar.copy)
         round_result(2, 0, 2 * P)
-        quantise(y_codes, y_scales, yq, runs[2])
+        round_result(2, 3 * P, 4 * P, nc.scalar.copy)
+        round_result(2, 2 * P, 3 * P)
+        quantise(y_codes, y_scales, yq, slice(2 * P, 4 * P))
         store_codes(slice(0, 4 * P))
-        round_result(3, 0, P)
-        round_result(3, P, 2 * P, nc.scalar.copy)
-        quantise(y_codes, y_scales, yq, runs[3])
-        store_codes(runs[3])
+        quantise(y_codes, y_scales, yq, slice(4 * P, 6 * P))
+        store_codes(slice(4 * P, 6 * P))
         for q in range(4):
             queue = nc.scalar if q % 2 else nc.sync
             queue.dma_start(out_2[0, 4 * q : 4 * q + 4, :].bitcast(I32), y_scales[32 * q : 32 * q + 4].bitcast(I32))

@@ -211,7 +211,7 @@ def tile_moe_pool_sigmoid_kernel(
         h_codes = held([P, T], U32, "h_codes")
         h_scales = held([P, T], U8, "h_scales")
         rows = out_0.rearrange("(p j) t -> p j t", j=4)
-        runs = [slice(0, 128), slice(128, 256), slice(256, 768)]
+        runs = [slice(0, 256), slice(256, 768)]
         y = [held([P, 4, run.stop - run.start], F32, "y%d" % r) for r, run in enumerate(runs)]
         yq = held([P, T, 4], BF16, "yq")
 
@@ -233,7 +233,7 @@ def tile_moe_pool_sigmoid_kernel(
                 out=codes[:, cols].bitcast(FP8X4), scales=scales[:, cols], in_=values[:, cols, :].rearrange("p t j -> p (t j)")
             )
 
-        def multiply(pool, name, cols, j0, j1, dest):
+        def multiply(pool, name, cols, j0, j1, dest, copy):
             bank = pool.tile([P, j1 - j0, cols.stop - cols.start], F32, name=name)
             for j in range(j0, j1):
                 nc.tensor.matmul_mx(
@@ -245,21 +245,11 @@ def tile_moe_pool_sigmoid_kernel(
                     start=True,
                     stop=True,
                 )
-            nc.scalar.copy(dest, bank[:])
+            copy(dest, bank[:])
 
-        def second_layer_by_pairs(r, cut=2):
-            quantise(h_codes, h_scales, hq, runs[r])
-            for pool, name, j0, j1 in ((psum_y, "acc_y", 0, cut), (psum_mm, "acc", cut, 4)):
-                multiply(pool, name, runs[r], j0, j1, y[r][:, j0:j1, :])
-                nc.sync.dma_start(rows[:, j0:j1, runs[r]], y[r][:, j0:j1, :])
-
-        def second_layer_by_units(r):
-            quantise(h_codes, h_scales, hq, runs[r])
-            for t0 in range(0, runs[r].stop - runs[r].start, P):
-                cols = slice(runs[r].start + t0, runs[r].start + t0 + P)
-                pool, name = (psum_mm, "acc") if t0 else (psum_y, "acc_y")
-                multiply(pool, name, cols, 0, 4, y[r][:, :, t0 : t0 + P])
-            nc.sync.dma_start(rows[:, :, runs[r]], y[r][:])
+        def result_rows(r, j0, j1, pool, name, copy):
+            multiply(pool, name, runs[r], j0, j1, y[r][:, j0:j1, :], copy)
+            nc.sync.dma_start(rows[:, j0:j1, runs[r]], y[r][:, j0:j1, :])
 
         def round_result(r, t0, t1, copy=nc.vector.tensor_copy):
             cols = slice(runs[r].start + t0, runs[r].start + t1)
@@ -273,41 +263,30 @@ def tile_moe_pool_sigmoid_kernel(
                 out_1[0, :, cols, :].rearrange("p t d -> p (t d)").bitcast(I32), y_codes[:, cols].bitcast(I32)
             )
 
-        def long_run_slice(j, copy):
-            pool, name = (psum_mm, "acc") if j in (1, 2) else (psum_y, "acc_y")
-            bank = pool.tile([P, 4 * P], F32, name=name)
-            nc.tensor.matmul_mx(
-                out=bank[:],
-                lhsT=w2d[:, 2 * P * j : 2 * P * (j + 1)].bitcast(FP4X4),
-                lhsT_scale=w2sd[j],
-                rhs=h_codes[:, runs[2]].bitcast(FP8X4),
-                rhs_scale=h_scales[:, runs[2]],
-                start=True,
-                stop=True,
-            )
-            copy(y[2][:, j, :], bank[:])
-            nc.sync.dma_start(rows[:, j, runs[2]], y[2][:, j, :])
-
         last_product(nc.gpsimd, 1)
         last_product(nc.gpsimd, 5)
         last_product_by_scalar(2)
         last_product(nc.vector, 0)
         last_product_by_scalar(3)
-        second_layer_by_pairs(0, 1)
-        second_layer_by_units(1)
+        quantise(h_codes, h_scales, hq, runs[0])
+        result_rows(0, 0, 1, psum_y, "acc_y", nc.scalar.copy)
+        result_rows(0, 1, 2, psum_mm, "acc", nc.scalar.copy)
+        result_rows(0, 2, 3, psum_y, "acc_y", nc.scalar.copy)
+        result_rows(0, 3, 4, psum_mm, "acc", nc.scalar.copy)
         last_product(nc.vector, 4)
         quantise(h_codes, h_scales, hq, slice(2 * P, 4 * P))
         quantise(h_codes, h_scales, hq, slice(4 * P, 6 * P))
-        round_result(0, 0, P)
-        round_result(1, 0, P)
-        long_run_slice(0, nc.scalar.copy)
-        quantise(y_codes, y_scales, yq, slice(0, 2 * P))
-        long_run_slice(1, nc.vector.tensor_copy)
-        long_run_slice(2, nc.scalar.copy)
-        long_run_slice(3, nc.scalar.copy)
-        round_result(2, 0, 2 * P)
-        round_result(2, 3 * P, 4 * P, nc.scalar.copy)
-        round_result(2, 2 * P, 3 * P)
+        result_rows(1, 0, 1, psum_y, "acc_y", nc.vector.tensor_copy)
+        result_rows(1, 1, 2, psum_mm, "acc", nc.scalar.copy)
+        round_result(0, 0, 2 * P)
+        result_rows(1, 2, 3, psum_y, "acc_y", nc.scalar.copy)
+        quantise(y_codes, y_scales, yq, runs[0])
+        multiply(psum_mm, "acc", slice(2 * P, 4 * P), 3, 4, y[1][:, 3:4, 0 : 2 * P], nc.vector.tensor_copy)
+        multiply(psum_y, "acc_y", slice(4 * P, 6 * P), 3, 4, y[1][:, 3:4, 2 * P : 4 * P], nc.scalar.copy)
+        nc.sync.dma_start(rows[:, 3, runs[1]], y[1][:, 3, :])
+        round_result(1, 5 * P // 2, 4 * P, nc.scalar.copy)
+        round_result(1, 0, 2 * P)
+        round_result(1, 2 * P, 5 * P // 2)
         quantise(y_codes, y_scales, yq, slice(2 * P, 4 * P))
         store_codes(slice(0, 4 * P))
         quantise(y_codes, y_scales, yq, slice(4 * P, 6 * P))

@@ -56,7 +56,7 @@ def tile_moe_pool_sigmoid_kernel(
             nc.sync.dma_start(xw[s][:, 0:T], x_words[s].rearrange("p t d -> p (t d)").bitcast(I32))
 
         nc.sync.dma_start(list_a[:], offs)
-        nc.scalar.dma_start(xs[0:32, 0:T].bitcast(I32), x_scales.rearrange("s b t -> (s b) t").bitcast(I32))
+        nc.sync.dma_start(xs[0:32, 0:T].bitcast(I32), x_scales.rearrange("s b t -> (s b) t").bitcast(I32))
         load_x(0)
         load_x(1)
         nc.sync.dma_start(list_b[:], offs2)

@@ -61,9 +61,9 @@ def tile_moe_pool_sigmoid_kernel(
         load_x(1)
         nc.sync.dma_start(list_b[:], offs2)
 
-        def load_scales(plane, scales):
+        def load_scales(plane, scales, queue):
             for q in range(4):
-                nc.sync.dma_start(
+                queue.dma_start(
                     plane[32 * q : 32 * q + 4].bitcast(I32),
                     scales[:, :, 4 * q : 4 * q + 4, :].rearrange("e s r i -> r (e s) i").bitcast(I32),
                 )
@@ -74,7 +74,7 @@ def tile_moe_pool_sigmoid_kernel(
 
         wa0 = held([P, PASSES, 2 * H], U8, "wa0")
         wa = [load_words(wa_words[0:1], wa0[:])]
-        load_scales(was, wa_scales)
+        load_scales(was, wa_scales, nc.sync)
 
         lists = [list_a, list_b]
         gw = [[held([P, T], U32, "gw%d%d" % (l, s)) for s in range(PASSES)] for l in range(2)]
@@ -91,19 +91,20 @@ def tile_moe_pool_sigmoid_kernel(
                     row = 16 * s + 4 * q
                     queue.dma_start(planes[s][l][32 * q : 32 * q + 4].bitcast(I32), gs[row : row + 4].bitcast(I32))
 
-        gather_scales(0, nc.sync, "late")
+        gather_scales(0, nc.scalar, "late")
         late = held([P, 24, 2 * H], U8, "late")
+        load_words(wa_words[1:E1], late[:, 0:4, :])
         for e in range(1, E1):
-            wa.append(load_words(wa_words[e : e + 1], late[:, 2 * e - 2 : 2 * e, :]))
+            wa.append(late[:, 2 * e - 2 : 2 * e, :])
         wbs = late[:, 16:22, :].rearrange("p a (b i) -> p (a b) i", b=2)
-        load_scales(wbs, wb_scales)
-        wb = [load_words(wb_words[2 * g : 2 * g + 2], late[:, 4 + 4 * g : 8 + 4 * g, :]) for g in range(E2 // 2)]
+        load_scales(wbs, wb_scales, nc.gpsimd)
+        wb = load_words(wb_words, late[:, 4:16, :])
         w2 = late[:, 22, :]
         w2s = late[:, 23, 0:N]
         nc.gpsimd.memset(w2s.bitcast(I32), 0)
-        nc.sync.dma_start(w2.bitcast(I32), w2_words[0].bitcast(I32))
+        nc.gpsimd.dma_start(w2.bitcast(I32), w2_words[0].bitcast(I32))
         for q in range(4):
-            nc.sync.dma_start(w2s[32 * q : 32 * q + 4].bitcast(I32), w2_scales[0, 4 * q : 4 * q + 4, :].bitcast(I32))
+            nc.gpsimd.dma_start(w2s[32 * q : 32 * q + 4].bitcast(I32), w2_scales[0, 4 * q : 4 * q + 4, :].bitcast(I32))
 
         for slots in (slice(0, C1), slice(C1, T)):
             for s in range(PASSES):
@@ -150,14 +151,13 @@ def tile_moe_pool_sigmoid_kernel(
                     0, slot0, [wa[e][:, s, :] for s in range(PASSES)],
                     [was[:, e * PASSES + s, :] for s in range(PASSES)], [(0, src_a[:, :, slot0 : slot0 + P])], True, [0, 1, 2, 3],
                 )
-        src_c = held([P, 3, T], F32, "src_c")
-        src_third = held([P, 1, T], F32, "src_third")
-        sources = [src_c[:, 0, :], src_c[:, 1, :], src_third[:, 0, :], src_c[:, 2, :]]
+        src_c = held([P, 4, T], F32, "src_c")
+        sources = [src_c[:, j, :] for j in range(4)]
         for f in range(E2):
             expert_tile(
-                1, f * C2, [wb[f // 2][:, (f % 2) * PASSES + s, :] for s in range(PASSES)],
+                1, f * C2, [wb[:, f * PASSES + s, :] for s in range(PASSES)],
                 [wbs[:, f * PASSES + s, :] for s in range(PASSES)],
-                [(0, src_c[:, :, f * C2 : (f + 1) * C2]), (3, src_third[:, :, f * C2 : (f + 1) * C2])], False, [0, 1, 3, 2],
+                [(0, src_c[:, :, f * C2 : (f + 1) * C2])], False, [0, 1, 2, 3],
             )
 
         gate = [held([P, T], F32, "gate%d" % j) for j in range(4)]
@@ -190,8 +190,8 @@ def tile_moe_pool_sigmoid_kernel(
                         half_units(hb[:, 0, :], half).unsqueeze(3).to_broadcast([P, T // P, P // 2, 2]),
                     )
 
-        gate_turned = held([P, 4, P], F32, "src_third")
-        nc.scalar.copy(gate_turned[:], there[:])
+        gate_turned = src_c[:, 2, 0 : 4 * P].rearrange("p (u t) -> p u t", t=P)
+        nc.scalar.copy(gate_turned, there[:])
         gate_bank = psum_tr.tile([P, 4, P], F32, name="turned")
         for u in range(4):
             nc.tensor.transpose(gate_bank[:, u, :], gate_turned[:, u, :], ident[:])

@@ -12,14 +12,16 @@ U8 = mybir.dt.uint8
 FP8X4 = mybir.dt.float8_e4m3fn_x4
 FP4X4 = mybir.dt.float4_e2m1fn_x4
 SIGMOID = mybir.ActivationFunctionType.Sigmoid
+COPY = mybir.ActivationFunctionType.Copy
 MULT = mybir.AluOpType.mult
 
 P = 128
 K, T, H, N = 1024, 768, 512, 512
 E1, C1, E2, C2 = 3, 256, 6, 128
 PASSES = 2
+LANES = 4
 WIDE = 1024
-CHUNK = 256
+HALF = T // 2
 FLOPS = 2 * K * H * T * 2 + 2 * H * N * T
 
 
@@ -39,219 +41,183 @@ def tile_moe_pool_sigmoid_kernel(
 
         list_a = keep.tile([P, T // 16], U16, name="list_a")
         list_b = keep.tile([P, T // 16], U16, name="list_b")
-        xs = held([P, WIDE], U8, "xs")
-        xw = [held([P, WIDE], I32, "xw%d" % s) for s in range(PASSES)]
+        lists = [list_a, list_b]
+        halves = [slice(0, HALF), slice(HALF, T)]
+
+        def offsets(l, slots):
+            return lists[l][:, slots.start // 16 : slots.stop // 16]
+
+        xs = held([P, T], U8, "xs")
+        xw = held([P, PASSES, T], I32, "xw")
         was = held([P, E1 * PASSES, H], U8, "was")
-        planes = [[held([P, T], U8, "plane%d%d" % (s, l)) for l in range(2)] for s in range(PASSES)]
         ident = held([P, P], F32, "ident")
 
-        nc.gpsimd.memset(xs[64:128].bitcast(I32), 0)
-        nc.gpsimd.memset(xs[32:64].bitcast(I32), 0)
-        nc.gpsimd.memset(xs[0:32, T:WIDE].bitcast(I32), 0)
-        nc.gpsimd.memset(xw[0][:, T:WIDE], 0)
-        nc.gpsimd.memset(xw[1][:, T:WIDE], 0)
-        make_identity(nc, ident[:])
-
-        def load_x(s):
-            nc.sync.dma_start(xw[s][:, 0:T], x_words[s].rearrange("p t d -> p (t d)").bitcast(I32))
-
-        nc.sync.dma_start(list_a[:], offs)
-        nc.sync.dma_start(xs[0:32, 0:T].bitcast(I32), x_scales.rearrange("s b t -> (s b) t").bitcast(I32))
-        load_x(0)
-        load_x(1)
-        nc.sync.dma_start(list_b[:], offs2)
-
-        def load_scales(plane, scales, queue):
-            for q in range(4):
+        def load_scales(plane, scales, queues):
+            for q, queue in enumerate(queues):
                 queue.dma_start(
                     plane[32 * q : 32 * q + 4].bitcast(I32),
                     scales[:, :, 4 * q : 4 * q + 4, :].rearrange("e s r i -> r (e s) i").bitcast(I32),
                 )
 
+        nc.gpsimd.memset(xs[:].bitcast(I32), 0)
+        nc.sync.dma_start(list_a[:], offs)
+        for q in range(4):
+            nc.sync.dma_start(xs[32 * q : 32 * q + 8].bitcast(I32), x_scales[:, 4 * q : 4 * q + 4, :].bitcast(I32))
+        nc.sync.dma_start(list_b[:], offs2)
+        load_scales(was, wa_scales, [nc.sync, nc.sync, nc.gpsimd, nc.gpsimd])
+        nc.sync.dma_start(xw[:], x_words.rearrange("s p t d -> p s (t d)").bitcast(I32))
+
         def load_words(words, tile):
             nc.sync.dma_start(tile.bitcast(I32), words.rearrange("e s p n -> p (e s) n").bitcast(I32))
             return tile
 
-        wa0 = held([P, PASSES, 2 * H], U8, "wa0")
-        wa = [load_words(wa_words[0:1], wa0[:])]
-        load_scales(was, wa_scales, nc.sync)
+        wa = held([P, E1 * PASSES, 2 * H], U8, "wa")
+        load_words(wa_words, wa[:])
+        make_identity(nc, ident[:])
+        wbs = held([P, E2 * PASSES, H], U8, "wbs")
+        load_scales(wbs, wb_scales, [nc.gpsimd] * 4)
 
-        lists = [list_a, list_b]
         gw = [[held([P, T], U32, "gw%d%d" % (l, s)) for s in range(PASSES)] for l in range(2)]
 
-        def gather_words(l, s, slots=slice(0, T)):
-            offsets = lists[l][:, slots.start // 16 : slots.stop // 16]
-            nc.vector.tensor_copy(gw[l][s][:, slots], xw[s][:].bitcast(U32).indirect(offsets))
-
-        def gather_scales(l, queue, name):
-            gs = held([P, T], U8, name)
-            nc.vector.tensor_copy(gs[:], xs[:].indirect(lists[l][:]))
+        def gather_words(l, slots):
             for s in range(PASSES):
-                for q in range(4):
-                    row = 16 * s + 4 * q
-                    queue.dma_start(planes[s][l][32 * q : 32 * q + 4].bitcast(I32), gs[row : row + 4].bitcast(I32))
+                nc.vector.tensor_copy(gw[l][s][:, slots], xw[:, s, :].bitcast(U32).indirect(offsets(l, slots)))
 
-        gather_scales(0, nc.scalar, "late")
-        late = held([P, 24, 2 * H], U8, "late")
-        load_words(wa_words[1:E1], late[:, 0:4, :])
-        for e in range(1, E1):
-            wa.append(late[:, 2 * e - 2 : 2 * e, :])
-        wbs = late[:, 16:22, :].rearrange("p a (b i) -> p (a b) i", b=2)
-        load_scales(wbs, wb_scales, nc.gpsimd)
-        wb = load_words(wb_words, late[:, 4:16, :])
-        w2 = late[:, 22, :]
-        w2s = late[:, 23, 0:N]
+        def gather_scales(l):
+            first = held([P, T], U8, "first%d" % l)
+            for half in halves:
+                nc.vector.tensor_copy(first[:, half], xs[:].indirect(offsets(l, half)))
+            second = held([P, T], U8, "second%d" % l)
+            for q in range(4):
+                nc.sync.dma_start(second[32 * q : 32 * q + 4].bitcast(I32), first[32 * q + 4 : 32 * q + 8].bitcast(I32))
+            return [first, second]
+
+        planes = [gather_scales(l) for l in range(2)]
+        late = held([P, E2 * PASSES + 2, 2 * H], U8, "xs")
+        wb = late[:, 0 : E2 * PASSES, :]
+        for f in range(0, E2, 2):
+            load_words(wb_words[f : f + 2], wb[:, PASSES * f : PASSES * (f + 2), :])
+        w2 = late[:, E2 * PASSES, :]
+        w2s = late[:, E2 * PASSES + 1, 0:N]
         nc.gpsimd.memset(w2s.bitcast(I32), 0)
-        nc.gpsimd.dma_start(w2.bitcast(I32), w2_words[0].bitcast(I32))
+        nc.sync.dma_start(w2.bitcast(I32), w2_words[0].bitcast(I32))
         for q in range(4):
-            nc.gpsimd.dma_start(w2s[32 * q : 32 * q + 4].bitcast(I32), w2_scales[0, 4 * q : 4 * q + 4, :].bitcast(I32))
+            nc.sync.dma_start(w2s[32 * q : 32 * q + 4].bitcast(I32), w2_scales[0, 4 * q : 4 * q + 4, :].bitcast(I32))
 
-        for slots in (slice(0, C1), slice(C1, T)):
-            for s in range(PASSES):
-                gather_words(0, s, slots)
-        gather_scales(1, nc.sync, "gs1")
-        gather_words(1, 0)
-        gather_words(1, 1)
+        gather_words(0, slice(0, C1))
+        gather_words(0, slice(C1, T))
+        gather_words(1, slice(0, C1))
+        gather_words(1, slice(C1, T))
 
         w2d = held([P, 2 * N], U8, "w2d")
         nc.gpsimd.tensor_copy(
-            w2d[:].rearrange("p (j m b) -> p j m b", j=4, b=2), w2.rearrange("p (m j b) -> p j m b", j=4, b=2)
+            w2d[:].rearrange("p (j m b) -> p j m b", j=LANES, b=2), w2.rearrange("p (m j b) -> p j m b", j=LANES, b=2)
         )
+        w2sd = held([P, LANES, P], U8, "w2sd")
+        nc.gpsimd.tensor_copy(w2sd[:], w2s.rearrange("p (m j) -> p j m", j=LANES))
 
-        def expert_tile(l, slot0, words, scales, dest, gate, place):
+        def sums(l, slot0, words, scales):
             acc = psum_mm.tile([P, H], F32, name="acc")
-            for s in range(PASSES):
+            for s in reversed(range(PASSES)):
                 nc.tensor.matmul_mx(
                     out=acc[:],
                     lhsT=gw[l][s][:, slot0 : slot0 + P].bitcast(FP8X4),
-                    lhsT_scale=planes[s][l][:, slot0 : slot0 + P],
+                    lhsT_scale=planes[l][s][:, slot0 : slot0 + P],
                     rhs=words[s].bitcast(FP4X4),
                     rhs_scale=scales[s],
-                    start=(s == 0),
-                    stop=(s == PASSES - 1),
+                    start=(s == PASSES - 1),
+                    stop=(s == 0),
                 )
-            dealt = ring.tile([P, 4, P], F32, name="dealt")
-            by_j = acc[:].rearrange("p (m j) -> p j m", j=4)
-            if gate:
-                nc.scalar.activation(dealt[:], by_j, SIGMOID)
-            else:
-                nc.scalar.copy(dealt[:], by_j)
-            turned = psum_tr.tile([P, 4, P], F32, name="turned")
-            for j in range(4):
-                nc.tensor.transpose(turned[:, place[j], :], dealt[:, j, :], ident[:])
-            for first, part in dest:
-                nc.scalar.copy(part, turned[:, first : first + part.shape[1], :])
+            return acc[:].rearrange("p (m j) -> p j m", j=LANES)
 
-        pieces = [slice(0, P), slice(P, C1), slice(C1, 2 * C1), slice(2 * C1, T)]
-        src_a = held([P, 4, T], F32, "src_a")
-        for e in range(E1):
-            for u in range(C1 // P):
-                slot0 = e * C1 + u * P
-                expert_tile(
-                    0, slot0, [wa[e][:, s, :] for s in range(PASSES)],
-                    [was[:, e * PASSES + s, :] for s in range(PASSES)], [(0, src_a[:, :, slot0 : slot0 + P])], True, [0, 1, 2, 3],
-                )
-        src_c = held([P, 4, T], F32, "src_c")
-        sources = [src_c[:, j, :] for j in range(4)]
+        def turn(blocks, dest):
+            turned = psum_tr.tile([P, len(blocks), P], F32, name="turned")
+            for b, block in enumerate(blocks):
+                nc.tensor.transpose(turned[:, b, :], block, ident[:])
+            nc.scalar.copy(dest, turned[:])
+
+        dealt_a = held([P, T // P, LANES, P], F32, "dealt_a")
+        src_a = held([P, LANES, T], F32, "src_a")
+
+        def turn_gate(j, half):
+            tiles = range(half.start // P, half.stop // P)
+            turn([dealt_a[:, u, j, :] for u in tiles], src_a[:, j, half].rearrange("p (u t) -> p u t", t=P))
+
+        for u in range(T // P):
+            e = u * P // C1
+            by_lane = sums(0, u * P, [wa[:, e * PASSES + s, :] for s in range(PASSES)], [was[:, e * PASSES + s, :] for s in range(PASSES)])
+            nc.scalar.activation(dealt_a[:, u], by_lane, SIGMOID)
+            if (u + 1) * P % HALF == 0:
+                turn_gate(0, halves[u * P // HALF])
+        src_c = held([P, LANES, T], F32, "src_c")
         for f in range(E2):
-            expert_tile(
-                1, f * C2, [wb[:, f * PASSES + s, :] for s in range(PASSES)],
-                [wbs[:, f * PASSES + s, :] for s in range(PASSES)],
-                [(0, src_c[:, :, f * C2 : (f + 1) * C2])], False, [0, 1, 2, 3],
-            )
+            by_lane = sums(1, f * C2, [wb[:, f * PASSES + s, :] for s in range(PASSES)], [wbs[:, f * PASSES + s, :] for s in range(PASSES)])
+            dealt = ring.tile([P, LANES, P], F32, name="dealt")
+            nc.scalar.copy(dealt[:], by_lane)
+            turn([dealt[:, j, :] for j in range(LANES)], src_c[:, :, f * C2 : (f + 1) * C2])
 
-        gate = [held([P, T], F32, "gate%d" % j) for j in range(4)]
-        for piece in pieces:
-            for j in range(4):
-                cols = slice(piece.start // 16, piece.stop // 16)
-                nc.vector.tensor_copy(gate[j][:].indirect(list_a[:, cols]), src_a[:, j, piece])
+        gate = [held([P, T], F32, "gate%d" % j) for j in range(LANES)]
+        value = [held([P, T if j < 2 else WIDE], F32, "value%d" % j) for j in range(LANES)]
+        hq = held([P, T, LANES], BF16, "hq")
 
-        there = psum_tr.tile([P, 4, P], F32, name="turned")
-        banked = [0, 2, 3, 4]
-        for u in range(4):
-            nc.tensor.transpose(there[:, u, :], gate[3][:, P * banked[u] : P * (banked[u] + 1)], ident[:])
-
-        hq = held([P, T, 4], BF16, "hq")
-        hb = held([P, 2, T], BF16, "hb")
-
-        def half_units(row, half):
-            return row.rearrange("p (u h t) -> p u h t", h=2, t=P // 2)[:, :, half, :]
-
-        value = [held([P, WIDE], F32, "value%d" % j) for j in range(4)]
-        for j in range(4):
-            nc.vector.tensor_copy(value[j][:].indirect(list_b[:]), sources[j])
-            if j < 2:
+        for half in halves:
+            nc.vector.tensor_copy(gate[0][:].indirect(offsets(0, half)), src_a[:, 0, half])
+        for half in halves:
+            for j in range(2):
+                nc.vector.tensor_copy(value[j][:].indirect(offsets(1, half)), src_c[:, j, half])
+        for j in range(LANES):
+            if j > 0:
+                for half in halves:
+                    turn_gate(j, half)
+                for half in halves:
+                    nc.scalar.activation(gate[j][:].indirect(offsets(0, half)), src_a[:, j, half], COPY)
+            if j > 1:
+                nc.vector.tensor_copy(value[j][:].indirect(list_b[:]), src_c[:, j, :])
+            if j < LANES - 1:
                 nc.gpsimd.tensor_tensor(hq[:, :, j], gate[j][:], value[j][:, 0:T], MULT)
-            if j == 2:
-                for half in range(2):
-                    nc.gpsimd.tensor_tensor(half_units(hb[:, 0, :], half), half_units(gate[j][:], half), half_units(value[j][:, 0:T], half), MULT)
-                    nc.scalar.copy(
-                        hq[:].rearrange("p (u h t) j -> p u h t j", h=2, t=P // 2)[:, :, half, :, 2:4],
-                        half_units(hb[:, 0, :], half).unsqueeze(3).to_broadcast([P, T // P, P // 2, 2]),
-                    )
 
-        gate_turned = src_c[:, 2, 0 : 4 * P].rearrange("p (u t) -> p u t", t=P)
-        nc.scalar.copy(gate_turned, there[:])
-        gate_bank = psum_tr.tile([P, 4, P], F32, name="turned")
-        for u in range(4):
-            nc.tensor.transpose(gate_bank[:, u, :], gate_turned[:, u, :], ident[:])
-        warm = psum_tr.tile([P, H], F32, name="turned")
-        for repeat in range(7):
-            nc.tensor.matmul_mx(
-                out=warm[:], lhsT=gw[0][0][:, 0:P].bitcast(FP8X4), lhsT_scale=planes[0][0][:, 0:P],
-                rhs=wa[0][:, 0, :].bitcast(FP4X4), rhs_scale=was[:, 0, :], start=True, stop=True,
-            )
-
-        w2sd_all = held([P, 4, P], U8, "w2sd_all")
-        nc.gpsimd.tensor_copy(w2sd_all[:], w2s.rearrange("p (m j) -> p j m", j=4))
-        w2sd = [w2sd_all[:, j, :] for j in range(4)]
-
+        last = held([P, T], BF16, "value2")
         y_codes = held([P, T], U32, "y_codes")
         y_scales = held([P, T], U8, "y_scales")
         h_codes = held([P, T], U32, "h_codes")
         h_scales = held([P, T], U8, "h_scales")
-        rows = out_0.rearrange("(p j) t -> p j t", j=4)
-        runs = [slice(0, 256), slice(256, 768)]
-        y = [held([P, 4, run.stop - run.start], F32, "y%d" % r) for r, run in enumerate(runs)]
-        yq = held([P, T, 4], BF16, "yq")
+        rows = out_0.rearrange("(p j) t -> p j t", j=LANES)
+        runs = [slice(0, 2 * P), slice(2 * P, T)]
+        y = [held([P, LANES, run.stop - run.start], F32, "y%d" % r) for r, run in enumerate(runs)]
+        yq = held([P, T, LANES], BF16, "yq")
 
-        def unit(u):
-            return slice(P * u, P * (u + 1))
+        def units(u0, u1):
+            return slice(P * u0, P * u1)
 
-        def gate_of(u):
-            return gate_bank[:, banked.index(u), :] if u in banked else gate[3][:, unit(u)]
+        def last_product(cols):
+            nc.vector.tensor_tensor(last[:, cols], value[3][:, cols], gate[3][:, cols], MULT)
 
-        def last_product(engine, u):
-            engine.tensor_tensor(hq[:, unit(u), 3], value[3][:, unit(u)], gate_of(u), MULT)
-
-        def last_product_by_scalar(u):
-            nc.vector.tensor_tensor(hb[:, 1, unit(u)], value[3][:, unit(u)], gate_of(u), MULT)
-            nc.scalar.copy(hq[:, unit(u), 3], hb[:, 1, unit(u)])
+        def weave(copy, cols):
+            copy(hq[:, cols, 3], last[:, cols])
 
         def quantise(codes, scales, values, cols):
             nc.vector.quantize_mx(
                 out=codes[:, cols].bitcast(FP8X4), scales=scales[:, cols], in_=values[:, cols, :].rearrange("p t j -> p (t j)")
             )
 
-        def multiply(pool, name, cols, j0, j1, dest, copy):
-            bank = pool.tile([P, j1 - j0, cols.stop - cols.start], F32, name=name)
-            for j in range(j0, j1):
-                nc.tensor.matmul_mx(
-                    out=bank[:, j - j0, :],
-                    lhsT=w2d[:, 2 * P * j : 2 * P * (j + 1)].bitcast(FP4X4),
-                    lhsT_scale=w2sd[j],
-                    rhs=h_codes[:, cols].bitcast(FP8X4),
-                    rhs_scale=h_scales[:, cols],
-                    start=True,
-                    stop=True,
-                )
+        def multiply(pool, name, cols, j, dest, copy):
+            bank = pool.tile([P, cols.stop - cols.start], F32, name=name)
+            nc.tensor.matmul_mx(
+                out=bank[:],
+                lhsT=w2d[:, 2 * P * j : 2 * P * (j + 1)].bitcast(FP4X4),
+                lhsT_scale=w2sd[:, j, :],
+                rhs=h_codes[:, cols].bitcast(FP8X4),
+                rhs_scale=h_scales[:, cols],
+                start=True,
+                stop=True,
+            )
             copy(dest, bank[:])
 
-        def result_rows(r, j0, j1, pool, name, copy):
-            multiply(pool, name, runs[r], j0, j1, y[r][:, j0:j1, :], copy)
-            nc.sync.dma_start(rows[:, j0:j1, runs[r]], y[r][:, j0:j1, :])
+        def result_rows(r, j, pool, name, copy):
+            multiply(pool, name, runs[r], j, y[r][:, j, :], copy)
+            nc.sync.dma_start(rows[:, j, runs[r]], y[r][:, j, :])
 
-        def round_result(r, t0, t1, copy=nc.vector.tensor_copy):
+        def round_result(r, t0, t1, copy):
             cols = slice(runs[r].start + t0, runs[r].start + t1)
             copy(
                 yq[:, cols, :].rearrange("p (c i) j -> p c j i", i=4),
@@ -263,34 +229,36 @@ def tile_moe_pool_sigmoid_kernel(
                 out_1[0, :, cols, :].rearrange("p t d -> p (t d)").bitcast(I32), y_codes[:, cols].bitcast(I32)
             )
 
-        last_product(nc.gpsimd, 1)
-        last_product(nc.gpsimd, 5)
-        last_product_by_scalar(2)
-        last_product(nc.vector, 0)
-        last_product_by_scalar(3)
+        on_vector, on_scalar = nc.vector.tensor_copy, nc.scalar.copy
+        last_product(units(0, 2))
+        weave(on_scalar, units(0, 1))
+        last_product(units(2, 4))
+        weave(on_scalar, units(2, 4))
+        weave(on_vector, units(1, 2))
+        last_product(units(4, 6))
         quantise(h_codes, h_scales, hq, runs[0])
-        result_rows(0, 0, 1, psum_y, "acc_y", nc.scalar.copy)
-        result_rows(0, 1, 2, psum_mm, "acc", nc.scalar.copy)
-        result_rows(0, 2, 3, psum_y, "acc_y", nc.scalar.copy)
-        result_rows(0, 3, 4, psum_mm, "acc", nc.scalar.copy)
-        last_product(nc.vector, 4)
-        quantise(h_codes, h_scales, hq, slice(2 * P, 4 * P))
-        quantise(h_codes, h_scales, hq, slice(4 * P, 6 * P))
-        result_rows(1, 0, 1, psum_y, "acc_y", nc.vector.tensor_copy)
-        result_rows(1, 1, 2, psum_mm, "acc", nc.scalar.copy)
-        round_result(0, 0, 2 * P)
-        result_rows(1, 2, 3, psum_y, "acc_y", nc.scalar.copy)
+        result_rows(0, 0, psum_y, "acc_y", on_scalar)
+        result_rows(0, 1, psum_mm, "acc", on_scalar)
+        result_rows(0, 2, psum_y, "acc_y", on_scalar)
+        result_rows(0, 3, psum_mm, "acc", on_scalar)
+        weave(on_vector, units(4, 6))
+        quantise(h_codes, h_scales, hq, units(2, 4))
+        quantise(h_codes, h_scales, hq, units(4, 6))
+        result_rows(1, 0, psum_y, "acc_y", on_vector)
+        result_rows(1, 1, psum_mm, "acc", on_scalar)
+        round_result(0, 0, 2 * P, on_vector)
+        result_rows(1, 2, psum_y, "acc_y", on_scalar)
         quantise(y_codes, y_scales, yq, runs[0])
-        multiply(psum_mm, "acc", slice(2 * P, 4 * P), 3, 4, y[1][:, 3:4, 0 : 2 * P], nc.vector.tensor_copy)
-        multiply(psum_y, "acc_y", slice(4 * P, 6 * P), 3, 4, y[1][:, 3:4, 2 * P : 4 * P], nc.scalar.copy)
+        multiply(psum_mm, "acc", units(2, 4), 3, y[1][:, 3, 0 : 2 * P], on_vector)
+        multiply(psum_y, "acc_y", units(4, 6), 3, y[1][:, 3, 2 * P : 4 * P], on_scalar)
         nc.sync.dma_start(rows[:, 3, runs[1]], y[1][:, 3, :])
-        round_result(1, 5 * P // 2, 4 * P, nc.scalar.copy)
-        round_result(1, 0, 2 * P)
-        round_result(1, 2 * P, 5 * P // 2)
-        quantise(y_codes, y_scales, yq, slice(2 * P, 4 * P))
-        store_codes(slice(0, 4 * P))
-        quantise(y_codes, y_scales, yq, slice(4 * P, 6 * P))
-        store_codes(slice(4 * P, 6 * P))
+        round_result(1, 5 * P // 2, 4 * P, on_scalar)
+        round_result(1, 0, 2 * P, on_vector)
+        round_result(1, 2 * P, 5 * P // 2, on_vector)
+        quantise(y_codes, y_scales, yq, units(2, 4))
+        store_codes(units(0, 4))
+        quantise(y_codes, y_scales, yq, units(4, 6))
+        store_codes(units(4, 6))
         for q in range(4):
             queue = nc.scalar if q % 2 else nc.sync
             queue.dma_start(out_2[0, 4 * q : 4 * q + 4, :].bitcast(I32), y_scales[32 * q : 32 * q + 4].bitcast(I32))

@@ -31,10 +31,7 @@ def tile_moe_pool_sigmoid_kernel(
     nc = tc.nc
     with ExitStack() as ctx:
         keep = ctx.enter_context(tc.tile_pool(name="keep", bufs=1))
-        ring = ctx.enter_context(tc.tile_pool(name="ring", bufs=3))
-        psum_mm = ctx.enter_context(tc.psum_pool(name="psum_mm", bufs=3))
-        psum_tr = ctx.enter_context(tc.psum_pool(name="psum_tr", bufs=2))
-        psum_y = ctx.enter_context(tc.psum_pool(name="psum_y", bufs=3))
+        psum = ctx.enter_context(tc.psum_pool(name="psum", bufs=8))
 
         def held(shape, dtype, name):
             return keep.tile(shape, dtype, name=name, align_bytes=64)
@@ -80,7 +77,7 @@ def tile_moe_pool_sigmoid_kernel(
         gw = [[held([P, T], U32, "gw%d%d" % (l, s)) for s in range(PASSES)] for l in range(2)]
 
         def gather_words(l, slots):
-            for s in range(PASSES):
+            for s in reversed(range(PASSES)):
                 nc.vector.tensor_copy(gw[l][s][:, slots], xw[:, s, :].bitcast(U32).indirect(offsets(l, slots)))
 
         def gather_scales(l):
@@ -117,7 +114,7 @@ def tile_moe_pool_sigmoid_kernel(
         nc.gpsimd.tensor_copy(w2sd[:], w2s.rearrange("p (m j) -> p j m", j=LANES))
 
         def sums(l, slot0, words, scales):
-            acc = psum_mm.tile([P, H], F32, name="acc")
+            acc = psum.tile([P, H], F32, name="bank")
             for s in reversed(range(PASSES)):
                 nc.tensor.matmul_mx(
                     out=acc[:],
@@ -131,52 +128,53 @@ def tile_moe_pool_sigmoid_kernel(
             return acc[:].rearrange("p (m j) -> p j m", j=LANES)
 
         def turn(blocks, dest):
-            turned = psum_tr.tile([P, len(blocks), P], F32, name="turned")
+            turned = psum.tile([P, len(blocks), P], F32, name="bank")
             for b, block in enumerate(blocks):
                 nc.tensor.transpose(turned[:, b, :], block, ident[:])
             nc.scalar.copy(dest, turned[:])
 
-        dealt_a = held([P, T // P, LANES, P], F32, "dealt_a")
-        src_a = held([P, LANES, T], F32, "src_a")
+        dealt = [held([P, T // P, LANES, P], F32, "dealt%d" % l) for l in range(2)]
+        src = [held([P, LANES, T], F32, "src%d" % l) for l in range(2)]
 
-        def turn_gate(j, half):
+        def turn_half(l, j, half):
             tiles = range(half.start // P, half.stop // P)
-            turn([dealt_a[:, u, j, :] for u in tiles], src_a[:, j, half].rearrange("p (u t) -> p u t", t=P))
+            turn([dealt[l][:, u, j, :] for u in tiles], src[l][:, j, half].rearrange("p (u t) -> p u t", t=P))
 
-        for u in range(T // P):
-            e = u * P // C1
-            by_lane = sums(0, u * P, [wa[:, e * PASSES + s, :] for s in range(PASSES)], [was[:, e * PASSES + s, :] for s in range(PASSES)])
-            nc.scalar.activation(dealt_a[:, u], by_lane, SIGMOID)
-            if (u + 1) * P % HALF == 0:
-                turn_gate(0, halves[u * P // HALF])
-        src_c = held([P, LANES, T], F32, "src_c")
-        for f in range(E2):
-            by_lane = sums(1, f * C2, [wb[:, f * PASSES + s, :] for s in range(PASSES)], [wbs[:, f * PASSES + s, :] for s in range(PASSES)])
-            dealt = ring.tile([P, LANES, P], F32, name="dealt")
-            nc.scalar.copy(dealt[:], by_lane)
-            turn([dealt[:, j, :] for j in range(LANES)], src_c[:, :, f * C2 : (f + 1) * C2])
-
-        gate = [held([P, T], F32, "gate%d" % j) for j in range(LANES)]
-        value = [held([P, T if j < 2 else WIDE], F32, "value%d" % j) for j in range(LANES)]
+        window = [[held([P, WIDE if l == 1 and j > 1 else T], F32, "window%d%d" % (l, j)) for j in range(LANES)] for l in range(2)]
+        gate, value = window
         hq = held([P, T, LANES], BF16, "hq")
 
-        for half in halves:
-            nc.vector.tensor_copy(gate[0][:].indirect(offsets(0, half)), src_a[:, 0, half])
-        for half in halves:
-            for j in range(2):
-                nc.vector.tensor_copy(value[j][:].indirect(offsets(1, half)), src_c[:, j, half])
-        for j in range(LANES):
-            if j > 0:
-                for half in halves:
-                    turn_gate(j, half)
-                for half in halves:
-                    nc.scalar.activation(gate[j][:].indirect(offsets(0, half)), src_a[:, j, half], COPY)
-            if j > 1:
-                nc.vector.tensor_copy(value[j][:].indirect(list_b[:]), src_c[:, j, :])
-            if j < LANES - 1:
-                nc.gpsimd.tensor_tensor(hq[:, :, j], gate[j][:], value[j][:, 0:T], MULT)
+        def scatter(engine, l, j, slots):
+            if engine == "scalar":
+                nc.scalar.activation(window[l][j][:].indirect(offsets(l, slots)), src[l][:, j, slots], COPY)
+            else:
+                nc.vector.tensor_copy(window[l][j][:].indirect(offsets(l, slots)), src[l][:, j, slots])
 
-        last = held([P, T], BF16, "value2")
+        def product(j):
+            nc.gpsimd.tensor_tensor(hq[:, :, j], gate[j][:], value[j][:, 0:T], MULT)
+
+        words, scales, room = [wa, wb], [was, wbs], [C1, C2]
+        early = [[(0, "vector"), (1, "vector"), (2, "scalar")], [(1, "vector")]]
+        for l in range(2):
+            for half in halves:
+                for u in range(half.start // P, half.stop // P):
+                    e = u * P // room[l]
+                    by_lane = sums(l, u * P, [words[l][:, e * PASSES + s, :] for s in range(PASSES)], [scales[l][:, e * PASSES + s, :] for s in range(PASSES)])
+                    nc.scalar.activation(dealt[l][:, u], by_lane, COPY if l else SIGMOID)
+                for j, engine in early[l]:
+                    turn_half(l, j, half)
+                for j, engine in early[l]:
+                    scatter(engine, l, j, half)
+        product(1)
+        for l, j, engine in ((1, 2, "vector"), (1, 0, "scalar"), (1, 3, "vector"), (0, 3, "scalar")):
+            for half in halves:
+                turn_half(l, j, half)
+            for slots in halves if engine == "scalar" else [slice(0, T)]:
+                scatter(engine, l, j, slots)
+        product(0)
+
+        pair = held([P, 2, T], BF16, "window10")
+        nc.gpsimd.tensor_tensor(pair[:, 0, :], gate[2][:], value[2][:, 0:T], MULT)
         y_codes = held([P, T], U32, "y_codes")
         y_scales = held([P, T], U8, "y_scales")
         h_codes = held([P, T], U32, "h_codes")
@@ -190,18 +188,18 @@ def tile_moe_pool_sigmoid_kernel(
             return slice(P * u0, P * u1)
 
         def last_product(cols):
-            nc.vector.tensor_tensor(last[:, cols], value[3][:, cols], gate[3][:, cols], MULT)
+            nc.vector.tensor_tensor(pair[:, 1, cols], value[3][:, cols], gate[3][:, cols], MULT)
 
         def weave(copy, cols):
-            copy(hq[:, cols, 3], last[:, cols])
+            copy(hq[:, cols, 2:4], pair[:, :, cols].rearrange("p j t -> p t j"))
 
         def quantise(codes, scales, values, cols):
             nc.vector.quantize_mx(
                 out=codes[:, cols].bitcast(FP8X4), scales=scales[:, cols], in_=values[:, cols, :].rearrange("p t j -> p (t j)")
             )
 
-        def multiply(pool, name, cols, j, dest, copy):
-            bank = pool.tile([P, cols.stop - cols.start], F32, name=name)
+        def multiply(cols, j, dest, copy):
+            bank = psum.tile([P, cols.stop - cols.start], F32, name="bank")
             nc.tensor.matmul_mx(
                 out=bank[:],
                 lhsT=w2d[:, 2 * P * j : 2 * P * (j + 1)].bitcast(FP4X4),
@@ -213,8 +211,8 @@ def tile_moe_pool_sigmoid_kernel(
             )
             copy(dest, bank[:])
 
-        def result_rows(r, j, pool, name, copy):
-            multiply(pool, name, runs[r], j, y[r][:, j, :], copy)
+        def result_rows(r, j, copy):
+            multiply(runs[r], j, y[r][:, j, :], copy)
             nc.sync.dma_start(rows[:, j, runs[r]], y[r][:, j, :])
 
         def round_result(r, t0, t1, copy):
@@ -237,20 +235,20 @@ def tile_moe_pool_sigmoid_kernel(
         weave(on_vector, units(1, 2))
         last_product(units(4, 6))
         quantise(h_codes, h_scales, hq, runs[0])
-        result_rows(0, 0, psum_y, "acc_y", on_scalar)
-        result_rows(0, 1, psum_mm, "acc", on_scalar)
-        result_rows(0, 2, psum_y, "acc_y", on_scalar)
-        result_rows(0, 3, psum_mm, "acc", on_scalar)
+        result_rows(0, 0, on_scalar)
+        result_rows(0, 1, on_scalar)
+        result_rows(0, 2, on_scalar)
+        result_rows(0, 3, on_scalar)
         weave(on_vector, units(4, 6))
         quantise(h_codes, h_scales, hq, units(2, 4))
         quantise(h_codes, h_scales, hq, units(4, 6))
-        result_rows(1, 0, psum_y, "acc_y", on_vector)
-        result_rows(1, 1, psum_mm, "acc", on_scalar)
+        result_rows(1, 0, on_vector)
+        result_rows(1, 1, on_scalar)
         round_result(0, 0, 2 * P, on_vector)
-        result_rows(1, 2, psum_y, "acc_y", on_scalar)
+        result_rows(1, 2, on_scalar)
         quantise(y_codes, y_scales, yq, runs[0])
-        multiply(psum_mm, "acc", units(2, 4), 3, y[1][:, 3, 0 : 2 * P], on_vector)
-        multiply(psum_y, "acc_y", units(4, 6), 3, y[1][:, 3, 2 * P : 4 * P], on_scalar)
+        multiply(units(2, 4), 3, y[1][:, 3, 0 : 2 * P], on_vector)
+        multiply(units(4, 6), 3, y[1][:, 3, 2 * P : 4 * P], on_scalar)
         nc.sync.dma_start(rows[:, 3, runs[1]], y[1][:, 3, :])
         round_result(1, 5 * P // 2, 4 * P, on_scalar)
         round_result(1, 0, 2 * P, on_vector)

@@ -22,6 +22,7 @@ PASSES = 2
 LANES = 4
 WIDE = 1024
 HALF = T // 2
+GATE, VALUE = 0, 1
 FLOPS = 2 * K * H * T * 2 + 2 * H * N * T
 
 
@@ -46,8 +47,9 @@ def tile_moe_pool_sigmoid_kernel(
 
         xs = held([P, T], U8, "xs")
         xw = held([P, PASSES, T], I32, "xw")
-        was = held([P, E1 * PASSES, H], U8, "was")
         ident = held([P, P], F32, "ident")
+        wa_all = held([P, E1 * PASSES, 2 * H], U8, "wa")
+        was = held([P, E1 * PASSES, H], U8, "was")
 
         def load_scales(plane, scales, queues):
             for q, queue in enumerate(queues):
@@ -56,6 +58,9 @@ def tile_moe_pool_sigmoid_kernel(
                     scales[:, :, 4 * q : 4 * q + 4, :].rearrange("e s r i -> r (e s) i").bitcast(I32),
                 )
 
+        def load_words(tile, words):
+            nc.sync.dma_start(tile.bitcast(I32), words.rearrange("e s p n -> p (e s) n").bitcast(I32))
+
         nc.gpsimd.memset(xs[:].bitcast(I32), 0)
         nc.sync.dma_start(list_a[:], offs)
         for q in range(4):
@@ -63,16 +68,8 @@ def tile_moe_pool_sigmoid_kernel(
         nc.sync.dma_start(list_b[:], offs2)
         load_scales(was, wa_scales, [nc.sync, nc.sync, nc.gpsimd, nc.gpsimd])
         nc.sync.dma_start(xw[:], x_words.rearrange("s p t d -> p s (t d)").bitcast(I32))
-
-        def load_words(words, tile):
-            nc.sync.dma_start(tile.bitcast(I32), words.rearrange("e s p n -> p (e s) n").bitcast(I32))
-            return tile
-
-        wa = held([P, E1 * PASSES, 2 * H], U8, "wa")
-        load_words(wa_words, wa[:])
+        load_words(wa_all[:], wa_words)
         make_identity(nc, ident[:])
-        wbs = held([P, E2 * PASSES, H], U8, "wbs")
-        load_scales(wbs, wb_scales, [nc.gpsimd] * 4)
 
         gw = [[held([P, T], U32, "gw%d%d" % (l, s)) for s in range(PASSES)] for l in range(2)]
 
@@ -90,21 +87,25 @@ def tile_moe_pool_sigmoid_kernel(
             return [first, second]
 
         planes = [gather_scales(l) for l in range(2)]
-        late = held([P, E2 * PASSES + 2, 2 * H], U8, "xs")
-        wb = late[:, 0 : E2 * PASSES, :]
-        for f in range(0, E2, 2):
-            load_words(wb_words[f : f + 2], wb[:, PASSES * f : PASSES * (f + 2), :])
-        w2 = late[:, E2 * PASSES, :]
-        w2s = late[:, E2 * PASSES + 1, 0:N]
+        late = held([P, 20, 2 * H], U8, "xs")
+        wa = [wa_all[:, a, :] for a in range(E1 * PASSES)]
+        wb = [late[:, a, :] for a in range(12)]
+        wbs = late[:, 12:18, :].rearrange("p a (b i) -> p (a b) i", b=2)
+        w2 = late[:, 18, :]
+        w2s = late[:, 19, 0:N]
+        load_words(late[:, 0:6, :], wb_words[0:3])
+        load_scales(wbs, wb_scales, [nc.sync, nc.sync, nc.gpsimd, nc.gpsimd])
+        load_words(late[:, 6:12, :], wb_words[3:6])
         nc.gpsimd.memset(w2s.bitcast(I32), 0)
         nc.sync.dma_start(w2.bitcast(I32), w2_words[0].bitcast(I32))
         for q in range(4):
-            nc.sync.dma_start(w2s[32 * q : 32 * q + 4].bitcast(I32), w2_scales[0, 4 * q : 4 * q + 4, :].bitcast(I32))
+            nc.gpsimd.dma_start(w2s[32 * q : 32 * q + 4].bitcast(I32), w2_scales[0, 4 * q : 4 * q + 4, :].bitcast(I32))
 
-        gather_words(0, slice(0, C1))
-        gather_words(0, slice(C1, T))
-        gather_words(1, slice(0, C1))
-        gather_words(1, slice(C1, T))
+        pieces = [slice(0, C1), slice(C1, T)]
+        for piece in pieces:
+            gather_words(GATE, piece)
+        for piece in pieces:
+            gather_words(VALUE, piece)
 
         w2d = held([P, 2 * N], U8, "w2d")
         nc.gpsimd.tensor_copy(
@@ -127,50 +128,63 @@ def tile_moe_pool_sigmoid_kernel(
                 )
             return acc[:].rearrange("p (m j) -> p j m", j=LANES)
 
-        def turn(blocks, dest):
+        def turn(blocks, dest, copy):
             turned = psum.tile([P, len(blocks), P], F32, name="bank")
             for b, block in enumerate(blocks):
                 nc.tensor.transpose(turned[:, b, :], block, ident[:])
-            nc.scalar.copy(dest, turned[:])
+            copy(dest, turned[:] if len(dest.shape) == 3 else turned[:].rearrange("p (j u) t -> p j u t", j=2))
 
         dealt = [held([P, T // P, LANES, P], F32, "dealt%d" % l) for l in range(2)]
         src = [held([P, LANES, T], F32, "src%d" % l) for l in range(2)]
+        early_values = src[VALUE][:, 0:3, :]
+        row = [[0, 1, 2, 3], [0, 1, 3, 2]]
 
-        def turn_half(l, j, half):
-            tiles = range(half.start // P, half.stop // P)
-            turn([dealt[l][:, u, j, :] for u in tiles], src[l][:, j, half].rearrange("p (u t) -> p u t", t=P))
+        def turn_slots(l, j, slots, copy=nc.scalar.copy):
+            tiles = range(slots.start // P, slots.stop // P)
+            turn([dealt[l][:, u, j, :] for u in tiles], src[l][:, row[l][j], slots].rearrange("p (u t) -> p u t", t=P), copy)
 
-        window = [[held([P, WIDE if l == 1 and j > 1 else T], F32, "window%d%d" % (l, j)) for j in range(LANES)] for l in range(2)]
+        window = [[held([P, WIDE if l == 1 and j == 3 else T], F32, "window%d%d" % (l, j)) for j in range(LANES)] for l in range(2)]
         gate, value = window
         hq = held([P, T, LANES], BF16, "hq")
 
         def scatter(engine, l, j, slots):
             if engine == "scalar":
-                nc.scalar.activation(window[l][j][:].indirect(offsets(l, slots)), src[l][:, j, slots], COPY)
+                nc.scalar.activation(window[l][j][:].indirect(offsets(l, slots)), src[l][:, row[l][j], slots], COPY)
             else:
-                nc.vector.tensor_copy(window[l][j][:].indirect(offsets(l, slots)), src[l][:, j, slots])
+                nc.vector.tensor_copy(window[l][j][:].indirect(offsets(l, slots)), src[l][:, row[l][j], slots])
 
         def product(j):
             nc.gpsimd.tensor_tensor(hq[:, :, j], gate[j][:], value[j][:, 0:T], MULT)
 
         words, scales, room = [wa, wb], [was, wbs], [C1, C2]
-        early = [[(0, "vector"), (1, "vector"), (2, "scalar")], [(1, "vector")]]
-        for l in range(2):
-            for half in halves:
-                for u in range(half.start // P, half.stop // P):
-                    e = u * P // room[l]
-                    by_lane = sums(l, u * P, [words[l][:, e * PASSES + s, :] for s in range(PASSES)], [scales[l][:, e * PASSES + s, :] for s in range(PASSES)])
-                    nc.scalar.activation(dealt[l][:, u], by_lane, COPY if l else SIGMOID)
-                for j, engine in early[l]:
-                    turn_half(l, j, half)
-                for j, engine in early[l]:
-                    scatter(engine, l, j, half)
+
+        def tiles(l, slots):
+            for u in range(slots.start // P, slots.stop // P):
+                e = u * P // room[l]
+                by_lane = sums(l, u * P, [words[l][e * PASSES + s] for s in range(PASSES)], [scales[l][:, e * PASSES + s, :] for s in range(PASSES)])
+                nc.scalar.activation(dealt[l][:, u], by_lane, COPY if l else SIGMOID)
+
+        tiles(GATE, slice(0, T))
+        for e in range(E1):
+            slots = slice(e * C1, (e + 1) * C1)
+            turn(
+                [dealt[GATE][:, u, j, :] for j in (1, 2) for u in (2 * e, 2 * e + 1)],
+                src[GATE][:, 1:3, slots].rearrange("p j (u t) -> p j u t", t=P), nc.scalar.copy,
+            )
+            scatter("vector", GATE, 1, slots)
+            scatter("vector", GATE, 2, slots)
+        tiles(VALUE, slice(0, T))
+        for f in range(E2):
+            slots = slice(f * P, (f + 1) * P)
+            turn([dealt[VALUE][:, f, j, :] for j in (0, 1, 3)], early_values[:, :, slots], nc.scalar.copy)
+            if (f + 1) * P % HALF == 0:
+                for j in (1, 0):
+                    scatter("vector", VALUE, j, halves[f * P // HALF])
+        scatter("vector", VALUE, 3, slice(0, T))
+        for l, j, half in [(l, j, half) for half in halves for l, j in ((GATE, 0), (VALUE, 2))] + [(GATE, 3, half) for half in halves]:
+            turn_slots(l, j, half)
+            scatter("scalar", l, j, half)
         product(1)
-        for l, j, engine in ((1, 2, "vector"), (1, 0, "scalar"), (1, 3, "vector"), (0, 3, "scalar")):
-            for half in halves:
-                turn_half(l, j, half)
-            for slots in halves if engine == "scalar" else [slice(0, T)]:
-                scatter(engine, l, j, slots)
         product(0)
 
         pair = held([P, 2, T], BF16, "window10")

@@ -22,7 +22,9 @@ PASSES = 2
 LANES = 4
 WIDE = 1024
 HALF = T // 2
+RUN = 256
 GATE, VALUE = 0, 1
+PASS_ORDER = (1, 0)
 FLOPS = 2 * K * H * T * 2 + 2 * H * N * T
 
 
@@ -48,7 +50,7 @@ def tile_moe_pool_sigmoid_kernel(
         xs = held([P, T], U8, "xs")
         xw = held([P, PASSES, T], I32, "xw")
         ident = held([P, P], F32, "ident")
-        wa_all = held([P, E1 * PASSES, 2 * H], U8, "wa")
+        wa_first = held([P, 2 * PASSES, 2 * H], U8, "wa_first")
         was = held([P, E1 * PASSES, H], U8, "was")
 
         def load_scales(plane, scales, queues):
@@ -68,27 +70,33 @@ def tile_moe_pool_sigmoid_kernel(
         nc.sync.dma_start(list_b[:], offs2)
         load_scales(was, wa_scales, [nc.sync, nc.sync, nc.gpsimd, nc.gpsimd])
         nc.sync.dma_start(xw[:], x_words.rearrange("s p t d -> p s (t d)").bitcast(I32))
-        load_words(wa_all[:], wa_words)
+        load_words(wa_first[:], wa_words[0:2])
         make_identity(nc, ident[:])
 
         gw = [[held([P, T], U32, "gw%d%d" % (l, s)) for s in range(PASSES)] for l in range(2)]
 
         def gather_words(l, slots):
-            for s in reversed(range(PASSES)):
+            for s in PASS_ORDER:
                 nc.vector.tensor_copy(gw[l][s][:, slots], xw[:, s, :].bitcast(U32).indirect(offsets(l, slots)))
 
         def gather_scales(l):
             first = held([P, T], U8, "first%d" % l)
             for half in halves:
                 nc.vector.tensor_copy(first[:, half], xs[:].indirect(offsets(l, half)))
+            return first
+
+        def move_rows(l, first):
             second = held([P, T], U8, "second%d" % l)
             for q in range(4):
                 nc.sync.dma_start(second[32 * q : 32 * q + 4].bitcast(I32), first[32 * q + 4 : 32 * q + 8].bitcast(I32))
             return [first, second]
 
-        planes = [gather_scales(l) for l in range(2)]
-        late = held([P, 20, 2 * H], U8, "xs")
-        wa = [wa_all[:, a, :] for a in range(E1 * PASSES)]
+        gathered = [gather_scales(l) for l in range(2)]
+        planes = [move_rows(GATE, gathered[GATE])]
+        late = held([P, 22, 2 * H], U8, "xs")
+        load_words(late[:, 20:22, :], wa_words[2:E1])
+        planes.append(move_rows(VALUE, gathered[VALUE]))
+        wa = [wa_first[:, a, :] for a in range(2 * PASSES)] + [late[:, a, :] for a in range(20, 22)]
         wb = [late[:, a, :] for a in range(12)]
         wbs = late[:, 12:18, :].rearrange("p a (b i) -> p (a b) i", b=2)
         w2 = late[:, 18, :]
@@ -101,30 +109,29 @@ def tile_moe_pool_sigmoid_kernel(
         for q in range(4):
             nc.gpsimd.dma_start(w2s[32 * q : 32 * q + 4].bitcast(I32), w2_scales[0, 4 * q : 4 * q + 4, :].bitcast(I32))
 
-        pieces = [slice(0, C1), slice(C1, T)]
-        for piece in pieces:
-            gather_words(GATE, piece)
-        for piece in pieces:
-            gather_words(VALUE, piece)
+        for l in (GATE, VALUE):
+            for first in range(0, T, C1):
+                gather_words(l, slice(first, first + C1))
 
         w2d = held([P, 2 * N], U8, "w2d")
         nc.gpsimd.tensor_copy(
             w2d[:].rearrange("p (j m b) -> p j m b", j=LANES, b=2), w2.rearrange("p (m j b) -> p j m b", j=LANES, b=2)
         )
-        w2sd = held([P, LANES, P], U8, "w2sd")
-        nc.gpsimd.tensor_copy(w2sd[:], w2s.rearrange("p (m j) -> p j m", j=LANES))
+        w2s_by_lane = w2s.rearrange("p (m j) -> p j m", j=LANES)
+        w2sd_rest = held([P, LANES - 1, P], U8, "w2sd_rest")
+        nc.gpsimd.tensor_copy(w2sd_rest[:], w2s_by_lane[:, 1:LANES, :])
 
         def sums(l, slot0, words, scales):
             acc = psum.tile([P, H], F32, name="bank")
-            for s in reversed(range(PASSES)):
+            for s in PASS_ORDER:
                 nc.tensor.matmul_mx(
                     out=acc[:],
                     lhsT=gw[l][s][:, slot0 : slot0 + P].bitcast(FP8X4),
                     lhsT_scale=planes[l][s][:, slot0 : slot0 + P],
                     rhs=words[s].bitcast(FP4X4),
                     rhs_scale=scales[s],
-                    start=(s == PASSES - 1),
-                    stop=(s == 0),
+                    start=(s == PASS_ORDER[0]),
+                    stop=(s == PASS_ORDER[-1]),
                 )
             return acc[:].rearrange("p (m j) -> p j m", j=LANES)
 
@@ -136,22 +143,20 @@ def tile_moe_pool_sigmoid_kernel(
 
         dealt = [held([P, T // P, LANES, P], F32, "dealt%d" % l) for l in range(2)]
         src = [held([P, LANES, T], F32, "src%d" % l) for l in range(2)]
-        early_values = src[VALUE][:, 0:3, :]
-        row = [[0, 1, 2, 3], [0, 1, 3, 2]]
 
         def turn_slots(l, j, slots, copy=nc.scalar.copy):
             tiles = range(slots.start // P, slots.stop // P)
-            turn([dealt[l][:, u, j, :] for u in tiles], src[l][:, row[l][j], slots].rearrange("p (u t) -> p u t", t=P), copy)
+            turn([dealt[l][:, u, j, :] for u in tiles], src[l][:, j, slots].rearrange("p (u t) -> p u t", t=P), copy)
 
-        window = [[held([P, WIDE if l == 1 and j == 3 else T], F32, "window%d%d" % (l, j)) for j in range(LANES)] for l in range(2)]
+        window = [[held([P, WIDE if l == VALUE and j > 0 else T], F32, "window%d%d" % (l, j)) for j in range(LANES)] for l in range(2)]
         gate, value = window
         hq = held([P, T, LANES], BF16, "hq")
 
         def scatter(engine, l, j, slots):
             if engine == "scalar":
-                nc.scalar.activation(window[l][j][:].indirect(offsets(l, slots)), src[l][:, row[l][j], slots], COPY)
+                nc.scalar.activation(window[l][j][:].indirect(offsets(l, slots)), src[l][:, j, slots], COPY)
             else:
-                nc.vector.tensor_copy(window[l][j][:].indirect(offsets(l, slots)), src[l][:, row[l][j], slots])
+                nc.vector.tensor_copy(window[l][j][:].indirect(offsets(l, slots)), src[l][:, j, slots])
 
         def product(j):
             nc.gpsimd.tensor_tensor(hq[:, :, j], gate[j][:], value[j][:, 0:T], MULT)
@@ -171,31 +176,53 @@ def tile_moe_pool_sigmoid_kernel(
                 [dealt[GATE][:, u, j, :] for j in (1, 2) for u in (2 * e, 2 * e + 1)],
                 src[GATE][:, 1:3, slots].rearrange("p j (u t) -> p j u t", t=P), nc.scalar.copy,
             )
+            if e == 0:
+                turn_slots(GATE, 0, slots)
+                scatter("scalar", GATE, 0, slots)
             scatter("vector", GATE, 1, slots)
             scatter("vector", GATE, 2, slots)
         tiles(VALUE, slice(0, T))
         for f in range(E2):
             slots = slice(f * P, (f + 1) * P)
-            turn([dealt[VALUE][:, f, j, :] for j in (0, 1, 3)], early_values[:, :, slots], nc.scalar.copy)
-            if (f + 1) * P % HALF == 0:
-                for j in (1, 0):
-                    scatter("vector", VALUE, j, halves[f * P // HALF])
-        scatter("vector", VALUE, 3, slice(0, T))
-        for l, j, half in [(l, j, half) for half in halves for l, j in ((GATE, 0), (VALUE, 2))] + [(GATE, 3, half) for half in halves]:
-            turn_slots(l, j, half)
-            scatter("scalar", l, j, half)
+            turn([dealt[VALUE][:, f, j, :] for j in range(1, LANES)], src[VALUE][:, 1:LANES, slots], nc.scalar.copy)
+        for j in range(1, LANES):
+            scatter("vector", VALUE, j, slice(0, T))
+        turn_slots(GATE, 0, slice(C1, T))
+        for b, half in enumerate(halves):
+            turn_slots(VALUE, 0, half)
+            scatter("scalar", GATE, 0, slice((b + 1) * C1, (b + 2) * C1))
+            scatter("scalar", VALUE, 0, half)
+        turn_slots(GATE, 3, halves[0])
+        scatter("scalar", GATE, 3, halves[0])
+        turned = psum.tile([P, HALF // P, P], F32, name="bank")
+        for b in range(HALF // P):
+            nc.tensor.transpose(turned[:, b, :], dealt[GATE][:, HALF // P + b, 3, :], ident[:])
+        middle = held([P, 2, P], F32, "middle")
+        nc.scalar.copy(middle[:], turned[:, 0:2, :])
+        nc.scalar.copy(src[GATE][:, 3, T - P : T], turned[:, 2, :])
+        nc.scalar.activation(gate[3][:].indirect(offsets(GATE, slice(HALF, T - P))), middle[:].rearrange("p u t -> p (u t)"), COPY)
+        scatter("scalar", GATE, 3, slice(T - P, T))
         product(1)
         product(0)
 
         pair = held([P, 2, T], BF16, "window10")
         nc.gpsimd.tensor_tensor(pair[:, 0, :], gate[2][:], value[2][:, 0:T], MULT)
+        w2sd_first = held([P, P], U8, "middle")
+        nc.gpsimd.tensor_copy(w2sd_first[:], w2s_by_lane[:, 0, :])
+        w2sd = [w2sd_first[:]] + [w2sd_rest[:, j, :] for j in range(LANES - 1)]
+        warm = psum.tile([P, H], F32, name="bank")
+        for repeat in range(3):
+            nc.tensor.matmul_mx(
+                out=warm[:], lhsT=w2d[:, 0 : 2 * P].bitcast(FP4X4), lhsT_scale=w2sd[0],
+                rhs=gw[VALUE][0][:, 0:H].bitcast(FP8X4), rhs_scale=planes[VALUE][0][:, 0:H], start=True, stop=True,
+            )
         y_codes = held([P, T], U32, "y_codes")
         y_scales = held([P, T], U8, "y_scales")
         h_codes = held([P, T], U32, "h_codes")
         h_scales = held([P, T], U8, "h_scales")
         rows = out_0.rearrange("(p j) t -> p j t", j=LANES)
-        runs = [slice(0, 2 * P), slice(2 * P, T)]
-        y = [held([P, LANES, run.stop - run.start], F32, "y%d" % r) for r, run in enumerate(runs)]
+        runs = [slice(first, first + RUN) for first in range(0, T, RUN)]
+        y = [held([P, LANES, RUN], F32, "y%d" % r) for r in range(len(runs))]
         yq = held([P, T, LANES], BF16, "yq")
 
         def units(u0, u1):
@@ -212,28 +239,25 @@ def tile_moe_pool_sigmoid_kernel(
                 out=codes[:, cols].bitcast(FP8X4), scales=scales[:, cols], in_=values[:, cols, :].rearrange("p t j -> p (t j)")
             )
 
-        def multiply(cols, j, dest, copy):
-            bank = psum.tile([P, cols.stop - cols.start], F32, name="bank")
-            nc.tensor.matmul_mx(
-                out=bank[:],
-                lhsT=w2d[:, 2 * P * j : 2 * P * (j + 1)].bitcast(FP4X4),
-                lhsT_scale=w2sd[:, j, :],
-                rhs=h_codes[:, cols].bitcast(FP8X4),
-                rhs_scale=h_scales[:, cols],
-                start=True,
-                stop=True,
-            )
-            copy(dest, bank[:])
+        def result_rows(r, lanes, copy):
+            bank = psum.tile([P, len(lanes), RUN], F32, name="bank")
+            for b, j in enumerate(lanes):
+                nc.tensor.matmul_mx(
+                    out=bank[:, b, :],
+                    lhsT=w2d[:, 2 * P * j : 2 * P * (j + 1)].bitcast(FP4X4),
+                    lhsT_scale=w2sd[j],
+                    rhs=h_codes[:, runs[r]].bitcast(FP8X4),
+                    rhs_scale=h_scales[:, runs[r]],
+                    start=True,
+                    stop=True,
+                )
+            copy(y[r][:, lanes.start : lanes.stop, :], bank[:])
+            nc.sync.dma_start(rows[:, lanes.start : lanes.stop, runs[r]], y[r][:, lanes.start : lanes.stop, :])
 
-        def result_rows(r, j, copy):
-            multiply(runs[r], j, y[r][:, j, :], copy)
-            nc.sync.dma_start(rows[:, j, runs[r]], y[r][:, j, :])
-
-        def round_result(r, t0, t1, copy):
-            cols = slice(runs[r].start + t0, runs[r].start + t1)
+        def round_result(r, copy):
             copy(
-                yq[:, cols, :].rearrange("p (c i) j -> p c j i", i=4),
-                y[r][:, :, t0:t1].rearrange("p j (c i) -> p c j i", i=4),
+                yq[:, runs[r], :].rearrange("p (c i) j -> p c j i", i=4),
+                y[r][:].rearrange("p j (c i) -> p c j i", i=4),
             )
 
         def store_codes(cols):
@@ -249,28 +273,23 @@ def tile_moe_pool_sigmoid_kernel(
         weave(on_vector, units(1, 2))
         last_product(units(4, 6))
         quantise(h_codes, h_scales, hq, runs[0])
-        result_rows(0, 0, on_scalar)
-        result_rows(0, 1, on_scalar)
-        result_rows(0, 2, on_scalar)
-        result_rows(0, 3, on_scalar)
         weave(on_vector, units(4, 6))
-        quantise(h_codes, h_scales, hq, units(2, 4))
-        quantise(h_codes, h_scales, hq, units(4, 6))
-        result_rows(1, 0, on_vector)
-        result_rows(1, 1, on_scalar)
-        round_result(0, 0, 2 * P, on_vector)
-        result_rows(1, 2, on_scalar)
+        quantise(h_codes, h_scales, hq, runs[1])
+        quantise(h_codes, h_scales, hq, runs[2])
+        for j in range(LANES):
+            result_rows(0, range(j, j + 1), on_scalar)
+        result_rows(1, range(0, 2), on_vector)
+        result_rows(1, range(2, 4), on_scalar)
+        round_result(0, on_vector)
+        result_rows(2, range(0, 2), on_scalar)
+        result_rows(2, range(2, 4), on_vector)
         quantise(y_codes, y_scales, yq, runs[0])
-        multiply(units(2, 4), 3, y[1][:, 3, 0 : 2 * P], on_vector)
-        multiply(units(4, 6), 3, y[1][:, 3, 2 * P : 4 * P], on_scalar)
-        nc.sync.dma_start(rows[:, 3, runs[1]], y[1][:, 3, :])
-        round_result(1, 5 * P // 2, 4 * P, on_scalar)
-        round_result(1, 0, 2 * P, on_vector)
-        round_result(1, 2 * P, 5 * P // 2, on_vector)
-        quantise(y_codes, y_scales, yq, units(2, 4))
-        store_codes(units(0, 4))
-        quantise(y_codes, y_scales, yq, units(4, 6))
-        store_codes(units(4, 6))
+        round_result(1, on_scalar)
+        round_result(2, on_vector)
+        quantise(y_codes, y_scales, yq, runs[1])
+        store_codes(slice(0, 2 * RUN))
+        quantise(y_codes, y_scales, yq, runs[2])
+        store_codes(runs[2])
         for q in range(4):
             queue = nc.scalar if q % 2 else nc.sync
             queue.dma_start(out_2[0, 4 * q : 4 * q + 4, :].bitcast(I32), y_scales[32 * q : 32 * q + 4].bitcast(I32))

@@ -24,6 +24,7 @@ WIDE = 1024
 HALF = T // 2
 RUN = 256
 GATE, VALUE = 0, 1
+SHARE = 128
 PASS_ORDER = (1, 0)
 FLOPS = 2 * K * H * T * 2 + 2 * H * N * T
 
@@ -185,8 +186,10 @@ def tile_moe_pool_sigmoid_kernel(
         for f in range(E2):
             slots = slice(f * P, (f + 1) * P)
             turn([dealt[VALUE][:, f, j, :] for j in range(1, LANES)], src[VALUE][:, 1:LANES, slots], nc.scalar.copy)
-        for j in range(1, LANES):
-            scatter("vector", VALUE, j, slice(0, T))
+        scatter("scalar", VALUE, 2, slice(0, SHARE))
+        scatter("vector", VALUE, 1, slice(0, T))
+        scatter("vector", VALUE, 2, slice(SHARE, T))
+        scatter("vector", VALUE, 3, slice(0, T))
         turn_slots(GATE, 0, slice(C1, T))
         for b, half in enumerate(halves):
             turn_slots(VALUE, 0, half)

@@ -1,7 +1,6 @@
 from contextlib import ExitStack
 
 import concourse.mybir as mybir
-from concourse.masks import make_identity
 
 F32 = mybir.dt.float32
 BF16 = mybir.dt.bfloat16
@@ -24,7 +23,7 @@ WIDE = 1024
 HALF = T // 2
 RUN = 256
 GATE, VALUE = 0, 1
-SHARE = 128
+SHARE = 192
 PASS_ORDER = (1, 0)
 FLOPS = 2 * K * H * T * 2 + 2 * H * N * T
 
@@ -50,7 +49,6 @@ def tile_moe_pool_sigmoid_kernel(
 
         xs = held([P, T], U8, "xs")
         xw = held([P, PASSES, T], I32, "xw")
-        ident = held([P, P], F32, "ident")
         wa_first = held([P, 2 * PASSES, 2 * H], U8, "wa_first")
         was = held([P, E1 * PASSES, H], U8, "was")
 
@@ -72,7 +70,6 @@ def tile_moe_pool_sigmoid_kernel(
         load_scales(was, wa_scales, [nc.sync, nc.sync, nc.gpsimd, nc.gpsimd])
         nc.sync.dma_start(xw[:], x_words.rearrange("s p t d -> p s (t d)").bitcast(I32))
         load_words(wa_first[:], wa_words[0:2])
-        make_identity(nc, ident[:])
 
         gw = [[held([P, T], U32, "gw%d%d" % (l, s)) for s in range(PASSES)] for l in range(2)]
 
@@ -122,35 +119,36 @@ def tile_moe_pool_sigmoid_kernel(
         w2sd_rest = held([P, LANES - 1, P], U8, "w2sd_rest")
         nc.gpsimd.tensor_copy(w2sd_rest[:], w2s_by_lane[:, 1:LANES, :])
 
-        def sums(l, slot0, words, scales):
-            acc = psum.tile([P, H], F32, name="bank")
-            for s in PASS_ORDER:
-                nc.tensor.matmul_mx(
-                    out=acc[:],
-                    lhsT=gw[l][s][:, slot0 : slot0 + P].bitcast(FP8X4),
-                    lhsT_scale=planes[l][s][:, slot0 : slot0 + P],
-                    rhs=words[s].bitcast(FP4X4),
-                    rhs_scale=scales[s],
-                    start=(s == PASS_ORDER[0]),
-                    stop=(s == PASS_ORDER[-1]),
-                )
-            return acc[:].rearrange("p (m j) -> p j m", j=LANES)
-
-        def turn(blocks, dest, copy):
-            turned = psum.tile([P, len(blocks), P], F32, name="bank")
-            for b, block in enumerate(blocks):
-                nc.tensor.transpose(turned[:, b, :], block, ident[:])
-            copy(dest, turned[:] if len(dest.shape) == 3 else turned[:].rearrange("p (j u) t -> p j u t", j=2))
-
-        dealt = [held([P, T // P, LANES, P], F32, "dealt%d" % l) for l in range(2)]
         src = [held([P, LANES, T], F32, "src%d" % l) for l in range(2)]
+        words, scales, room = [wa, wb], [was, wbs], [C1, C2]
 
-        def turn_slots(l, j, slots, copy=nc.scalar.copy):
-            tiles = range(slots.start // P, slots.stop // P)
-            turn([dealt[l][:, u, j, :] for u in tiles], src[l][:, j, slots].rearrange("p (u t) -> p u t", t=P), copy)
+        def sums(l, pairs):
+            acc = psum.tile([P, len(pairs), room[l]], F32, name="bank")
+            for b, (j, e) in enumerate(pairs):
+                slots = slice(e * room[l], (e + 1) * room[l])
+                for s in PASS_ORDER:
+                    nc.tensor.matmul_mx(
+                        out=acc[:, b, :],
+                        lhsT=words[l][e * PASSES + s][:, 2 * P * j : 2 * P * (j + 1)].bitcast(FP4X4),
+                        lhsT_scale=scales[l][:, e * PASSES + s, P * j : P * (j + 1)],
+                        rhs=gw[l][s][:, slots].bitcast(FP8X4),
+                        rhs_scale=planes[l][s][:, slots],
+                        start=(s == PASS_ORDER[0]),
+                        stop=(s == PASS_ORDER[-1]),
+                    )
+            return acc
 
-        window = [[held([P, WIDE if l == VALUE and j > 0 else T], F32, "window%d%d" % (l, j)) for j in range(LANES)] for l in range(2)]
+        def rows_of(l, slices, experts):
+            acc = sums(l, [(j, e) for j in slices for e in experts])
+            nc.scalar.activation(
+                src[l][:, slices.start : slices.stop : slices.step, experts.start * room[l] : experts.stop * room[l]],
+                acc[:].rearrange("p (j e) t -> p j (e t)", j=len(slices)), COPY if l else SIGMOID,
+            )
+
+        window = [[held([P, WIDE if l == VALUE and j % 2 else T], F32, "window%d%d" % (l, j)) for j in range(LANES)] for l in range(2)]
         gate, value = window
+        h_rows = [held([P, T], BF16, "h_rows%d" % j) for j in range(LANES - 1)]
+        h_moved = held([P, LANES, T], BF16, "h_moved")
         hq = held([P, T, LANES], BF16, "hq")
 
         def scatter(engine, l, j, slots):
@@ -159,66 +157,47 @@ def tile_moe_pool_sigmoid_kernel(
             else:
                 nc.vector.tensor_copy(window[l][j][:].indirect(offsets(l, slots)), src[l][:, j, slots])
 
+        def move(j, cols, queues):
+            for d in range(LANES):
+                queues[d % len(queues)].dma_start(h_moved[32 * j : 32 * (j + 1), d, cols], h_rows[j][d:P:LANES, cols])
+
         def product(j):
-            nc.gpsimd.tensor_tensor(hq[:, :, j], gate[j][:], value[j][:, 0:T], MULT)
+            nc.gpsimd.tensor_tensor(h_rows[j][:], gate[j][:], value[j][:, 0:T], MULT)
+            move(j, slice(0, T), [nc.sync])
 
-        words, scales, room = [wa, wb], [was, wbs], [C1, C2]
-
-        def tiles(l, slots):
-            for u in range(slots.start // P, slots.stop // P):
-                e = u * P // room[l]
-                by_lane = sums(l, u * P, [words[l][e * PASSES + s] for s in range(PASSES)], [scales[l][:, e * PASSES + s, :] for s in range(PASSES)])
-                nc.scalar.activation(dealt[l][:, u], by_lane, COPY if l else SIGMOID)
-
-        tiles(GATE, slice(0, T))
-        for e in range(E1):
-            slots = slice(e * C1, (e + 1) * C1)
-            turn(
-                [dealt[GATE][:, u, j, :] for j in (1, 2) for u in (2 * e, 2 * e + 1)],
-                src[GATE][:, 1:3, slots].rearrange("p j (u t) -> p j u t", t=P), nc.scalar.copy,
-            )
-            if e == 0:
-                turn_slots(GATE, 0, slots)
-                scatter("scalar", GATE, 0, slots)
-            scatter("vector", GATE, 1, slots)
-            scatter("vector", GATE, 2, slots)
-        tiles(VALUE, slice(0, T))
-        for f in range(E2):
-            slots = slice(f * P, (f + 1) * P)
-            turn([dealt[VALUE][:, f, j, :] for j in range(1, LANES)], src[VALUE][:, 1:LANES, slots], nc.scalar.copy)
-        scatter("scalar", VALUE, 2, slice(0, SHARE))
+        thirds = [slice(first, first + C1) for first in range(0, T, C1)]
+        rows_of(GATE, range(0, 2), range(0, 1))
+        scatter("scalar", GATE, 0, thirds[0])
+        scatter("vector", GATE, 1, thirds[0])
+        rows_of(GATE, range(2, 3), range(0, 2))
+        scatter("vector", GATE, 2, thirds[0])
+        for e in (1, 2):
+            rows_of(GATE, range(0, 2), range(e, e + 1))
+            if e == 2:
+                scatter("scalar", GATE, 0, slice(C1, T - SHARE))
+            scatter("vector", GATE, 1, thirds[e])
+            if e == 2:
+                rows_of(GATE, range(2, 4), range(2, 3))
+            scatter("vector", GATE, 2, thirds[e])
+        scatter("vector", GATE, 0, slice(T - SHARE, T))
+        for first in range(0, E2, 2):
+            rows_of(VALUE, range(0, 3, 2), range(first, first + 2))
+        scatter("scalar", VALUE, 0, halves[0])
+        for first in range(0, E2, 2):
+            rows_of(VALUE, range(1, 4, 2), range(first, first + 2))
+        scatter("scalar", VALUE, 0, halves[1])
         scatter("vector", VALUE, 1, slice(0, T))
-        scatter("vector", VALUE, 2, slice(SHARE, T))
         scatter("vector", VALUE, 3, slice(0, T))
-        turn_slots(GATE, 0, slice(C1, T))
-        for b, half in enumerate(halves):
-            turn_slots(VALUE, 0, half)
-            scatter("scalar", GATE, 0, slice((b + 1) * C1, (b + 2) * C1))
-            scatter("scalar", VALUE, 0, half)
-        turn_slots(GATE, 3, halves[0])
-        scatter("scalar", GATE, 3, halves[0])
-        turned = psum.tile([P, HALF // P, P], F32, name="bank")
-        for b in range(HALF // P):
-            nc.tensor.transpose(turned[:, b, :], dealt[GATE][:, HALF // P + b, 3, :], ident[:])
-        middle = held([P, 2, P], F32, "middle")
-        nc.scalar.copy(middle[:], turned[:, 0:2, :])
-        nc.scalar.copy(src[GATE][:, 3, T - P : T], turned[:, 2, :])
-        nc.scalar.activation(gate[3][:].indirect(offsets(GATE, slice(HALF, T - P))), middle[:].rearrange("p u t -> p (u t)"), COPY)
-        scatter("scalar", GATE, 3, slice(T - P, T))
-        product(1)
-        product(0)
+        scatter("scalar", VALUE, 2, halves[0])
+        rows_of(GATE, range(3, 4), range(0, 2))
+        scatter("scalar", VALUE, 2, halves[1])
+        for half in halves:
+            scatter("scalar", GATE, 3, half)
+        for j in range(LANES - 1):
+            product(j)
 
-        pair = held([P, 2, T], BF16, "window10")
-        nc.gpsimd.tensor_tensor(pair[:, 0, :], gate[2][:], value[2][:, 0:T], MULT)
-        w2sd_first = held([P, P], U8, "middle")
-        nc.gpsimd.tensor_copy(w2sd_first[:], w2s_by_lane[:, 0, :])
-        w2sd = [w2sd_first[:]] + [w2sd_rest[:, j, :] for j in range(LANES - 1)]
-        warm = psum.tile([P, H], F32, name="bank")
-        for repeat in range(3):
-            nc.tensor.matmul_mx(
-                out=warm[:], lhsT=w2d[:, 0 : 2 * P].bitcast(FP4X4), lhsT_scale=w2sd[0],
-                rhs=gw[VALUE][0][:, 0:H].bitcast(FP8X4), rhs_scale=planes[VALUE][0][:, 0:H], start=True, stop=True,
-            )
+        h_rows.append(held([P, T], BF16, "window12"))
+        w2sd = [None] + [w2sd_rest[:, j, :] for j in range(LANES - 1)]
         y_codes = held([P, T], U32, "y_codes")
         y_scales = held([P, T], U8, "y_scales")
         h_codes = held([P, T], U32, "h_codes")
@@ -232,10 +211,10 @@ def tile_moe_pool_sigmoid_kernel(
             return slice(P * u0, P * u1)
 
         def last_product(cols):
-            nc.vector.tensor_tensor(pair[:, 1, cols], value[3][:, cols], gate[3][:, cols], MULT)
+            nc.vector.tensor_tensor(h_rows[3][:, cols], value[3][:, cols], gate[3][:, cols], MULT)
 
         def weave(copy, cols):
-            copy(hq[:, cols, 2:4], pair[:, :, cols].rearrange("p j t -> p t j"))
+            copy(hq[:, cols, :].rearrange("p (c i) j -> p c j i", i=4), h_moved[:, :, cols].rearrange("p j (c i) -> p c j i", i=4))
 
         def quantise(codes, scales, values, cols):
             nc.vector.quantize_mx(
@@ -269,15 +248,24 @@ def tile_moe_pool_sigmoid_kernel(
             )
 
         on_vector, on_scalar = nc.vector.tensor_copy, nc.scalar.copy
-        last_product(units(0, 2))
-        weave(on_scalar, units(0, 1))
-        last_product(units(2, 4))
-        weave(on_scalar, units(2, 4))
-        weave(on_vector, units(1, 2))
-        last_product(units(4, 6))
+        last_product(slice(0, T))
+        move(3, slice(0, T), [nc.sync])
+        w2sd_first = held([P, P], U8, "window13")
+        nc.gpsimd.tensor_copy(w2sd_first[:], w2s_by_lane[:, 0, :])
+        w2sd[0] = w2sd_first[:]
+        warm = psum.tile([P, H], F32, name="bank")
+        for repeat in range(3):
+            nc.tensor.matmul_mx(
+                out=warm[:], lhsT=w2d[:, 0 : 2 * P].bitcast(FP4X4), lhsT_scale=w2sd[0],
+                rhs=gw[VALUE][0][:, 0:H].bitcast(FP8X4), rhs_scale=planes[VALUE][0][:, 0:H], start=True, stop=True,
+            )
+        weave(on_vector, slice(0, 160))
+        weave(on_scalar, slice(160, RUN))
         quantise(h_codes, h_scales, hq, runs[0])
-        weave(on_vector, units(4, 6))
+        weave(on_scalar, units(2, 3))
+        weave(on_vector, units(3, 4))
         quantise(h_codes, h_scales, hq, runs[1])
+        weave(on_vector, runs[2])
         quantise(h_codes, h_scales, hq, runs[2])
         for j in range(LANES):
             result_rows(0, range(j, j + 1), on_scalar)

@@ -157,13 +157,13 @@ def tile_moe_pool_sigmoid_kernel(
             else:
                 nc.vector.tensor_copy(window[l][j][:].indirect(offsets(l, slots)), src[l][:, j, slots])
 
-        def move(j, cols, queues):
+        def move(j, cols, rows_in):
             for d in range(LANES):
-                queues[d % len(queues)].dma_start(h_moved[32 * j : 32 * (j + 1), d, cols], h_rows[j][d:P:LANES, cols])
+                nc.sync.dma_start(h_moved[32 * j : 32 * (j + 1), d, cols], rows_in[d:P:LANES])
 
         def product(j):
             nc.gpsimd.tensor_tensor(h_rows[j][:], gate[j][:], value[j][:, 0:T], MULT)
-            move(j, slice(0, T), [nc.sync])
+            move(j, slice(0, T), h_rows[j][:])
 
         thirds = [slice(first, first + C1) for first in range(0, T, C1)]
         rows_of(GATE, range(0, 2), range(0, 1))
@@ -174,29 +174,31 @@ def tile_moe_pool_sigmoid_kernel(
         for e in (1, 2):
             rows_of(GATE, range(0, 2), range(e, e + 1))
             if e == 2:
-                scatter("scalar", GATE, 0, slice(C1, T - SHARE))
+                rows_of(GATE, range(2, 3), range(2, 3))
+            scatter("scalar", GATE, 0, thirds[e])
             scatter("vector", GATE, 1, thirds[e])
-            if e == 2:
-                rows_of(GATE, range(2, 4), range(2, 3))
             scatter("vector", GATE, 2, thirds[e])
-        scatter("vector", GATE, 0, slice(T - SHARE, T))
         for first in range(0, E2, 2):
             rows_of(VALUE, range(0, 3, 2), range(first, first + 2))
-        scatter("scalar", VALUE, 0, halves[0])
         for first in range(0, E2, 2):
             rows_of(VALUE, range(1, 4, 2), range(first, first + 2))
-        scatter("scalar", VALUE, 0, halves[1])
+            if first == 0:
+                scatter("scalar", VALUE, 0, halves[0])
         scatter("vector", VALUE, 1, slice(0, T))
+        rows_of(GATE, range(3, 4), range(2, 3))
+        scatter("vector", GATE, 3, slice(T - SHARE, T))
+        scatter("scalar", VALUE, 0, halves[1])
         scatter("vector", VALUE, 3, slice(0, T))
         scatter("scalar", VALUE, 2, halves[0])
         rows_of(GATE, range(3, 4), range(0, 2))
         scatter("scalar", VALUE, 2, halves[1])
-        for half in halves:
-            scatter("scalar", GATE, 3, half)
+        for first in (0, (T - SHARE) // 2):
+            scatter("scalar", GATE, 3, slice(first, first + (T - SHARE) // 2))
         for j in range(LANES - 1):
             product(j)
 
-        h_rows.append(held([P, T], BF16, "window12"))
+        pieces = [slice(0, RUN), slice(RUN, T)]
+        h_last = [held([P, piece.stop - piece.start], BF16, name) for piece, name in zip(pieces, ("window12", "window02"))]
         w2sd = [None] + [w2sd_rest[:, j, :] for j in range(LANES - 1)]
         y_codes = held([P, T], U32, "y_codes")
         y_scales = held([P, T], U8, "y_scales")
@@ -210,8 +212,9 @@ def tile_moe_pool_sigmoid_kernel(
         def units(u0, u1):
             return slice(P * u0, P * u1)
 
-        def last_product(cols):
-            nc.vector.tensor_tensor(h_rows[3][:, cols], value[3][:, cols], gate[3][:, cols], MULT)
+        def last_product(b):
+            nc.vector.tensor_tensor(h_last[b][:], value[3][:, pieces[b]], gate[3][:, pieces[b]], MULT)
+            move(3, pieces[b], h_last[b][:])
 
         def weave(copy, cols):
             copy(hq[:, cols, :].rearrange("p (c i) j -> p c j i", i=4), h_moved[:, :, cols].rearrange("p j (c i) -> p c j i", i=4))
@@ -248,8 +251,8 @@ def tile_moe_pool_sigmoid_kernel(
             )
 
         on_vector, on_scalar = nc.vector.tensor_copy, nc.scalar.copy
-        last_product(slice(0, T))
-        move(3, slice(0, T), [nc.sync])
+        last_product(0)
+        last_product(1)
         w2sd_first = held([P, P], U8, "window13")
         nc.gpsimd.tensor_copy(w2sd_first[:], w2s_by_lane[:, 0, :])
         w2sd[0] = w2sd_first[:]
@@ -265,7 +268,8 @@ def tile_moe_pool_sigmoid_kernel(
         weave(on_scalar, units(2, 3))
         weave(on_vector, units(3, 4))
         quantise(h_codes, h_scales, hq, runs[1])
-        weave(on_vector, runs[2])
+        weave(on_scalar, units(4, 5))
+        weave(on_vector, units(5, 6))
         quantise(h_codes, h_scales, hq, runs[2])
         for j in range(LANES):
             result_rows(0, range(j, j + 1), on_scalar)

@@ -23,7 +23,6 @@ WIDE = 1024
 HALF = T // 2
 RUN = 256
 GATE, VALUE = 0, 1
-SHARE = 192
 PASS_ORDER = (1, 0)
 FLOPS = 2 * K * H * T * 2 + 2 * H * N * T
 
@@ -116,8 +115,8 @@ def tile_moe_pool_sigmoid_kernel(
             w2d[:].rearrange("p (j m b) -> p j m b", j=LANES, b=2), w2.rearrange("p (m j b) -> p j m b", j=LANES, b=2)
         )
         w2s_by_lane = w2s.rearrange("p (m j) -> p j m", j=LANES)
-        w2sd_rest = held([P, LANES - 1, P], U8, "w2sd_rest")
-        nc.gpsimd.tensor_copy(w2sd_rest[:], w2s_by_lane[:, 1:LANES, :])
+        w2sd_early = held([P, P], U8, "w2sd_early")
+        nc.gpsimd.tensor_copy(w2sd_early[:], w2s_by_lane[:, LANES - 1, :])
 
         src = [held([P, LANES, T], F32, "src%d" % l) for l in range(2)]
         words, scales, room = [wa, wb], [was, wbs], [C1, C2]
@@ -169,12 +168,11 @@ def tile_moe_pool_sigmoid_kernel(
         rows_of(GATE, range(0, 2), range(0, 1))
         scatter("scalar", GATE, 0, thirds[0])
         scatter("vector", GATE, 1, thirds[0])
-        rows_of(GATE, range(2, 3), range(0, 2))
-        scatter("vector", GATE, 2, thirds[0])
         for e in (1, 2):
             rows_of(GATE, range(0, 2), range(e, e + 1))
-            if e == 2:
-                rows_of(GATE, range(2, 3), range(2, 3))
+            rows_of(GATE, range(2, 3), range(0, 2) if e == 1 else range(2, 3))
+            if e == 1:
+                scatter("vector", GATE, 2, thirds[0])
             scatter("scalar", GATE, 0, thirds[e])
             scatter("vector", GATE, 1, thirds[e])
             scatter("vector", GATE, 2, thirds[e])
@@ -186,20 +184,20 @@ def tile_moe_pool_sigmoid_kernel(
                 scatter("scalar", VALUE, 0, halves[0])
         scatter("vector", VALUE, 1, slice(0, T))
         rows_of(GATE, range(3, 4), range(2, 3))
-        scatter("vector", GATE, 3, slice(T - SHARE, T))
+        scatter("vector", GATE, 3, thirds[2])
         scatter("scalar", VALUE, 0, halves[1])
         scatter("vector", VALUE, 3, slice(0, T))
         scatter("scalar", VALUE, 2, halves[0])
         rows_of(GATE, range(3, 4), range(0, 2))
         scatter("scalar", VALUE, 2, halves[1])
-        for first in (0, (T - SHARE) // 2):
-            scatter("scalar", GATE, 3, slice(first, first + (T - SHARE) // 2))
+        for third in thirds[0:2]:
+            scatter("scalar", GATE, 3, third)
         for j in range(LANES - 1):
             product(j)
 
         pieces = [slice(0, RUN), slice(RUN, T)]
         h_last = [held([P, piece.stop - piece.start], BF16, name) for piece, name in zip(pieces, ("window12", "window02"))]
-        w2sd = [None] + [w2sd_rest[:, j, :] for j in range(LANES - 1)]
+        w2sd = []
         y_codes = held([P, T], U32, "y_codes")
         y_scales = held([P, T], U8, "y_scales")
         h_codes = held([P, T], U32, "h_codes")
@@ -253,9 +251,9 @@ def tile_moe_pool_sigmoid_kernel(
         on_vector, on_scalar = nc.vector.tensor_copy, nc.scalar.copy
         last_product(0)
         last_product(1)
-        w2sd_first = held([P, P], U8, "window13")
-        nc.gpsimd.tensor_copy(w2sd_first[:], w2s_by_lane[:, 0, :])
-        w2sd[0] = w2sd_first[:]
+        w2sd_late = held([P, LANES - 1, P], U8, "window13")
+        nc.gpsimd.tensor_copy(w2sd_late[:], w2s_by_lane[:, 0 : LANES - 1, :])
+        w2sd.extend([w2sd_late[:, j, :] for j in range(LANES - 1)] + [w2sd_early[:]])
         warm = psum.tile([P, H], F32, name="bank")
         for repeat in range(3):
             nc.tensor.matmul_mx(

@@ -23,6 +23,7 @@ WIDE = 1024
 HALF = T // 2
 RUN = 256
 GATE, VALUE = 0, 1
+SHARE = 192
 PASS_ORDER = (1, 0)
 FLOPS = 2 * K * H * T * 2 + 2 * H * N * T
 
@@ -165,17 +166,18 @@ def tile_moe_pool_sigmoid_kernel(
             move(j, slice(0, T), h_rows[j][:])
 
         thirds = [slice(first, first + C1) for first in range(0, T, C1)]
-        rows_of(GATE, range(0, 2), range(0, 1))
+        rows_of(GATE, range(0, 1), range(0, 1))
         scatter("scalar", GATE, 0, thirds[0])
-        scatter("vector", GATE, 1, thirds[0])
-        for e in (1, 2):
-            rows_of(GATE, range(0, 2), range(e, e + 1))
-            rows_of(GATE, range(2, 3), range(0, 2) if e == 1 else range(2, 3))
-            if e == 1:
-                scatter("vector", GATE, 2, thirds[0])
-            scatter("scalar", GATE, 0, thirds[e])
-            scatter("vector", GATE, 1, thirds[e])
-            scatter("vector", GATE, 2, thirds[e])
+        rows_of(GATE, range(0, 1), range(1, 2))
+        rows_of(GATE, range(1, 2), range(0, 2))
+        scatter("scalar", GATE, 0, thirds[1])
+        rows_of(GATE, range(2, 3), range(0, 2))
+        rows_of(GATE, range(0, 1), range(2, 3))
+        rows_of(GATE, range(1, 3), range(2, 3))
+        scatter("scalar", GATE, 0, thirds[2])
+        for third in thirds:
+            scatter("vector", GATE, 1, third)
+            scatter("vector", GATE, 2, third)
         for first in range(0, E2, 2):
             rows_of(VALUE, range(0, 3, 2), range(first, first + 2))
         for first in range(0, E2, 2):
@@ -184,14 +186,14 @@ def tile_moe_pool_sigmoid_kernel(
                 scatter("scalar", VALUE, 0, halves[0])
         scatter("vector", VALUE, 1, slice(0, T))
         rows_of(GATE, range(3, 4), range(2, 3))
-        scatter("vector", GATE, 3, thirds[2])
+        scatter("vector", GATE, 3, slice(T - SHARE, T))
         scatter("scalar", VALUE, 0, halves[1])
         scatter("vector", VALUE, 3, slice(0, T))
         scatter("scalar", VALUE, 2, halves[0])
         rows_of(GATE, range(3, 4), range(0, 2))
         scatter("scalar", VALUE, 2, halves[1])
-        for third in thirds[0:2]:
-            scatter("scalar", GATE, 3, third)
+        for first in (0, (T - SHARE) // 2):
+            scatter("scalar", GATE, 3, slice(first, first + (T - SHARE) // 2))
         for j in range(LANES - 1):
             product(j)
 

from contextlib import ExitStack

import concourse.mybir as mybir

F32 = mybir.dt.float32
BF16 = mybir.dt.bfloat16
I32 = mybir.dt.int32
U32 = mybir.dt.uint32
U16 = mybir.dt.uint16
U8 = mybir.dt.uint8
FP8X4 = mybir.dt.float8_e4m3fn_x4
FP4X4 = mybir.dt.float4_e2m1fn_x4
SIGMOID = mybir.ActivationFunctionType.Sigmoid
COPY = mybir.ActivationFunctionType.Copy
MULT = mybir.AluOpType.mult

P = 128
K, T, H, N = 1024, 768, 512, 512
E1, C1, E2, C2 = 3, 256, 6, 128
PASSES = 2
LANES = 4
WIDE = 1024
HALF = T // 2
RUN = 256
GATE, VALUE = 0, 1
SHARE = 192
PASS_ORDER = (1, 0)
FLOPS = 2 * K * H * T * 2 + 2 * H * N * T


def tile_moe_pool_sigmoid_kernel(
    tc, x_words, x_scales, wa_words, wa_scales, wb_words, wb_scales, w2_words, w2_scales, offs, offs2, out_0, out_1, out_2
):
    nc = tc.nc
    with ExitStack() as ctx:
        keep = ctx.enter_context(tc.tile_pool(name="keep", bufs=1))
        psum = ctx.enter_context(tc.psum_pool(name="psum", bufs=8))

        def held(shape, dtype, name):
            return keep.tile(shape, dtype, name=name, align_bytes=64)

        list_a = keep.tile([P, T // 16], U16, name="list_a")
        list_b = keep.tile([P, T // 16], U16, name="list_b")
        lists = [list_a, list_b]
        halves = [slice(0, HALF), slice(HALF, T)]

        def offsets(l, slots):
            return lists[l][:, slots.start // 16 : slots.stop // 16]

        xs = held([P, T], U8, "xs")
        xw = held([P, PASSES, T], I32, "xw")
        wa_first = held([P, 2 * PASSES, 2 * H], U8, "wa_first")
        was = held([P, E1 * PASSES, H], U8, "was")

        def load_scales(plane, scales, queues):
            for q, queue in enumerate(queues):
                queue.dma_start(
                    plane[32 * q : 32 * q + 4].bitcast(I32),
                    scales[:, :, 4 * q : 4 * q + 4, :].rearrange("e s r i -> r (e s) i").bitcast(I32),
                )

        def load_words(tile, words):
            nc.sync.dma_start(tile.bitcast(I32), words.rearrange("e s p n -> p (e s) n").bitcast(I32))

        nc.gpsimd.memset(xs[:].bitcast(I32), 0)
        nc.sync.dma_start(list_a[:], offs)
        for q in range(4):
            nc.sync.dma_start(xs[32 * q : 32 * q + 8].bitcast(I32), x_scales[:, 4 * q : 4 * q + 4, :].bitcast(I32))
        nc.sync.dma_start(list_b[:], offs2)
        load_scales(was, wa_scales, [nc.sync, nc.sync, nc.gpsimd, nc.gpsimd])
        nc.sync.dma_start(xw[:], x_words.rearrange("s p t d -> p s (t d)").bitcast(I32))
        load_words(wa_first[:], wa_words[0:2])

        gw = [[held([P, T], U32, "gw%d%d" % (l, s)) for s in range(PASSES)] for l in range(2)]

        def gather_words(l, slots):
            for s in PASS_ORDER:
                nc.vector.tensor_copy(gw[l][s][:, slots], xw[:, s, :].bitcast(U32).indirect(offsets(l, slots)))

        def gather_scales(l):
            first = held([P, T], U8, "first%d" % l)
            for half in halves:
                nc.vector.tensor_copy(first[:, half], xs[:].indirect(offsets(l, half)))
            return first

        def move_rows(l, first):
            second = held([P, T], U8, "second%d" % l)
            for q in range(4):
                nc.sync.dma_start(second[32 * q : 32 * q + 4].bitcast(I32), first[32 * q + 4 : 32 * q + 8].bitcast(I32))
            return [first, second]

        gathered = [gather_scales(l) for l in range(2)]
        planes = [move_rows(GATE, gathered[GATE])]
        late = held([P, 22, 2 * H], U8, "xs")
        load_words(late[:, 20:22, :], wa_words[2:E1])
        planes.append(move_rows(VALUE, gathered[VALUE]))
        wa = [wa_first[:, a, :] for a in range(2 * PASSES)] + [late[:, a, :] for a in range(20, 22)]
        wb = [late[:, a, :] for a in range(12)]
        wbs = late[:, 12:18, :].rearrange("p a (b i) -> p (a b) i", b=2)
        w2 = late[:, 18, :]
        w2s = late[:, 19, 0:N]
        load_words(late[:, 0:6, :], wb_words[0:3])
        load_scales(wbs, wb_scales, [nc.sync, nc.sync, nc.gpsimd, nc.gpsimd])
        load_words(late[:, 6:12, :], wb_words[3:6])
        nc.gpsimd.memset(w2s.bitcast(I32), 0)
        nc.sync.dma_start(w2.bitcast(I32), w2_words[0].bitcast(I32))
        for q in range(4):
            nc.gpsimd.dma_start(w2s[32 * q : 32 * q + 4].bitcast(I32), w2_scales[0, 4 * q : 4 * q + 4, :].bitcast(I32))

        for l in (GATE, VALUE):
            for first in range(0, T, C1):
                gather_words(l, slice(first, first + C1))

        w2d = held([P, 2 * N], U8, "w2d")
        nc.gpsimd.tensor_copy(
            w2d[:].rearrange("p (j m b) -> p j m b", j=LANES, b=2), w2.rearrange("p (m j b) -> p j m b", j=LANES, b=2)
        )
        w2s_by_lane = w2s.rearrange("p (m j) -> p j m", j=LANES)
        w2sd_early = held([P, P], U8, "w2sd_early")
        nc.gpsimd.tensor_copy(w2sd_early[:], w2s_by_lane[:, LANES - 1, :])

        src = [held([P, LANES, T], F32, "src%d" % l) for l in range(2)]
        words, scales, room = [wa, wb], [was, wbs], [C1, C2]

        def sums(l, pairs):
            acc = psum.tile([P, len(pairs), room[l]], F32, name="bank")
            for b, (j, e) in enumerate(pairs):
                slots = slice(e * room[l], (e + 1) * room[l])
                for s in PASS_ORDER:
                    nc.tensor.matmul_mx(
                        out=acc[:, b, :],
                        lhsT=words[l][e * PASSES + s][:, 2 * P * j : 2 * P * (j + 1)].bitcast(FP4X4),
                        lhsT_scale=scales[l][:, e * PASSES + s, P * j : P * (j + 1)],
                        rhs=gw[l][s][:, slots].bitcast(FP8X4),
                        rhs_scale=planes[l][s][:, slots],
                        start=(s == PASS_ORDER[0]),
                        stop=(s == PASS_ORDER[-1]),
                    )
            return acc

        def rows_of(l, slices, experts):
            acc = sums(l, [(j, e) for j in slices for e in experts])
            nc.scalar.activation(
                src[l][:, slices.start : slices.stop : slices.step, experts.start * room[l] : experts.stop * room[l]],
                acc[:].rearrange("p (j e) t -> p j (e t)", j=len(slices)), COPY if l else SIGMOID,
            )

        window = [[held([P, WIDE if l == VALUE and j % 2 else T], F32, "window%d%d" % (l, j)) for j in range(LANES)] for l in range(2)]
        gate, value = window
        h_rows = [held([P, T], BF16, "h_rows%d" % j) for j in range(LANES - 1)]
        h_moved = held([P, LANES, T], BF16, "h_moved")
        hq = held([P, T, LANES], BF16, "hq")

        def scatter(engine, l, j, slots):
            if engine == "scalar":
                nc.scalar.activation(window[l][j][:].indirect(offsets(l, slots)), src[l][:, j, slots], COPY)
            else:
                nc.vector.tensor_copy(window[l][j][:].indirect(offsets(l, slots)), src[l][:, j, slots])

        def move(j, cols, rows_in):
            for d in range(LANES):
                nc.sync.dma_start(h_moved[32 * j : 32 * (j + 1), d, cols], rows_in[d:P:LANES])

        def product(j):
            nc.gpsimd.tensor_tensor(h_rows[j][:], gate[j][:], value[j][:, 0:T], MULT)
            move(j, slice(0, T), h_rows[j][:])

        thirds = [slice(first, first + C1) for first in range(0, T, C1)]
        rows_of(GATE, range(0, 1), range(0, 1))
        scatter("scalar", GATE, 0, thirds[0])
        rows_of(GATE, range(0, 1), range(1, 2))
        rows_of(GATE, range(1, 2), range(0, 2))
        scatter("scalar", GATE, 0, thirds[1])
        rows_of(GATE, range(2, 3), range(0, 2))
        rows_of(GATE, range(0, 1), range(2, 3))
        rows_of(GATE, range(1, 3), range(2, 3))
        scatter("scalar", GATE, 0, thirds[2])
        for third in thirds:
            scatter("vector", GATE, 1, third)
            scatter("vector", GATE, 2, third)
        for first in range(0, E2, 2):
            rows_of(VALUE, range(0, 3, 2), range(first, first + 2))
        for first in range(0, E2, 2):
            rows_of(VALUE, range(1, 4, 2), range(first, first + 2))
            if first == 0:
                scatter("scalar", VALUE, 0, halves[0])
        scatter("vector", VALUE, 1, slice(0, T))
        rows_of(GATE, range(3, 4), range(2, 3))
        scatter("vector", GATE, 3, slice(T - SHARE, T))
        scatter("scalar", VALUE, 0, halves[1])
        scatter("vector", VALUE, 3, slice(0, T))
        scatter("scalar", VALUE, 2, halves[0])
        rows_of(GATE, range(3, 4), range(0, 2))
        scatter("scalar", VALUE, 2, halves[1])
        for first in (0, (T - SHARE) // 2):
            scatter("scalar", GATE, 3, slice(first, first + (T - SHARE) // 2))
        for j in range(LANES - 1):
            product(j)

        pieces = [slice(0, RUN), slice(RUN, T)]
        h_last = [held([P, piece.stop - piece.start], BF16, name) for piece, name in zip(pieces, ("window12", "window02"))]
        w2sd = []
        y_codes = held([P, T], U32, "y_codes")
        y_scales = held([P, T], U8, "y_scales")
        h_codes = held([P, T], U32, "h_codes")
        h_scales = held([P, T], U8, "h_scales")
        rows = out_0.rearrange("(p j) t -> p j t", j=LANES)
        runs = [slice(first, first + RUN) for first in range(0, T, RUN)]
        y = [held([P, LANES, RUN], F32, "y%d" % r) for r in range(len(runs))]
        yq = held([P, T, LANES], BF16, "yq")

        def units(u0, u1):
            return slice(P * u0, P * u1)

        def last_product(b):
            nc.vector.tensor_tensor(h_last[b][:], value[3][:, pieces[b]], gate[3][:, pieces[b]], MULT)
            move(3, pieces[b], h_last[b][:])

        def weave(copy, cols):
            copy(hq[:, cols, :].rearrange("p (c i) j -> p c j i", i=4), h_moved[:, :, cols].rearrange("p j (c i) -> p c j i", i=4))

        def quantise(codes, scales, values, cols):
            nc.vector.quantize_mx(
                out=codes[:, cols].bitcast(FP8X4), scales=scales[:, cols], in_=values[:, cols, :].rearrange("p t j -> p (t j)")
            )

        def result_rows(r, lanes, copy):
            bank = psum.tile([P, len(lanes), RUN], F32, name="bank")
            for b, j in enumerate(lanes):
                nc.tensor.matmul_mx(
                    out=bank[:, b, :],
                    lhsT=w2d[:, 2 * P * j : 2 * P * (j + 1)].bitcast(FP4X4),
                    lhsT_scale=w2sd[j],
                    rhs=h_codes[:, runs[r]].bitcast(FP8X4),
                    rhs_scale=h_scales[:, runs[r]],
                    start=True,
                    stop=True,
                )
            copy(y[r][:, lanes.start : lanes.stop, :], bank[:])
            nc.sync.dma_start(rows[:, lanes.start : lanes.stop, runs[r]], y[r][:, lanes.start : lanes.stop, :])

        def round_result(r, copy):
            copy(
                yq[:, runs[r], :].rearrange("p (c i) j -> p c j i", i=4),
                y[r][:].rearrange("p j (c i) -> p c j i", i=4),
            )

        def store_codes(cols):
            nc.sync.dma_start(
                out_1[0, :, cols, :].rearrange("p t d -> p (t d)").bitcast(I32), y_codes[:, cols].bitcast(I32)
            )

        on_vector, on_scalar = nc.vector.tensor_copy, nc.scalar.copy
        last_product(0)
        last_product(1)
        w2sd_late = held([P, LANES - 1, P], U8, "window13")
        nc.gpsimd.tensor_copy(w2sd_late[:], w2s_by_lane[:, 0 : LANES - 1, :])
        w2sd.extend([w2sd_late[:, j, :] for j in range(LANES - 1)] + [w2sd_early[:]])
        warm = psum.tile([P, H], F32, name="bank")
        for repeat in range(3):
            nc.tensor.matmul_mx(
                out=warm[:], lhsT=w2d[:, 0 : 2 * P].bitcast(FP4X4), lhsT_scale=w2sd[0],
                rhs=gw[VALUE][0][:, 0:H].bitcast(FP8X4), rhs_scale=planes[VALUE][0][:, 0:H], start=True, stop=True,
            )
        weave(on_vector, slice(0, 160))
        weave(on_scalar, slice(160, RUN))
        quantise(h_codes, h_scales, hq, runs[0])
        weave(on_scalar, units(2, 3))
        weave(on_vector, units(3, 4))
        quantise(h_codes, h_scales, hq, runs[1])
        weave(on_scalar, units(4, 5))
        weave(on_vector, units(5, 6))
        quantise(h_codes, h_scales, hq, runs[2])
        for j in range(LANES):
            result_rows(0, range(j, j + 1), on_scalar)
        result_rows(1, range(0, 2), on_vector)
        result_rows(1, range(2, 4), on_scalar)
        round_result(0, on_vector)
        result_rows(2, range(0, 2), on_scalar)
        result_rows(2, range(2, 4), on_vector)
        quantise(y_codes, y_scales, yq, runs[0])
        round_result(1, on_scalar)
        round_result(2, on_vector)
        quantise(y_codes, y_scales, yq, runs[1])
        store_codes(slice(0, 2 * RUN))
        quantise(y_codes, y_scales, yq, runs[2])
        store_codes(runs[2])
        for q in range(4):
            queue = nc.scalar if q % 2 else nc.sync
            queue.dma_start(out_2[0, 4 * q : 4 * q + 4, :].bitcast(I32), y_scales[32 * q : 32 * q + 4].bitcast(I32))
